import numpy as np
import ml_dtypes


def mxq(x, axis, fmt="e4m3"):
    dtype, down = {"e4m3": (ml_dtypes.float8_e4m3fn, 7), "e5m2": (ml_dtypes.float8_e5m2, 14)}[fmt]
    v = np.moveaxis(np.asarray(x, np.float32).astype(ml_dtypes.bfloat16).astype(np.float64), axis, -1)
    blocks = v.reshape(v.shape[:-1] + (-1, 32))
    amax = np.abs(blocks).max(-1, keepdims=True)
    byte = np.maximum(np.where(amax > 0, np.frexp(amax)[1] - 1 + 127, 0) - down, 1)
    scale = np.exp2(byte - 127.0)
    codes = (blocks / scale).astype(np.float32).astype(dtype).astype(np.float64)
    return np.moveaxis((codes * scale).reshape(v.shape), -1, axis)


WIDE = False


def mx_kscale(k):
    if not WIDE:
        return np.ones(k)
    levels = np.array([10, -10, 5, -5, 0])
    if k % 512:
        return np.exp2(np.random.permutation(np.resize(levels, k // 32))).repeat(32)
    a = np.empty((k // 512, 16))
    for p in range(k // 512):
        a[p, :8] = np.random.permutation(np.resize(levels, 8))
        for g in range(8):
            far = levels[np.abs(levels - a[p, g]) >= 10]
            a[p, g + 8] = far[np.random.randint(len(far))]
    return np.exp2(a.ravel()).repeat(32)


BF16 = ml_dtypes.bfloat16


def bf(x):
    return np.asarray(x, np.float32).astype(BF16)


def f64(x):
    return np.asarray(x).astype(np.float64)


E2M1 = np.array([0.0, 0.5, 1.0, 1.5, 2.0, 3.0, 4.0, 6.0, -0.0, -0.5, -1.0, -1.5, -2.0, -3.0, -4.0, -6.0])


def pack_weight(w, fmt):
    k, n = w.shape
    w = f64(bf(w)).reshape(k // 32, 32, n)
    amax = np.abs(w).max(1)
    if fmt == "e4m3":
        byte = np.frexp(amax)[1] - 1 + 127 - 7
    else:
        mant, ex = np.frexp(amax / 6.0)
        byte = np.where(mant > 0.5, ex, ex - 1) + 127
    byte = np.clip(np.where(amax > 0, byte, 1), 1, 254)
    scaled = (w * np.exp2(127.0 - byte)[:, None, :]).reshape(k, n).astype(np.float32)
    by_word = np.ascontiguousarray(scaled.reshape(k // 512, 128, 4, n).transpose(0, 1, 3, 2))
    if fmt == "e4m3":
        words = by_word.astype(ml_dtypes.float8_e4m3fn).view(np.uint8)
    else:
        c = by_word.astype(ml_dtypes.float4_e2m1fn).view(np.uint8) & 0xF
        words = c[..., 0::2] | (c[..., 1::2] << 4)
    return np.ascontiguousarray(words), np.ascontiguousarray(byte.astype(np.uint8).reshape(k // 512, 16, n))


def unpack_weight(words, scales, fmt):
    g, p, n, _ = words.shape
    if fmt == "e4m3":
        vals = np.ascontiguousarray(words).view(ml_dtypes.float8_e4m3fn).astype(np.float64)
    else:
        nib = np.empty((g, p, n, 4), np.uint8)
        nib[..., 0::2] = words & 0xF
        nib[..., 1::2] = words >> 4
        vals = E2M1[nib]
    vals = vals * np.repeat(np.exp2(scales.astype(np.float64) - 127.0), 8, axis=1)[..., None]
    return vals.transpose(0, 1, 3, 2).reshape(g * 512, n)
def pack4(w):
    words, scales = pack_weight(w, "e2m1")
    return words.reshape(words.shape[0], 128, -1), scales


def unpack4(words, scales):
    return unpack_weight(words.reshape(words.shape[0], 128, -1, 2), scales, "e2m1")


N, R = 1536, 512


def draw0():
    s, u, t = mx_kscale(N), mx_kscale(N), mx_kscale(R)
    hop = np.random.standard_normal((N, N)) / np.sqrt(N) * s
    left = np.random.standard_normal((N, R)) / R ** 0.25 / s[:, None] * t
    right = np.random.standard_normal((R, N)) / R ** 0.25 / t[:, None] * u
    hinv = np.random.standard_normal((N, N)) / np.sqrt(N) / u[:, None]
    hinv_words, hinv_scales = pack4(hinv)
    return {"hop": bf(hop),
            "left": bf(left),
            "right": bf(right),
            "hinv_words": hinv_words,
            "hinv_scales": hinv_scales,
            "field": bf(0.5 * np.random.standard_normal(N))}


def core(hop, left, right, hinv_words, hinv_scales, field):
    w = np.exp(f64(field))
    a = (mxq(f64(hop), 1, "e4m3") @ mxq(f64(left), 0, "e4m3")) * w[:, None]
    c = (mxq(f64(right), 1, "e4m3") @ unpack4(hinv_words, hinv_scales)) / w
    return mxq(a, 1, "e4m3") @ mxq(c, 0, "e4m3")


def e4m3fn_bytes(y):
    return np.clip(np.asarray(y, np.float64), -448.0, 448.0).astype(np.float32).astype(ml_dtypes.float8_e4m3fn).view(np.uint8)


def e4m3fn_values(b):
    return np.asarray(b, np.uint8).view(ml_dtypes.float8_e4m3fn).astype(np.float64)


def setup_inputs():
    d = draw0()
    x0 = np.asarray(d['hop']).astype(np.float64)
    s = (np.max(np.abs(x0), axis=(0,), keepdims=True) / 448.0).astype(np.float32)
    out = {}
    for k, v in d.items():
        if k == 'hop':
            out['hop_bytes'] = e4m3fn_bytes(x0 / s.astype(np.float64))
            out['hop_scale'] = s
        else:
            out[k] = v
    return out


def reference(hop_bytes, hop_scale, left, right, hinv_words, hinv_scales, field):
    return core(e4m3fn_values(hop_bytes) * hop_scale.astype(np.float64), left, right, hinv_words, hinv_scales, field)

@@ -1,0 +1,347 @@
+from contextlib import ExitStack
+
+import concourse.mybir as mybir
+from concourse.masks import make_identity
+
+SITES, ORB = 1536, 512
+
+F32 = mybir.dt.float32
+BF16 = mybir.dt.bfloat16
+U32 = mybir.dt.uint32
+I32 = mybir.dt.int32
+U8 = mybir.dt.uint8
+FP8 = mybir.dt.float8_e4m3fn
+E4M3X4 = mybir.dt.float8_e4m3fn_x4
+E2M1X4 = mybir.dt.float4_e2m1fn_x4
+MULT = mybir.AluOpType.mult
+EXP = mybir.ActivationFunctionType.Exp
+
+P = 128
+PACK = 4
+K_PASS = P * PACK
+PASSES = SITES // K_PASS
+PAIRS = SITES // (2 * P)
+TILES = SITES // P
+N_OUT = 512
+
+FLOPS = 3 * 2 * SITES * SITES * ORB
+
+
+def tile_wrap_occupied_green_s11_kernel(tc, hop_bytes, hop_scale, left, right, hinv_words, hinv_scales, field, out):
+    nc = tc.nc
+
+    with ExitStack() as ctx:
+        keep = ctx.enter_context(tc.tile_pool(name="keep", bufs=1))
+        work = ctx.enter_context(tc.tile_pool(name="work", bufs=2))
+        results = ctx.enter_context(tc.tile_pool(name="results", bufs=6))
+        psum = ctx.enter_context(tc.psum_pool(name="psum", bufs=1))
+
+        ident = keep.tile([P, P], F32)
+        warm = keep.tile([P, 1], F32)
+        scale_bc = keep.tile([P, SITES], F32)
+        scale_cols = keep.tile([P, PASSES, PACK], F32)
+        field_cols = keep.tile([P, PASSES, PACK], BF16)
+        w_cols = keep.tile([P, PASSES, PACK], F32)
+        winv_cols = keep.tile([P, PASSES, PACK], F32)
+        zeros = keep.tile([P, N_OUT], BF16)
+        w_bc = keep.tile([P, SITES], F32)
+        winv_bc = keep.tile([P, SITES], F32)
+        right_rows = keep.tile([P, PACK, SITES], BF16)
+        hinv_codes = keep.tile([P, PASSES, 2 * SITES], U8, align_bytes=64)
+        hinv_sc = keep.tile([P, PASSES, SITES], U8, align_bytes=64)
+        right_codes = keep.tile([P, 2, PASSES, 2 * P], U32, align_bytes=64)
+        right_sc = keep.tile([P, 2, PASSES, 2 * P], U8, align_bytes=64)
+        left_codes = keep.tile([P, PASSES, ORB], U32, align_bytes=64)
+        left_sc = keep.tile([P, PASSES, ORB], U8, align_bytes=64)
+        c_codes = keep.tile([P, SITES], U32, align_bytes=64)
+        c_sc = keep.tile([P, SITES], U8, align_bytes=64)
+
+        hop_raw, left_rows = {}, {}
+        hop_view = hop_bytes.rearrange("(c p s) k -> c p s k", p=P, s=2)
+        left_view = left.rearrange("(g p j) r -> g p j r", p=P, j=PACK)
+        right_view = right.rearrange("(m t) k -> m t k", t=PACK)
+        out_view = out.rearrange("(c p s) j -> c p s j", p=P, s=2)
+
+        def load_hop(c):
+            hop_tile = keep.tile([P, 2, SITES], U8, name=f"hop_raw{c}")
+            nc.sync.dma_start(out=hop_tile[:], in_=hop_view[c])
+            hop_raw[c] = hop_tile
+
+        def load_columns(cols, row):
+            nc.sync.dma_start(out=cols[:], in_=row.rearrange("(g n q) -> n g q", n=P, q=PACK))
+
+        def spread(cols, g, row_bc):
+            bank = psum.tile([P, PACK, P], F32, name="res", bufs=3)
+            for q in range(PACK):
+                nc.tensor.transpose(bank[:, q, :], cols[:, g, q : q + 1].to_broadcast([P, P]), ident[:])
+            nc.scalar.copy(
+                out=row_bc[:, K_PASS * g : K_PASS * (g + 1)].rearrange("p (n q) -> p n q", q=PACK),
+                in_=bank[:].rearrange("p q n -> p n q"),
+            )
+
+        def keep_warm(n):
+            bank = psum.tile([P, N_OUT], F32, name="res", bufs=3)
+            for x in range(n):
+                nc.tensor.matmul(bank[:], zeros[:, 0:P], zeros[:], start=True, stop=True)
+
+        def load_left(g):
+            left_tile = keep.tile([P, PACK, ORB], BF16, name=f"left_rows{g}")
+            nc.sync.dma_start(out=left_tile[:], in_=left_view[g])
+            left_rows[g] = left_tile
+
+        def load_right(h):
+            nc.sync.dma_start(out=right_rows[:, 2 * h : 2 * h + 2, :], in_=right_view[:, 2 * h : 2 * h + 2, :])
+
+        hop_bf, hop_grouped, hop_codes, hop_sc = {}, {}, {}, {}
+
+        def widen(i, g0=0, g1=PASSES):
+            if g0 == 0:
+                bf_tile = work.tile([P, SITES], BF16, name="hop_bf", bufs=4)
+                hop_bf[i] = bf_tile
+            k = slice(K_PASS * g0, K_PASS * g1)
+            nc.vector.tensor_tensor(out=hop_bf[i][:, k], in0=hop_raw[i // 2][:, i % 2, k].bitcast(FP8), in1=scale_bc[:, k], op=MULT)
+
+        def turn(rows_of_slot, grouped, slots, copy):
+            for b in range(0, slots, 2):
+                n = min(2, slots - b)
+                bank = psum.tile([P, 2, 2, P], F32, name="turned", bufs=3)
+                for l in range(n):
+                    words = rows_of_slot(b + l)
+                    for u in range(2):
+                        nc.tensor.transpose(bank[:, l, u, :], words[:, u : 2 * P : 2], ident[:])
+                copy(
+                    out=grouped[:, b : b + n, :].bitcast(F32).rearrange("p l (r u) -> p l r u", u=2),
+                    in_=bank[:, 0:n, :, :].rearrange("p l u r -> p l r u"),
+                )
+
+        def turn_hop(i):
+            grouped = work.tile([P, PASSES, K_PASS], BF16, name="hop_grouped", align_bytes=64, bufs=4)
+            hop_grouped[i] = grouped
+            turn(lambda g: hop_bf[i][:, K_PASS * g : K_PASS * (g + 1)].bitcast(F32), grouped, PASSES, S)
+
+        def quantize_slots(grouped, codes, sc, spans):
+            flat = grouped[:].rearrange("p l k -> p (l k)")
+            for a, b in spans:
+                nc.vector.quantize_mx(out=codes[:, a // 4 : b // 4].bitcast(E4M3X4), scales=sc[:, a // 4 : b // 4], in_=flat[:, a:b])
+
+        def quantize_hop(i):
+            code_tile = keep.tile([P, PASSES * P], U32, name=f"hop_codes{i}", align_bytes=64)
+            sc_tile = keep.tile([P, PASSES * P], U8, name=f"hop_sc{i}", align_bytes=64)
+            hop_codes[i], hop_sc[i] = code_tile, sc_tile
+            quantize_slots(hop_grouped[i], code_tile, sc_tile, ((0, 1024), (1024, 1536)))
+
+        right_grouped = {}
+
+        def turn_right(h):
+            grouped = work.tile([P, 2 * PASSES, K_PASS], BF16, name="right_grouped", align_bytes=64)
+            right_grouped[h] = grouped
+            turn(lambda i: right_rows[:, 2 * h + i % 2, K_PASS * (i // 2) : K_PASS * (i // 2 + 1)].bitcast(F32), grouped, 2 * PASSES, S)
+
+        def quantize_right(h):
+            quantize_slots(
+                right_grouped[h],
+                right_codes[:, h, :, :].rearrange("p g m -> p (g m)"),
+                right_sc[:, h, :, :].rearrange("p g m -> p (g m)"),
+                ((0, 2048), (2048, 3072)),
+            )
+
+        def load_hinv(h):
+            cols = slice(SITES * h, SITES * (h + 1))
+            nc.sync.dma_start(out=hinv_codes[:, :, cols], in_=hinv_words[:, :, cols].rearrange("g p n -> p g n"))
+
+        left_grouped = {}
+
+        def interleave_left(g, engine_copy):
+            grouped = work.tile([P, ORB * PACK], BF16, name="left_grouped", align_bytes=64)
+            left_grouped[g] = grouped
+            engine_copy(
+                out=grouped[:].rearrange("p (t m j) -> p t m j", t=PACK, j=PACK),
+                in_=left_rows[g][:].rearrange("p j (m t) -> p t m j", t=PACK),
+            )
+
+        def quantize_left(g):
+            nc.vector.quantize_mx(out=left_codes[:, g, :].bitcast(E4M3X4), scales=left_sc[:, g, :], in_=left_grouped[g][:])
+
+        c_acc, c_grouped, a_acc, a_grouped, a_codes, a_sc = {}, {}, {}, {}, {}, {}
+
+        def mult_c(n):
+            acc = psum.tile([P, PACK, P], F32, name="acc", bufs=2)
+            c_acc[n] = acc
+            for t in range(PACK):
+                for g in range(PASSES):
+                    m = P * (t % 2)
+                    nc.tensor.matmul_mx(
+                        out=acc[:, t, :],
+                        lhsT=right_codes[:, t // 2, g, m : m + P].bitcast(E4M3X4),
+                        lhsT_scale=right_sc[:, t // 2, g, m : m + P],
+                        rhs=hinv_codes[:, g, 2 * P * n : 2 * P * (n + 1)].bitcast(E2M1X4),
+                        rhs_scale=hinv_sc[:, g, P * n : P * (n + 1)],
+                        start=(g == 0),
+                        stop=(g == PASSES - 1),
+                    )
+
+        def empty_c(n):
+            if n % 2 == 0:
+                grouped = work.tile([P, 2, P, PACK], BF16, name="c_grouped", align_bytes=64)
+                c_grouped[n // 2] = grouped
+            nc.vector.tensor_tensor(
+                out=c_grouped[n // 2][:, n % 2, :, :],
+                in0=c_acc[n][:].rearrange("p t n -> p n t"),
+                in1=winv_bc[:, P * n : P * (n + 1)].unsqueeze(2).to_broadcast([P, P, PACK]),
+                op=MULT,
+            )
+
+        def quantize_c(q):
+            cols = slice(2 * P * q, 2 * P * (q + 1))
+            nc.vector.quantize_mx(
+                out=c_codes[:, cols].bitcast(E4M3X4),
+                scales=c_sc[:, cols],
+                in_=c_grouped[q][:].rearrange("p s n t -> p (s n t)"),
+            )
+
+        def mult_a(i):
+            acc = psum.tile([P, PACK, P], F32, name="acc", bufs=2)
+            a_acc[i] = acc
+            for t in range(PACK):
+                for g in range(PASSES):
+                    cols = slice(g * P, (g + 1) * P)
+                    nc.tensor.matmul_mx(
+                        out=acc[:, t, :],
+                        lhsT=left_codes[:, g, P * t : P * (t + 1)].bitcast(E4M3X4),
+                        lhsT_scale=left_sc[:, g, P * t : P * (t + 1)],
+                        rhs=hop_codes[i][:, cols].bitcast(E4M3X4),
+                        rhs_scale=hop_sc[i][:, cols],
+                        start=(g == 0),
+                        stop=(g == PASSES - 1),
+                    )
+
+        def empty_a(i):
+            grouped = work.tile([P, P, PACK], BF16, name="a_grouped", align_bytes=64, bufs=3)
+            a_grouped[i] = grouped
+            w0 = 2 * P * (i // 2) + i % 2
+            nc.vector.tensor_tensor(
+                out=grouped[:],
+                in0=a_acc[i][:].rearrange("p t n -> p n t"),
+                in1=w_bc[:, w0 : w0 + 2 * P - 1 : 2].unsqueeze(2).to_broadcast([P, P, PACK]),
+                op=MULT,
+            )
+
+        def quantize_a(i):
+            code_tile = work.tile([P, P], U32, name="a_codes", align_bytes=64, bufs=3)
+            sc_tile = work.tile([P, P], U8, name="a_sc", align_bytes=64, bufs=3)
+            a_codes[i], a_sc[i] = code_tile, sc_tile
+            nc.vector.quantize_mx(out=code_tile[:].bitcast(E4M3X4), scales=sc_tile[:], in_=a_grouped[i][:].rearrange("p n t -> p (n t)"))
+
+        def finish(i, copies):
+            result = results.tile([P, SITES], F32, name="result")
+            for q in range(SITES // N_OUT):
+                cols = slice(N_OUT * q, N_OUT * (q + 1))
+                bank = psum.tile([P, N_OUT], F32, name="res", bufs=3)
+                nc.tensor.matmul_mx(
+                    out=bank[:],
+                    lhsT=a_codes[i][:].bitcast(E4M3X4),
+                    lhsT_scale=a_sc[i][:],
+                    rhs=c_codes[:, cols].bitcast(E4M3X4),
+                    rhs_scale=c_sc[:, cols],
+                    start=True,
+                    stop=True,
+                )
+                copies[q](out=result[:, cols], in_=bank[:])
+                if i >= TILES - 2:
+                    nc.sync.dma_start(out=out_view[i // 2, :, i % 2, cols], in_=result[:, cols])
+            if i < TILES - 2:
+                nc.sync.dma_start(out=out_view[i // 2, :, i % 2, :], in_=result[:])
+
+        S = nc.scalar.copy
+        V = nc.vector.tensor_copy
+
+        with tc.manual_schedule():
+            nc.vector.memset(zeros[:].bitcast(U32), 0)
+            nc.gpsimd.memset(warm[:], 0.0)
+            make_identity(nc, ident[:])
+            nc.vector.memset(hinv_sc[:].rearrange("p g n -> p (g n)").bitcast(U32), 0)
+            load_columns(scale_cols, hop_scale.rearrange("o k -> (o k)"))
+            load_hop(0)
+            load_columns(field_cols, field)
+            load_right(0)
+            load_hop(1)
+            load_right(1)
+            for q in range(4):
+                nc.sync.dma_start(
+                    out=hinv_sc[32 * q : 32 * q + 4, :, :].bitcast(I32),
+                    in_=hinv_scales[:, 4 * q : 4 * q + 4, :].rearrange("g q n -> q g n").bitcast(I32),
+                )
+            load_hinv(0)
+            load_left(0)
+            load_hinv(1)
+            load_left(1)
+            load_left(2)
+            load_hop(2)
+            load_hop(3)
+            load_hop(4)
+            load_hop(5)
+
+            nc.scalar.activation(out=warm[:], in_=warm[:], func=EXP)
+
+            keep_warm(4)
+            for g in range(PASSES):
+                spread(scale_cols, g, scale_bc)
+                widen(0, g, g + 1)
+            nc.scalar.activation(out=winv_cols[:], in_=field_cols[:], func=EXP, scale=-1.0)
+            nc.scalar.activation(out=w_cols[:], in_=field_cols[:], func=EXP)
+            keep_warm(2)
+            turn_hop(0)
+            widen(1)
+
+            keep_warm(2)
+            turn_right(0)
+            keep_warm(2)
+            turn_hop(1)
+            widen(2)
+            quantize_right(0)
+            turn_right(1)
+            quantize_right(1)
+            for g in range(PASSES):
+                spread(winv_cols, g, winv_bc)
+            keep_warm(2)
+            quantize_hop(0)
+            H = {"w":{3:0},"t":{2:5},"q":{1:0},"li":{0:0,1:1,2:2},"w_bc":3,"lq":{0:2,1:3,2:4}}
+            for q in range(6):
+                mult_c(2 * q)
+                mult_c(2 * q + 1)
+                for x, at in H["w"].items():
+                    if at == q:
+                        widen(x)
+                empty_c(2 * q)
+                for x, at in H["q"].items():
+                    if at == q:
+                        quantize_hop(x)
+                for x, at in H["t"].items():
+                    if at == q:
+                        turn_hop(x)
+                empty_c(2 * q + 1)
+                for x, at in H["li"].items():
+                    if at == q:
+                        interleave_left(x, S)
+                if q == H["w_bc"]:
+                    for g in range(PASSES):
+                        spread(w_cols, g, w_bc)
+                for x, at in H["lq"].items():
+                    if at == q:
+                        quantize_left(x)
+                quantize_c(q)
+            for i in range(TILES + 1):
+                if i + 4 < TILES:
+                    widen(i + 4)
+                if i < TILES:
+                    mult_a(i)
+                if i + 3 < TILES:
+                    turn_hop(i + 3)
+                if i < TILES:
+                    empty_a(i)
+                if i > 0:
+                    finish(i - 1, (S, V, S) if i > 9 else (S, S, S))
+                if i + 2 < TILES:
+                    quantize_hop(i + 2)
+                if i < TILES:
+                    quantize_a(i)

@@ -20,9 +20,9 @@ P = 128
 PACK = 4
 K_PASS = P * PACK
 PASSES = SITES // K_PASS
-PAIRS = SITES // (2 * P)
 TILES = SITES // P
-N_OUT = 512
+BANK = 512
+CHUNKS = SITES // BANK
 
 FLOPS = 3 * 2 * SITES * SITES * ORB
 
@@ -33,130 +33,137 @@ def tile_wrap_occupied_green_s11_kernel(tc, hop_bytes, hop_scale, left, right, h
     with ExitStack() as ctx:
         keep = ctx.enter_context(tc.tile_pool(name="keep", bufs=1))
         work = ctx.enter_context(tc.tile_pool(name="work", bufs=2))
-        results = ctx.enter_context(tc.tile_pool(name="results", bufs=6))
+        results = ctx.enter_context(tc.tile_pool(name="results", bufs=5))
         psum = ctx.enter_context(tc.psum_pool(name="psum", bufs=1))
 
         ident = keep.tile([P, P], F32)
-        warm = keep.tile([P, 1], F32)
-        scale_bc = keep.tile([P, SITES], F32)
+        table = keep.tile([P, 1], F32)
+        ones = keep.tile([P, BANK], BF16)
+        field_row = keep.tile([P, SITES], BF16)
         scale_cols = keep.tile([P, PASSES, PACK], F32)
-        field_cols = keep.tile([P, PASSES, PACK], BF16)
-        w_cols = keep.tile([P, PASSES, PACK], F32)
-        winv_cols = keep.tile([P, PASSES, PACK], F32)
-        zeros = keep.tile([P, N_OUT], BF16)
+        scale_bc = keep.tile([P, SITES], F32)
         w_bc = keep.tile([P, SITES], F32)
         winv_bc = keep.tile([P, SITES], F32)
-        right_rows = keep.tile([P, PACK, SITES], BF16)
-        hinv_codes = keep.tile([P, PASSES, 2 * SITES], U8, align_bytes=64)
         hinv_sc = keep.tile([P, PASSES, SITES], U8, align_bytes=64)
-        right_codes = keep.tile([P, 2, PASSES, 2 * P], U32, align_bytes=64)
-        right_sc = keep.tile([P, 2, PASSES, 2 * P], U8, align_bytes=64)
         left_codes = keep.tile([P, PASSES, ORB], U32, align_bytes=64)
         left_sc = keep.tile([P, PASSES, ORB], U8, align_bytes=64)
         c_codes = keep.tile([P, SITES], U32, align_bytes=64)
         c_sc = keep.tile([P, SITES], U8, align_bytes=64)
 
-        hop_raw, left_rows = {}, {}
-        hop_view = hop_bytes.rearrange("(c p s) k -> c p s k", p=P, s=2)
-        left_view = left.rearrange("(g p j) r -> g p j r", p=P, j=PACK)
-        right_view = right.rearrange("(m t) k -> m t k", t=PACK)
-        out_view = out.rearrange("(c p s) j -> c p s j", p=P, s=2)
+        hop_raw, left_rows, right_rows, hinv_codes = {}, {}, {}, {}
 
-        def load_hop(c):
-            hop_tile = keep.tile([P, 2, SITES], U8, name=f"hop_raw{c}")
-            nc.sync.dma_start(out=hop_tile[:], in_=hop_view[c])
-            hop_raw[c] = hop_tile
-
-        def load_columns(cols, row):
-            nc.sync.dma_start(out=cols[:], in_=row.rearrange("(g n q) -> n g q", n=P, q=PACK))
-
-        def spread(cols, g, row_bc):
-            bank = psum.tile([P, PACK, P], F32, name="res", bufs=3)
-            for q in range(PACK):
-                nc.tensor.transpose(bank[:, q, :], cols[:, g, q : q + 1].to_broadcast([P, P]), ident[:])
-            nc.scalar.copy(
-                out=row_bc[:, K_PASS * g : K_PASS * (g + 1)].rearrange("p (n q) -> p n q", q=PACK),
-                in_=bank[:].rearrange("p q n -> p n q"),
-            )
-
-        def keep_warm(n):
-            bank = psum.tile([P, N_OUT], F32, name="res", bufs=3)
-            for x in range(n):
-                nc.tensor.matmul(bank[:], zeros[:, 0:P], zeros[:], start=True, stop=True)
+        def load_hop(i0, i1):
+            rows = keep.tile([P, i1 - i0, SITES], U8, name=f"hop_raw{i0}")
+            nc.sync.dma_start(out=rows[:], in_=hop_bytes[P * i0 : P * i1, :].rearrange("(s p) k -> p s k", p=P))
+            for i in range(i0, i1):
+                hop_raw[i] = rows[:, i - i0, :]
 
         def load_left(g):
-            left_tile = keep.tile([P, PACK, ORB], BF16, name=f"left_rows{g}")
-            nc.sync.dma_start(out=left_tile[:], in_=left_view[g])
-            left_rows[g] = left_tile
+            rows = keep.tile([P, PACK, ORB], BF16, name=f"left_rows{g}")
+            nc.sync.dma_start(out=rows[:], in_=left.rearrange("(g p j) r -> g p j r", p=P, j=PACK)[g])
+            left_rows[g] = rows
 
-        def load_right(h):
-            nc.sync.dma_start(out=right_rows[:, 2 * h : 2 * h + 2, :], in_=right_view[:, 2 * h : 2 * h + 2, :])
+        def load_right(t):
+            rows = keep.tile([P, SITES], BF16, name=f"right_rows{t}")
+            nc.sync.dma_start(out=rows[:], in_=right.rearrange("(m t) k -> t m k", t=PACK)[t])
+            right_rows[t] = rows
 
-        hop_bf, hop_grouped, hop_codes, hop_sc = {}, {}, {}, {}
+        def load_hinv(q):
+            words = keep.tile([P, PASSES, 2 * BANK], U8, name=f"hinv_codes{q}", align_bytes=64)
+            nc.sync.dma_start(out=words[:], in_=hinv_words[:, :, 2 * BANK * q : 2 * BANK * (q + 1)].rearrange("g p n -> p g n"))
+            hinv_codes[q] = words
+
+        def load_hinv_scales():
+            for q in range(4):
+                nc.sync.dma_start(
+                    out=hinv_sc[32 * q : 32 * q + 4, :, :].bitcast(I32),
+                    in_=hinv_scales[:, 4 * q : 4 * q + 4, :].rearrange("g q n -> q g n").bitcast(I32),
+                )
+
+        def wide_bank():
+            return psum.tile([P, BANK], F32, name="wide", bufs=3)
+
+        def sum_bank():
+            return psum.tile([P, BANK], F32, name="sums", bufs=2)
+
+        def warm_up(n):
+            bank = wide_bank()
+            for x in range(n):
+                nc.tensor.matmul(bank[:], ones[:, 0:P], ones[:], start=True, stop=True)
+
+        def spread_scale(g):
+            bank = wide_bank()
+            for q in range(PACK):
+                nc.tensor.transpose(bank[:, P * q : P * (q + 1)], scale_cols[:, g, q : q + 1].to_broadcast([P, P]), ident[:])
+            nc.scalar.copy(
+                out=scale_bc[:, K_PASS * g : K_PASS * (g + 1)].rearrange("p (n q) -> p n q", q=PACK),
+                in_=bank[:].rearrange("p (q n) -> p n q", q=PACK),
+            )
+
+        field_bank = {}
+
+        def spread_field(q, bank):
+            field_bank[q] = bank
+            nc.tensor.matmul(bank[:], ones[:, 0:P], field_row[:, BANK * q : BANK * (q + 1)], start=True, stop=True)
+
+        def exp_field(q, row_bc, sign):
+            nc.scalar.activation(out=row_bc[:, BANK * q : BANK * (q + 1)], in_=field_bank[q][:], func=EXP, scale=sign)
+
+        hop_bf, turned, hop_codes, hop_sc, right_codes, right_sc = {}, {}, {}, {}, {}, {}
 
         def widen(i, g0=0, g1=PASSES):
             if g0 == 0:
-                bf_tile = work.tile([P, SITES], BF16, name="hop_bf", bufs=4)
-                hop_bf[i] = bf_tile
+                wide = work.tile([P, SITES], BF16, name="hop_bf", bufs=5)
+                hop_bf[i] = wide
             k = slice(K_PASS * g0, K_PASS * g1)
-            nc.vector.tensor_tensor(out=hop_bf[i][:, k], in0=hop_raw[i // 2][:, i % 2, k].bitcast(FP8), in1=scale_bc[:, k], op=MULT)
+            nc.vector.tensor_tensor(out=hop_bf[i][:, k], in0=hop_raw[i][:, k].bitcast(FP8), in1=scale_bc[:, k], op=MULT)
 
-        def turn(rows_of_slot, grouped, slots, copy):
-            for b in range(0, slots, 2):
-                n = min(2, slots - b)
-                bank = psum.tile([P, 2, 2, P], F32, name="turned", bufs=3)
-                for l in range(n):
-                    words = rows_of_slot(b + l)
+        def turn(rows, key):
+            grouped = work.tile([P, SITES], BF16, name="turned_sb", align_bytes=64, bufs=5)
+            turned[key] = grouped
+            words = rows[:].bitcast(F32)
+            for g0, g1 in ((0, 2), (2, 3)):
+                bank = psum.tile([P, 2, 2, P], F32, name="turned_ps", bufs=3)
+                for g in range(g0, g1):
                     for u in range(2):
-                        nc.tensor.transpose(bank[:, l, u, :], words[:, u : 2 * P : 2], ident[:])
-                copy(
-                    out=grouped[:, b : b + n, :].bitcast(F32).rearrange("p l (r u) -> p l r u", u=2),
-                    in_=bank[:, 0:n, :, :].rearrange("p l u r -> p l r u"),
+                        nc.tensor.transpose(bank[:, g - g0, u, :], words[:, 2 * P * g + u : 2 * P * (g + 1) : 2], ident[:])
+                nc.scalar.copy(
+                    out=grouped[:, K_PASS * g0 : K_PASS * g1].bitcast(F32).rearrange("p (l r u) -> p l r u", r=P, u=2),
+                    in_=bank[:, 0 : g1 - g0, :, :].rearrange("p l u r -> p l r u"),
                 )
 
-        def turn_hop(i):
-            grouped = work.tile([P, PASSES, K_PASS], BF16, name="hop_grouped", align_bytes=64, bufs=4)
-            hop_grouped[i] = grouped
-            turn(lambda g: hop_bf[i][:, K_PASS * g : K_PASS * (g + 1)].bitcast(F32), grouped, PASSES, S)
+        def quantize_turned(key, codes, sc):
+            for a, b in ((0, 2 * P), (2 * P, 3 * P)):
+                nc.vector.quantize_mx(out=codes[:, a:b].bitcast(E4M3X4), scales=sc[:, a:b], in_=turned[key][:, PACK * a : PACK * b])
 
-        def quantize_slots(grouped, codes, sc, spans):
-            flat = grouped[:].rearrange("p l k -> p (l k)")
-            for a, b in spans:
-                nc.vector.quantize_mx(out=codes[:, a // 4 : b // 4].bitcast(E4M3X4), scales=sc[:, a // 4 : b // 4], in_=flat[:, a:b])
+        def turn_hop(i):
+            turn(hop_bf[i], ("hop", i))
+
+        def turn_right(t):
+            turn(right_rows[t], ("right", t))
 
         def quantize_hop(i):
-            code_tile = keep.tile([P, PASSES * P], U32, name=f"hop_codes{i}", align_bytes=64)
-            sc_tile = keep.tile([P, PASSES * P], U8, name=f"hop_sc{i}", align_bytes=64)
-            hop_codes[i], hop_sc[i] = code_tile, sc_tile
-            quantize_slots(hop_grouped[i], code_tile, sc_tile, ((0, 1024), (1024, 1536)))
+            codes = work.tile([P, PASSES * P], U32, name="hop_codes", align_bytes=64, bufs=4)
+            sc = work.tile([P, PASSES * P], U8, name="hop_sc", align_bytes=64, bufs=4)
+            hop_codes[i], hop_sc[i] = codes, sc
+            quantize_turned(("hop", i), codes, sc)
 
-        right_grouped = {}
-
-        def turn_right(h):
-            grouped = work.tile([P, 2 * PASSES, K_PASS], BF16, name="right_grouped", align_bytes=64)
-            right_grouped[h] = grouped
-            turn(lambda i: right_rows[:, 2 * h + i % 2, K_PASS * (i // 2) : K_PASS * (i // 2 + 1)].bitcast(F32), grouped, 2 * PASSES, S)
-
-        def quantize_right(h):
-            quantize_slots(
-                right_grouped[h],
-                right_codes[:, h, :, :].rearrange("p g m -> p (g m)"),
-                right_sc[:, h, :, :].rearrange("p g m -> p (g m)"),
-                ((0, 2048), (2048, 3072)),
-            )
-
-        def load_hinv(h):
-            cols = slice(SITES * h, SITES * (h + 1))
-            nc.sync.dma_start(out=hinv_codes[:, :, cols], in_=hinv_words[:, :, cols].rearrange("g p n -> p g n"))
+        def quantize_right(t):
+            codes = keep.tile([P, PASSES * P], U32, name=f"right_codes{t}", align_bytes=64)
+            sc = keep.tile([P, PASSES * P], U8, name=f"right_sc{t}", align_bytes=64)
+            right_codes[t], right_sc[t] = codes, sc
+            quantize_turned(("right", t), codes, sc)
 
         left_grouped = {}
 
-        def interleave_left(g, engine_copy):
-            grouped = work.tile([P, ORB * PACK], BF16, name="left_grouped", align_bytes=64)
-            left_grouped[g] = grouped
-            engine_copy(
-                out=grouped[:].rearrange("p (t m j) -> p t m j", t=PACK, j=PACK),
-                in_=left_rows[g][:].rearrange("p j (m t) -> p t m j", t=PACK),
+        def interleave_left(g, h, copy):
+            if h == 0:
+                grouped = work.tile([P, ORB * PACK], BF16, name="left_grouped", align_bytes=64)
+                left_grouped[g] = grouped
+            m = slice(P // 2 * h, P // 2 * (h + 1))
+            copy(
+                out=left_grouped[g][:].rearrange("p (t m j) -> p m t j", t=PACK, j=PACK)[:, m, :, :],
+                in_=left_rows[g][:].rearrange("p j (m t) -> p m t j", t=PACK)[:, m, :, :],
             )
 
         def quantize_left(g):
@@ -164,17 +171,16 @@ def tile_wrap_occupied_green_s11_kernel(tc, hop_bytes, hop_scale, left, right, h
 
         c_acc, c_grouped, a_acc, a_grouped, a_codes, a_sc = {}, {}, {}, {}, {}, {}
 
-        def mult_c(n):
-            acc = psum.tile([P, PACK, P], F32, name="acc", bufs=2)
+        def mult_c(n, acc):
             c_acc[n] = acc
+            q, m = divmod(n, BANK // P)
             for t in range(PACK):
                 for g in range(PASSES):
-                    m = P * (t % 2)
                     nc.tensor.matmul_mx(
-                        out=acc[:, t, :],
-                        lhsT=right_codes[:, t // 2, g, m : m + P].bitcast(E4M3X4),
-                        lhsT_scale=right_sc[:, t // 2, g, m : m + P],
-                        rhs=hinv_codes[:, g, 2 * P * n : 2 * P * (n + 1)].bitcast(E2M1X4),
+                        out=acc[:, P * t : P * (t + 1)],
+                        lhsT=right_codes[t][:, P * g : P * (g + 1)].bitcast(E4M3X4),
+                        lhsT_scale=right_sc[t][:, P * g : P * (g + 1)],
+                        rhs=hinv_codes[q][:, g, 2 * P * m : 2 * P * (m + 1)].bitcast(E2M1X4),
                         rhs_scale=hinv_sc[:, g, P * n : P * (n + 1)],
                         start=(g == 0),
                         stop=(g == PASSES - 1),
@@ -186,27 +192,27 @@ def tile_wrap_occupied_green_s11_kernel(tc, hop_bytes, hop_scale, left, right, h
                 c_grouped[n // 2] = grouped
             nc.vector.tensor_tensor(
                 out=c_grouped[n // 2][:, n % 2, :, :],
-                in0=c_acc[n][:].rearrange("p t n -> p n t"),
+                in0=c_acc[n][:].rearrange("p (t n) -> p n t", t=PACK),
                 in1=winv_bc[:, P * n : P * (n + 1)].unsqueeze(2).to_broadcast([P, P, PACK]),
                 op=MULT,
             )
 
-        def quantize_c(q):
-            cols = slice(2 * P * q, 2 * P * (q + 1))
+        def quantize_c(pair):
+            cols = slice(2 * P * pair, 2 * P * (pair + 1))
             nc.vector.quantize_mx(
                 out=c_codes[:, cols].bitcast(E4M3X4),
                 scales=c_sc[:, cols],
-                in_=c_grouped[q][:].rearrange("p s n t -> p (s n t)"),
+                in_=c_grouped[pair][:].rearrange("p s n t -> p (s n t)"),
             )
 
         def mult_a(i):
-            acc = psum.tile([P, PACK, P], F32, name="acc", bufs=2)
+            acc = sum_bank()
             a_acc[i] = acc
             for t in range(PACK):
                 for g in range(PASSES):
                     cols = slice(g * P, (g + 1) * P)
                     nc.tensor.matmul_mx(
-                        out=acc[:, t, :],
+                        out=acc[:, P * t : P * (t + 1)],
                         lhsT=left_codes[:, g, P * t : P * (t + 1)].bitcast(E4M3X4),
                         lhsT_scale=left_sc[:, g, P * t : P * (t + 1)],
                         rhs=hop_codes[i][:, cols].bitcast(E4M3X4),
@@ -218,25 +224,25 @@ def tile_wrap_occupied_green_s11_kernel(tc, hop_bytes, hop_scale, left, right, h
         def empty_a(i):
             grouped = work.tile([P, P, PACK], BF16, name="a_grouped", align_bytes=64, bufs=3)
             a_grouped[i] = grouped
-            w0 = 2 * P * (i // 2) + i % 2
             nc.vector.tensor_tensor(
                 out=grouped[:],
-                in0=a_acc[i][:].rearrange("p t n -> p n t"),
-                in1=w_bc[:, w0 : w0 + 2 * P - 1 : 2].unsqueeze(2).to_broadcast([P, P, PACK]),
+                in0=a_acc[i][:].rearrange("p (t n) -> p n t", t=PACK),
+                in1=w_bc[:, P * i : P * (i + 1)].unsqueeze(2).to_broadcast([P, P, PACK]),
                 op=MULT,
             )
 
         def quantize_a(i):
-            code_tile = work.tile([P, P], U32, name="a_codes", align_bytes=64, bufs=3)
-            sc_tile = work.tile([P, P], U8, name="a_sc", align_bytes=64, bufs=3)
-            a_codes[i], a_sc[i] = code_tile, sc_tile
-            nc.vector.quantize_mx(out=code_tile[:].bitcast(E4M3X4), scales=sc_tile[:], in_=a_grouped[i][:].rearrange("p n t -> p (n t)"))
+            codes = work.tile([P, P], U32, name="a_codes", align_bytes=64, bufs=3)
+            sc = work.tile([P, P], U8, name="a_sc", align_bytes=64, bufs=3)
+            a_codes[i], a_sc[i] = codes, sc
+            nc.vector.quantize_mx(out=codes[:].bitcast(E4M3X4), scales=sc[:], in_=a_grouped[i][:].rearrange("p n t -> p (n t)"))
 
-        def finish(i, copies):
+        def finish(i, copies, by_bank):
             result = results.tile([P, SITES], F32, name="result")
-            for q in range(SITES // N_OUT):
-                cols = slice(N_OUT * q, N_OUT * (q + 1))
-                bank = psum.tile([P, N_OUT], F32, name="res", bufs=3)
+            rows = slice(P * i, P * (i + 1))
+            for q in range(CHUNKS):
+                cols = slice(BANK * q, BANK * (q + 1))
+                bank = wide_bank()
                 nc.tensor.matmul_mx(
                     out=bank[:],
                     lhsT=a_codes[i][:].bitcast(E4M3X4),
@@ -247,101 +253,95 @@ def tile_wrap_occupied_green_s11_kernel(tc, hop_bytes, hop_scale, left, right, h
                     stop=True,
                 )
                 copies[q](out=result[:, cols], in_=bank[:])
-                if i >= TILES - 2:
-                    nc.sync.dma_start(out=out_view[i // 2, :, i % 2, cols], in_=result[:, cols])
-            if i < TILES - 2:
-                nc.sync.dma_start(out=out_view[i // 2, :, i % 2, :], in_=result[:])
+                if by_bank:
+                    nc.sync.dma_start(out=out[rows, cols], in_=result[:, cols])
+            if not by_bank:
+                nc.sync.dma_start(out=out[rows, :], in_=result[:])
 
         S = nc.scalar.copy
         V = nc.vector.tensor_copy
 
         with tc.manual_schedule():
-            nc.vector.memset(zeros[:].bitcast(U32), 0)
-            nc.gpsimd.memset(warm[:], 0.0)
+            nc.vector.memset(ones[:], 1.0)
+            nc.vector.memset(field_row[:].bitcast(U32), 0)
+            nc.gpsimd.memset(table[:], 0.0)
             make_identity(nc, ident[:])
-            nc.vector.memset(hinv_sc[:].rearrange("p g n -> p (g n)").bitcast(U32), 0)
-            load_columns(scale_cols, hop_scale.rearrange("o k -> (o k)"))
-            load_hop(0)
-            load_columns(field_cols, field)
+            nc.gpsimd.memset(hinv_sc[:].rearrange("p g n -> p (g n)").bitcast(U32), 0)
+            nc.sync.dma_start(out=scale_cols[:], in_=hop_scale.rearrange("o (g n q) -> n (o g) q", n=P, q=PACK))
+            load_hop(0, 1)
+            nc.sync.dma_start(out=field_row[0:1, :], in_=field.rearrange("(o k) -> o k", o=1))
             load_right(0)
-            load_hop(1)
-            load_right(1)
-            for q in range(4):
-                nc.sync.dma_start(
-                    out=hinv_sc[32 * q : 32 * q + 4, :, :].bitcast(I32),
-                    in_=hinv_scales[:, 4 * q : 4 * q + 4, :].rearrange("g q n -> q g n").bitcast(I32),
-                )
+            load_hop(1, 3)
+            for t in range(1, PACK):
+                load_right(t)
+            load_hinv_scales()
             load_hinv(0)
             load_left(0)
+            load_hop(3, 5)
             load_hinv(1)
             load_left(1)
             load_left(2)
-            load_hop(2)
-            load_hop(3)
-            load_hop(4)
-            load_hop(5)
+            load_hinv(2)
+            load_hop(5, 8)
+            load_hop(8, 12)
 
-            nc.scalar.activation(out=warm[:], in_=warm[:], func=EXP)
-
-            keep_warm(4)
+            nc.scalar.activation(out=table[:], in_=table[:], func=EXP)
+            warm_up(4)
             for g in range(PASSES):
-                spread(scale_cols, g, scale_bc)
+                spread_scale(g)
                 widen(0, g, g + 1)
-            nc.scalar.activation(out=winv_cols[:], in_=field_cols[:], func=EXP, scale=-1.0)
-            nc.scalar.activation(out=w_cols[:], in_=field_cols[:], func=EXP)
-            keep_warm(2)
-            turn_hop(0)
-            widen(1)
-
-            keep_warm(2)
+            spread_field(0, sum_bank())
             turn_right(0)
-            keep_warm(2)
-            turn_hop(1)
-            widen(2)
+            exp_field(0, winv_bc, -1.0)
+            exp_field(0, w_bc, 1.0)
+            spread_field(1, sum_bank())
+            spread_field(2, wide_bank())
+            widen(1)
             quantize_right(0)
             turn_right(1)
+            turn_hop(0)
             quantize_right(1)
-            for g in range(PASSES):
-                spread(winv_cols, g, winv_bc)
-            keep_warm(2)
+            widen(2, 0, 2)
+            turn_right(2)
+            turn_right(3)
+            quantize_right(2)
+            widen(2, 2, 3)
+            quantize_right(3)
+            exp_field(2, winv_bc, -1.0)
+            exp_field(2, w_bc, 1.0)
+            exp_field(1, winv_bc, -1.0)
+            exp_field(1, w_bc, 1.0)
             quantize_hop(0)
-            H = {"w":{3:0},"t":{2:5},"q":{1:0},"li":{0:0,1:1,2:2},"w_bc":3,"lq":{0:2,1:3,2:4}}
-            for q in range(6):
-                mult_c(2 * q)
-                mult_c(2 * q + 1)
-                for x, at in H["w"].items():
-                    if at == q:
-                        widen(x)
-                empty_c(2 * q)
-                for x, at in H["q"].items():
-                    if at == q:
-                        quantize_hop(x)
-                for x, at in H["t"].items():
-                    if at == q:
-                        turn_hop(x)
-                empty_c(2 * q + 1)
-                for x, at in H["li"].items():
-                    if at == q:
-                        interleave_left(x, S)
-                if q == H["w_bc"]:
-                    for g in range(PASSES):
-                        spread(w_cols, g, w_bc)
-                for x, at in H["lq"].items():
-                    if at == q:
-                        quantize_left(x)
-                quantize_c(q)
+            banks = (wide_bank, wide_bank, sum_bank, sum_bank, wide_bank)
+            for n in range(TILES):
+                mult_c(n, banks[n % 5]())
+                if n in (2, 6):
+                    turn_hop(1 + n // 4)
+                empty_c(n)
+                if n < 6:
+                    interleave_left(n // 2, n % 2, S)
+                if n < 6:
+                    widen(3 + n // 3, n % 3, n % 3 + 1)
+                if n in (4, 6, 8):
+                    quantize_left((n - 4) // 2)
+                if n == 9:
+                    quantize_hop(1)
+                if n >= 2 and n % 2 == 0:
+                    quantize_c(n // 2 - 1)
             for i in range(TILES + 1):
-                if i + 4 < TILES:
-                    widen(i + 4)
                 if i < TILES:
                     mult_a(i)
-                if i + 3 < TILES:
-                    turn_hop(i + 3)
+                if 0 < i < TILES - 4:
+                    widen(i + 4)
                 if i < TILES:
                     empty_a(i)
-                if i > 0:
-                    finish(i - 1, (S, V, S) if i > 9 else (S, S, S))
                 if i + 2 < TILES:
                     quantize_hop(i + 2)
+                if i == 0:
+                    quantize_c(5)
+                if i > 0:
+                    finish(i - 1, (S, V, S) if i > 9 else (S, S, S), i > 8)
+                if i + 3 < TILES:
+                    turn_hop(i + 3)
                 if i < TILES:
                     quantize_a(i)

@@ -44,13 +44,12 @@ def tile_wrap_occupied_green_s11_kernel(tc, hop_bytes, hop_scale, left, right, h
         scale_bc = keep.tile([P, SITES], F32)
         w_bc = keep.tile([P, SITES], F32)
         winv_bc = keep.tile([P, SITES], F32)
-        hinv_sc = keep.tile([P, PASSES, SITES], U8, align_bytes=64)
         left_codes = keep.tile([P, PASSES, ORB], U32, align_bytes=64)
         left_sc = keep.tile([P, PASSES, ORB], U8, align_bytes=64)
         c_codes = keep.tile([P, SITES], U32, align_bytes=64)
         c_sc = keep.tile([P, SITES], U8, align_bytes=64)
 
-        hop_raw, left_rows, right_rows, hinv_codes = {}, {}, {}, {}
+        hop_raw, left_rows, right_rows, hinv_codes, hinv_sc, planes = {}, {}, {}, {}, {}, {}
 
         def load_hop(i0, i1):
             rows = keep.tile([P, i1 - i0, SITES], U8, name=f"hop_raw{i0}")
@@ -68,16 +67,24 @@ def tile_wrap_occupied_green_s11_kernel(tc, hop_bytes, hop_scale, left, right, h
             nc.sync.dma_start(out=rows[:], in_=right.rearrange("(m t) k -> t m k", t=PACK)[t])
             right_rows[t] = rows
 
-        def load_hinv(q):
-            words = keep.tile([P, PASSES, 2 * BANK], U8, name=f"hinv_codes{q}", align_bytes=64)
-            nc.sync.dma_start(out=words[:], in_=hinv_words[:, :, 2 * BANK * q : 2 * BANK * (q + 1)].rearrange("g p n -> p g n"))
-            hinv_codes[q] = words
+        def load_hinv(n0, n1):
+            words = keep.tile([P, PASSES, 2 * P * (n1 - n0)], U8, name=f"hinv_codes{n0}", align_bytes=64)
+            nc.sync.dma_start(out=words[:], in_=hinv_words[:, :, 2 * P * n0 : 2 * P * n1].rearrange("g p n -> p g n"))
+            for n in range(n0, n1):
+                hinv_codes[n] = words[:, :, 2 * P * (n - n0) : 2 * P * (n - n0 + 1)]
 
-        def load_hinv_scales():
+        def clear_scales(n0, n1):
+            plane = keep.tile([P, PASSES, P * (n1 - n0)], U8, name=f"hinv_sc{n0}", align_bytes=64)
+            nc.gpsimd.memset(plane[:].rearrange("p g n -> p (g n)").bitcast(U32), 0)
+            planes[n0] = plane
+            for n in range(n0, n1):
+                hinv_sc[n] = plane[:, :, P * (n - n0) : P * (n - n0 + 1)]
+
+        def load_scales(n0, n1):
             for q in range(4):
                 nc.sync.dma_start(
-                    out=hinv_sc[32 * q : 32 * q + 4, :, :].bitcast(I32),
-                    in_=hinv_scales[:, 4 * q : 4 * q + 4, :].rearrange("g q n -> q g n").bitcast(I32),
+                    out=planes[n0][32 * q : 32 * q + 4, :, :].bitcast(I32),
+                    in_=hinv_scales[:, 4 * q : 4 * q + 4, P * n0 : P * n1].rearrange("g q n -> q g n").bitcast(I32),
                 )
 
         def wide_bank():
@@ -85,6 +92,9 @@ def tile_wrap_occupied_green_s11_kernel(tc, hop_bytes, hop_scale, left, right, h
 
         def sum_bank():
             return psum.tile([P, BANK], F32, name="sums", bufs=2)
+
+        def turn_bank():
+            return psum.tile([P, BANK], F32, name="turned_ps", bufs=3)
 
         def warm_up(n):
             bank = wide_bank()
@@ -171,17 +181,18 @@ def tile_wrap_occupied_green_s11_kernel(tc, hop_bytes, hop_scale, left, right, h
 
         c_acc, c_grouped, a_acc, a_grouped, a_codes, a_sc = {}, {}, {}, {}, {}, {}
 
-        def mult_c(n, acc):
-            c_acc[n] = acc
-            q, m = divmod(n, BANK // P)
-            for t in range(PACK):
+        def mult_c(n, new_bank, slots=range(PACK)):
+            if slots[0] == 0:
+                c_acc[n] = new_bank()
+            acc = c_acc[n]
+            for t in slots:
                 for g in range(PASSES):
                     nc.tensor.matmul_mx(
                         out=acc[:, P * t : P * (t + 1)],
                         lhsT=right_codes[t][:, P * g : P * (g + 1)].bitcast(E4M3X4),
                         lhsT_scale=right_sc[t][:, P * g : P * (g + 1)],
-                        rhs=hinv_codes[q][:, g, 2 * P * m : 2 * P * (m + 1)].bitcast(E2M1X4),
-                        rhs_scale=hinv_sc[:, g, P * n : P * (n + 1)],
+                        rhs=hinv_codes[n][:, g, :].bitcast(E2M1X4),
+                        rhs_scale=hinv_sc[n][:, g, :],
                         start=(g == 0),
                         stop=(g == PASSES - 1),
                     )
@@ -237,12 +248,15 @@ def tile_wrap_occupied_green_s11_kernel(tc, hop_bytes, hop_scale, left, right, h
             a_codes[i], a_sc[i] = codes, sc
             nc.vector.quantize_mx(out=codes[:].bitcast(E4M3X4), scales=sc[:], in_=a_grouped[i][:].rearrange("p n t -> p (n t)"))
 
-        def finish(i, copies, by_bank):
-            result = results.tile([P, SITES], F32, name="result")
-            rows = slice(P * i, P * (i + 1))
+        out_banks, result = {}, {}
+
+        def mult_out(i):
+            rows = results.tile([P, SITES], F32, name="result")
+            result[i] = rows
             for q in range(CHUNKS):
                 cols = slice(BANK * q, BANK * (q + 1))
                 bank = wide_bank()
+                out_banks[i, q] = bank
                 nc.tensor.matmul_mx(
                     out=bank[:],
                     lhsT=a_codes[i][:].bitcast(E4M3X4),
@@ -252,11 +266,16 @@ def tile_wrap_occupied_green_s11_kernel(tc, hop_bytes, hop_scale, left, right, h
                     start=True,
                     stop=True,
                 )
-                copies[q](out=result[:, cols], in_=bank[:])
-                if by_bank:
-                    nc.sync.dma_start(out=out[rows, cols], in_=result[:, cols])
-            if not by_bank:
-                nc.sync.dma_start(out=out[rows, :], in_=result[:])
+
+        def empty_out(i, q, copy, store):
+            cols = slice(BANK * q, BANK * (q + 1))
+            copy(out=result[i][:, cols], in_=out_banks[i, q][:])
+            if store:
+                nc.sync.dma_start(out=out[P * i : P * (i + 1), cols], in_=result[i][:, cols])
+
+        def store_rows(i, q0=0, q1=CHUNKS):
+            cols = slice(BANK * q0, BANK * q1)
+            nc.sync.dma_start(out=out[P * i : P * (i + 1), cols], in_=result[i][:, cols])
 
         S = nc.scalar.copy
         V = nc.vector.tensor_copy
@@ -266,24 +285,28 @@ def tile_wrap_occupied_green_s11_kernel(tc, hop_bytes, hop_scale, left, right, h
             nc.vector.memset(field_row[:].bitcast(U32), 0)
             nc.gpsimd.memset(table[:], 0.0)
             make_identity(nc, ident[:])
-            nc.gpsimd.memset(hinv_sc[:].rearrange("p g n -> p (g n)").bitcast(U32), 0)
+            clear_scales(0, 4)
+            clear_scales(4, 12)
             nc.sync.dma_start(out=scale_cols[:], in_=hop_scale.rearrange("o (g n q) -> n (o g) q", n=P, q=PACK))
             load_hop(0, 1)
             nc.sync.dma_start(out=field_row[0:1, :], in_=field.rearrange("(o k) -> o k", o=1))
             load_right(0)
-            load_hop(1, 3)
-            for t in range(1, PACK):
-                load_right(t)
-            load_hinv_scales()
-            load_hinv(0)
+            load_right(1)
+            load_hop(1, 2)
+            load_right(2)
+            load_right(3)
+            load_scales(0, 4)
+            load_hinv(0, 4)
+            load_hop(2, 4)
             load_left(0)
-            load_hop(3, 5)
-            load_hinv(1)
+            load_scales(4, 12)
+            load_hinv(4, 8)
             load_left(1)
+            load_hop(4, 6)
             load_left(2)
-            load_hinv(2)
-            load_hop(5, 8)
-            load_hop(8, 12)
+            load_hinv(8, 12)
+            load_hop(6, 9)
+            load_hop(9, 12)
 
             nc.scalar.activation(out=table[:], in_=table[:], func=EXP)
             warm_up(4)
@@ -291,57 +314,78 @@ def tile_wrap_occupied_green_s11_kernel(tc, hop_bytes, hop_scale, left, right, h
                 spread_scale(g)
                 widen(0, g, g + 1)
             spread_field(0, sum_bank())
-            turn_right(0)
-            exp_field(0, winv_bc, -1.0)
-            exp_field(0, w_bc, 1.0)
             spread_field(1, sum_bank())
-            spread_field(2, wide_bank())
-            widen(1)
-            quantize_right(0)
+            turn_right(0)
             turn_right(1)
-            turn_hop(0)
+            quantize_right(0)
+            widen(1, 0, 2)
             quantize_right(1)
-            widen(2, 0, 2)
+            turn_hop(0)
             turn_right(2)
+            widen(1, 2, 3)
             turn_right(3)
             quantize_right(2)
-            widen(2, 2, 3)
-            quantize_right(3)
-            exp_field(2, winv_bc, -1.0)
-            exp_field(2, w_bc, 1.0)
-            exp_field(1, winv_bc, -1.0)
-            exp_field(1, w_bc, 1.0)
             quantize_hop(0)
+            quantize_right(3)
+            spread_field(2, wide_bank())
+            exp_field(0, winv_bc, -1.0)
+            exp_field(0, w_bc, 1.0)
+            exp_field(1, winv_bc, -1.0)
+            exp_field(2, winv_bc, -1.0)
+            widen(2)
             banks = (wide_bank, wide_bank, sum_bank, sum_bank, wide_bank)
             for n in range(TILES):
-                mult_c(n, banks[n % 5]())
-                if n in (2, 6):
-                    turn_hop(1 + n // 4)
+                if n == 11:
+                    mult_a(0)
+                mult_c(n, banks[n % 5] if n < 10 else wide_bank)
+                if n in (2, 8):
+                    turn_hop(1 if n == 2 else 2)
+                if n in (5, 7, 9):
+                    quantize_left((5, 7, 9).index(n))
+                if n == 11:
+                    empty_a(0)
                 empty_c(n)
+                if n == 11:
+                    quantize_a(0)
                 if n < 6:
                     interleave_left(n // 2, n % 2, S)
-                if n < 6:
+                if n < 3 + 1:
                     widen(3 + n // 3, n % 3, n % 3 + 1)
-                if n in (4, 6, 8):
-                    quantize_left((n - 4) // 2)
-                if n == 9:
+                if n == 10:
                     quantize_hop(1)
                 if n >= 2 and n % 2 == 0:
                     quantize_c(n // 2 - 1)
-            for i in range(TILES + 1):
+            turn_hop(3)
+            for q in (1, 2):
+                spread_field(q, wide_bank())
+                exp_field(q, w_bc, 1.0)
+            quantize_c(5)
+            quantize_hop(2)
+            for i in range(1, TILES + 1):
+                ahead = 3 if i < 8 else 2
                 if i < TILES:
                     mult_a(i)
-                if 0 < i < TILES - 4:
+                if i + 3 < TILES and 1 < 3:
+                    widen(i + 3, 1, 3)
+                if i + 4 < TILES and 1 == 3:
                     widen(i + 4)
+                if i > 8 and i + 1 < TILES:
+                    quantize_hop(i + 1)
                 if i < TILES:
                     empty_a(i)
-                if i + 2 < TILES:
+                if i < 8 and i + 2 < TILES:
                     quantize_hop(i + 2)
-                if i == 0:
-                    quantize_c(5)
-                if i > 0:
-                    finish(i - 1, (S, V, S) if i > 9 else (S, S, S), i > 8)
-                if i + 3 < TILES:
-                    turn_hop(i + 3)
+                mult_out(i - 1)
+                shared = i > 8
+                for q in (0, 2) if shared else range(CHUNKS):
+                    empty_out(i - 1, q, S, i > 7)
+                if i <= 7:
+                    store_rows(i - 1)
+                if i + 4 < TILES and 1 < 3:
+                    widen(i + 4, 0, 1)
+                if i != 8 and i + ahead < TILES:
+                    turn_hop(i + ahead)
                 if i < TILES:
                     quantize_a(i)
+                if shared:
+                    empty_out(i - 1, 1, V, True)

@@ -15,6 +15,7 @@ E4M3X4 = mybir.dt.float8_e4m3fn_x4
 E2M1X4 = mybir.dt.float4_e2m1fn_x4
 MULT = mybir.AluOpType.mult
 EXP = mybir.ActivationFunctionType.Exp
+COPY = mybir.ActivationFunctionType.Copy
 
 P = 128
 PACK = 4
@@ -46,6 +47,10 @@ def tile_wrap_occupied_green_s11_kernel(tc, hop_bytes, hop_scale, left, right, h
         winv_bc = keep.tile([P, SITES], F32)
         left_codes = keep.tile([P, PASSES, ORB], U32, align_bytes=64)
         left_sc = keep.tile([P, PASSES, ORB], U8, align_bytes=64)
+        right_codes = keep.tile([P, PASSES, ORB], U32, align_bytes=64)
+        right_sc = keep.tile([P, PASSES, ORB], U8, align_bytes=64)
+        w_cols = keep.tile([P, TILES, 2], F32)
+        winv_cols = keep.tile([P, TILES, 2], F32)
         c_codes = keep.tile([P, SITES], U32, align_bytes=64)
         c_sc = keep.tile([P, SITES], U8, align_bytes=64)
 
@@ -119,7 +124,7 @@ def tile_wrap_occupied_green_s11_kernel(tc, hop_bytes, hop_scale, left, right, h
         def exp_field(q, row_bc, sign):
             nc.scalar.activation(out=row_bc[:, BANK * q : BANK * (q + 1)], in_=field_bank[q][:], func=EXP, scale=sign)
 
-        hop_bf, turned, hop_codes, hop_sc, right_codes, right_sc = {}, {}, {}, {}, {}, {}
+        hop_bf, turned, hop_codes, hop_sc = {}, {}, {}, {}
 
         def widen(i, g0=0, g1=PASSES):
             if g0 == 0:
@@ -127,6 +132,10 @@ def tile_wrap_occupied_green_s11_kernel(tc, hop_bytes, hop_scale, left, right, h
                 hop_bf[i] = wide
             k = slice(K_PASS * g0, K_PASS * g1)
             nc.vector.tensor_tensor(out=hop_bf[i][:, k], in0=hop_raw[i][:, k].bitcast(FP8), in1=scale_bc[:, k], op=MULT)
+
+        def widen_passes(a, b):
+            for i in range(a // PASSES, (b - 1) // PASSES + 1):
+                widen(i, max(a - PASSES * i, 0), min(b - PASSES * i, PASSES))
 
         def turn(rows, key):
             grouped = work.tile([P, SITES], BF16, name="turned_sb", align_bytes=64, bufs=5)
@@ -159,10 +168,11 @@ def tile_wrap_occupied_green_s11_kernel(tc, hop_bytes, hop_scale, left, right, h
             quantize_turned(("hop", i), codes, sc)
 
         def quantize_right(t):
-            codes = keep.tile([P, PASSES * P], U32, name=f"right_codes{t}", align_bytes=64)
-            sc = keep.tile([P, PASSES * P], U8, name=f"right_sc{t}", align_bytes=64)
-            right_codes[t], right_sc[t] = codes, sc
-            quantize_turned(("right", t), codes, sc)
+            m = slice(P * t, P * (t + 1))
+            for g in range(PASSES):
+                nc.vector.quantize_mx(
+                    out=right_codes[:, g, m].bitcast(E4M3X4), scales=right_sc[:, g, m], in_=turned["right", t][:, K_PASS * g : K_PASS * (g + 1)]
+                )
 
         left_grouped = {}
 
@@ -189,13 +199,79 @@ def tile_wrap_occupied_green_s11_kernel(tc, hop_bytes, hop_scale, left, right, h
                 for g in range(PASSES):
                     nc.tensor.matmul_mx(
                         out=acc[:, P * t : P * (t + 1)],
-                        lhsT=right_codes[t][:, P * g : P * (g + 1)].bitcast(E4M3X4),
-                        lhsT_scale=right_sc[t][:, P * g : P * (g + 1)],
+                        lhsT=right_codes[:, g, P * t : P * (t + 1)].bitcast(E4M3X4),
+                        lhsT_scale=right_sc[:, g, P * t : P * (t + 1)],
                         rhs=hinv_codes[n][:, g, :].bitcast(E2M1X4),
                         rhs_scale=hinv_sc[n][:, g, :],
                         start=(g == 0),
                         stop=(g == PASSES - 1),
                     )
+
+        def field_columns(tiles, cols, sign):
+            bank = turn_bank()
+            for i in tiles:
+                nc.tensor.matmul(bank[:, 2 * i : 2 * i + 2], field_row[:, P * i : P * (i + 1)], ones[:, 0:2], start=True, stop=True)
+            lo, hi = tiles[0], tiles[-1] + 1
+            nc.scalar.activation(out=cols[:, lo:hi, :].rearrange("p i e -> p (i e)"), in_=bank[:, 2 * lo : 2 * hi], func=EXP, scale=sign)
+
+        rows_acc, rows_bf = {}, {}
+
+        def mult_rows(key, new_bank, lhs, lhs_sc, lhs_type, codes, sc):
+            acc = new_bank()
+            rows_acc[key] = acc
+            for g in range(PASSES):
+                nc.tensor.matmul_mx(
+                    out=acc[:],
+                    lhsT=lhs(g).bitcast(lhs_type),
+                    lhsT_scale=lhs_sc(g),
+                    rhs=codes[:, g, :].bitcast(E4M3X4),
+                    rhs_scale=sc[:, g, :],
+                    start=(g == 0),
+                    stop=(g == PASSES - 1),
+                )
+
+        def scale_rows(key, column):
+            rows = work.tile([P, ORB], BF16, name="rows_bf", bufs=3)
+            rows_bf[key] = rows
+            nc.scalar.activation(
+                out=rows[:].rearrange("p (u m e) -> p u m e", u=2, e=2),
+                in_=rows_acc[key][:].rearrange("p (u e m) -> p u m e", u=2, e=2),
+                func=COPY,
+                scale=column,
+            )
+
+        def turn_rows(keys, grouped):
+            bank = psum.tile([P, 2, 2, P], F32, name="turned_ps", bufs=3)
+            for l, key in enumerate(keys):
+                words = rows_bf[key][:].bitcast(F32)
+                for u in range(2):
+                    nc.tensor.transpose(bank[:, l, u, :], words[:, P * u : P * (u + 1)], ident[:])
+            nc.scalar.copy(
+                out=grouped.bitcast(F32).rearrange("p (l r u) -> p l r u", r=P, u=2),
+                in_=bank[:, 0 : len(keys), :, :].rearrange("p l u r -> p l r u"),
+            )
+
+        def mult_c_rows(n, new_bank):
+            mult_rows(("c", n), new_bank, lambda g: hinv_codes[n][:, g, :], lambda g: hinv_sc[n][:, g, :], E2M1X4, right_codes, right_sc)
+
+        def scale_c_rows(n):
+            scale_rows(("c", n), winv_cols[:, n, 0:1])
+
+        def turn_c_rows(pair):
+            grouped = work.tile([P, 2, P, PACK], BF16, name="c_grouped", align_bytes=64)
+            c_grouped[pair] = grouped
+            turn_rows([("c", 2 * pair), ("c", 2 * pair + 1)], grouped[:].rearrange("p s n t -> p (s n t)"))
+
+        def mult_a_rows(i):
+            mult_rows(("a", i), sum_bank, lambda g: hop_codes[i][:, P * g : P * (g + 1)], lambda g: hop_sc[i][:, P * g : P * (g + 1)], E4M3X4, left_codes, left_sc)
+
+        def scale_a_rows(i):
+            scale_rows(("a", i), w_cols[:, i, 0:1])
+
+        def turn_a_rows(i):
+            grouped = work.tile([P, P, PACK], BF16, name="a_grouped", align_bytes=64, bufs=3)
+            a_grouped[i] = grouped
+            turn_rows([("a", i)], grouped[:].rearrange("p n t -> p (n t)"))
 
         def empty_c(n):
             if n % 2 == 0:
@@ -250,12 +326,12 @@ def tile_wrap_occupied_green_s11_kernel(tc, hop_bytes, hop_scale, left, right, h
 
         out_banks, result = {}, {}
 
-        def mult_out(i):
+        def mult_out(i, new_banks):
             rows = results.tile([P, SITES], F32, name="result")
             result[i] = rows
             for q in range(CHUNKS):
                 cols = slice(BANK * q, BANK * (q + 1))
-                bank = wide_bank()
+                bank = new_banks[q]()
                 out_banks[i, q] = bank
                 nc.tensor.matmul_mx(
                     out=bank[:],
@@ -318,73 +394,71 @@ def tile_wrap_occupied_green_s11_kernel(tc, hop_bytes, hop_scale, left, right, h
             turn_right(0)
             turn_right(1)
             quantize_right(0)
-            widen(1, 0, 2)
+            widen(1)
             quantize_right(1)
             turn_hop(0)
             turn_right(2)
-            widen(1, 2, 3)
             turn_right(3)
             quantize_right(2)
             quantize_hop(0)
             quantize_right(3)
-            spread_field(2, wide_bank())
             exp_field(0, winv_bc, -1.0)
             exp_field(0, w_bc, 1.0)
             exp_field(1, winv_bc, -1.0)
-            exp_field(2, winv_bc, -1.0)
+            field_columns(range(8, 12), winv_cols, -1.0)
             widen(2)
-            banks = (wide_bank, wide_bank, sum_bank, sum_bank, wide_bank)
-            for n in range(TILES):
-                if n == 11:
-                    mult_a(0)
-                mult_c(n, banks[n % 5] if n < 10 else wide_bank)
-                if n in (2, 8):
+            banks = (wide_bank, wide_bank, wide_bank, sum_bank, sum_bank)
+            for n in range(8):
+                mult_c(n, banks[n % 5])
+                if n in (2, 6):
                     turn_hop(1 if n == 2 else 2)
-                if n in (5, 7, 9):
-                    quantize_left((5, 7, 9).index(n))
-                if n == 11:
-                    empty_a(0)
+                if n in (5, 7):
+                    quantize_left((5, 7).index(n))
                 empty_c(n)
-                if n == 11:
-                    quantize_a(0)
                 if n < 6:
                     interleave_left(n // 2, n % 2, S)
-                if n < 3 + 1:
-                    widen(3 + n // 3, n % 3, n % 3 + 1)
-                if n == 10:
+                if n in (1, 4):
+                    widen(3 if n == 1 else 4)
+                if n == 6:
                     quantize_hop(1)
                 if n >= 2 and n % 2 == 0:
                     quantize_c(n // 2 - 1)
+            quantize_c(3)
+            for n in range(8, 12):
+                mult_c_rows(n, banks[n % 5])
+                scale_c_rows(n)
+            quantize_left(2)
+            quantize_hop(2)
+            widen(5)
             turn_hop(3)
+            turn_c_rows(4)
+            mult_a(0)
+            turn_c_rows(5)
+            turn_hop(4)
+            empty_a(0)
+            quantize_c(4)
+            quantize_a(0)
             for q in (1, 2):
                 spread_field(q, wide_bank())
                 exp_field(q, w_bc, 1.0)
             quantize_c(5)
-            quantize_hop(2)
             for i in range(1, TILES + 1):
-                ahead = 3 if i < 8 else 2
                 if i < TILES:
                     mult_a(i)
-                if i + 3 < TILES and 1 < 3:
-                    widen(i + 3, 1, 3)
-                if i + 4 < TILES and 1 == 3:
-                    widen(i + 4)
-                if i > 8 and i + 1 < TILES:
-                    quantize_hop(i + 1)
+                if i <= 8:
+                    widen_passes(18 + 18 * (i - 1) // 8, 18 + 18 * i // 8)
                 if i < TILES:
                     empty_a(i)
-                if i < 8 and i + 2 < TILES:
+                if i + 2 < TILES:
                     quantize_hop(i + 2)
-                mult_out(i - 1)
-                shared = i > 8
+                mult_out(i - 1, (wide_bank, turn_bank if i > 9 else wide_bank, wide_bank))
+                shared = i > 9
                 for q in (0, 2) if shared else range(CHUNKS):
                     empty_out(i - 1, q, S, i > 7)
                 if i <= 7:
                     store_rows(i - 1)
-                if i + 4 < TILES and 1 < 3:
-                    widen(i + 4, 0, 1)
-                if i != 8 and i + ahead < TILES:
-                    turn_hop(i + ahead)
+                if 1 < i and i + 3 < TILES:
+                    turn_hop(i + 3)
                 if i < TILES:
                     quantize_a(i)
                 if shared:

@@ -25,6 +25,12 @@ TILES = SITES // P
 BANK = 512
 CHUNKS = SITES // BANK
 
+C_ROWS_FROM = 8
+STORE_BY_BANK_FROM = 7
+SHARE_FROM = 9
+
+PARK_ROWS, PARK_COLS = 64, 24
+
 FLOPS = 3 * 2 * SITES * SITES * ORB
 
 
@@ -34,27 +40,39 @@ def tile_wrap_occupied_green_s11_kernel(tc, hop_bytes, hop_scale, left, right, h
     with ExitStack() as ctx:
         keep = ctx.enter_context(tc.tile_pool(name="keep", bufs=1))
         work = ctx.enter_context(tc.tile_pool(name="work", bufs=2))
-        results = ctx.enter_context(tc.tile_pool(name="results", bufs=5))
         psum = ctx.enter_context(tc.psum_pool(name="psum", bufs=1))
 
         ident = keep.tile([P, P], F32)
         table = keep.tile([P, 1], F32)
         ones = keep.tile([P, BANK], BF16)
         field_row = keep.tile([P, SITES], BF16)
+        field_cols = keep.tile([PARK_ROWS, PARK_COLS], BF16)
+        w_cols = keep.tile([PARK_ROWS, PARK_COLS], F32)
         scale_cols = keep.tile([P, PASSES, PACK], F32)
         scale_bc = keep.tile([P, SITES], F32)
         w_bc = keep.tile([P, SITES], F32)
-        winv_bc = keep.tile([P, SITES], F32)
+        winv_bc = keep.tile([P, P * C_ROWS_FROM], F32)
+        winv_cols = keep.tile([P, TILES - C_ROWS_FROM], F32)
         left_codes = keep.tile([P, PASSES, ORB], U32, align_bytes=64)
         left_sc = keep.tile([P, PASSES, ORB], U8, align_bytes=64)
         right_codes = keep.tile([P, PASSES, ORB], U32, align_bytes=64)
         right_sc = keep.tile([P, PASSES, ORB], U8, align_bytes=64)
-        w_cols = keep.tile([P, TILES, 2], F32)
-        winv_cols = keep.tile([P, TILES, 2], F32)
         c_codes = keep.tile([P, SITES], U32, align_bytes=64)
         c_sc = keep.tile([P, SITES], U8, align_bytes=64)
 
-        hop_raw, left_rows, right_rows, hinv_codes, hinv_sc, planes = {}, {}, {}, {}, {}, {}
+        on_scalar = nc.scalar.copy
+        on_vector = nc.vector.tensor_copy
+
+        def wide_bank():
+            return psum.tile([P, BANK], F32, name="wide", bufs=3)
+
+        def sum_bank():
+            return psum.tile([P, BANK], F32, name="sums", bufs=2)
+
+        def turn_bank():
+            return psum.tile([P, BANK], F32, name="turns", bufs=3)
+
+        hop_raw, left_rows, right_rows, hinv_codes, hinv_sc, scale_tiles = {}, {}, {}, {}, {}, {}
 
         def load_hop(i0, i1):
             rows = keep.tile([P, i1 - i0, SITES], U8, name=f"hop_raw{i0}")
@@ -79,32 +97,18 @@ def tile_wrap_occupied_green_s11_kernel(tc, hop_bytes, hop_scale, left, right, h
                 hinv_codes[n] = words[:, :, 2 * P * (n - n0) : 2 * P * (n - n0 + 1)]
 
         def clear_scales(n0, n1):
-            plane = keep.tile([P, PASSES, P * (n1 - n0)], U8, name=f"hinv_sc{n0}", align_bytes=64)
-            nc.gpsimd.memset(plane[:].rearrange("p g n -> p (g n)").bitcast(U32), 0)
-            planes[n0] = plane
+            sc = keep.tile([P, PASSES, P * (n1 - n0)], U8, name=f"hinv_sc{n0}", align_bytes=64)
+            nc.gpsimd.memset(sc[:].rearrange("p g n -> p (g n)").bitcast(U32), 0)
+            scale_tiles[n0] = sc
             for n in range(n0, n1):
-                hinv_sc[n] = plane[:, :, P * (n - n0) : P * (n - n0 + 1)]
+                hinv_sc[n] = sc[:, :, P * (n - n0) : P * (n - n0 + 1)]
 
         def load_scales(n0, n1):
             for q in range(4):
                 nc.sync.dma_start(
-                    out=planes[n0][32 * q : 32 * q + 4, :, :].bitcast(I32),
+                    out=scale_tiles[n0][32 * q : 32 * q + 4, :, :].bitcast(I32),
                     in_=hinv_scales[:, 4 * q : 4 * q + 4, P * n0 : P * n1].rearrange("g q n -> q g n").bitcast(I32),
                 )
-
-        def wide_bank():
-            return psum.tile([P, BANK], F32, name="wide", bufs=3)
-
-        def sum_bank():
-            return psum.tile([P, BANK], F32, name="sums", bufs=2)
-
-        def turn_bank():
-            return psum.tile([P, BANK], F32, name="turned_ps", bufs=3)
-
-        def warm_up(n):
-            bank = wide_bank()
-            for x in range(n):
-                nc.tensor.matmul(bank[:], ones[:, 0:P], ones[:], start=True, stop=True)
 
         def spread_scale(g):
             bank = wide_bank()
@@ -115,21 +119,27 @@ def tile_wrap_occupied_green_s11_kernel(tc, hop_bytes, hop_scale, left, right, h
                 in_=bank[:].rearrange("p (q n) -> p n q", q=PACK),
             )
 
-        field_bank = {}
-
-        def spread_field(q, bank):
-            field_bank[q] = bank
+        def spread_field(q):
+            bank = sum_bank()
             nc.tensor.matmul(bank[:], ones[:, 0:P], field_row[:, BANK * q : BANK * (q + 1)], start=True, stop=True)
+            return bank
 
-        def exp_field(q, row_bc, sign):
-            nc.scalar.activation(out=row_bc[:, BANK * q : BANK * (q + 1)], in_=field_bank[q][:], func=EXP, scale=sign)
+        def exp_winv(q, bank):
+            nc.scalar.activation(out=winv_bc[:, BANK * q : BANK * (q + 1)], in_=bank[:], func=EXP, scale=-1.0)
+
+        def make_winv_cols():
+            bank = turn_bank()
+            for n in range(C_ROWS_FROM, TILES):
+                j = n - C_ROWS_FROM
+                nc.tensor.matmul(bank[:, j : j + 1], field_row[:, P * n : P * (n + 1)], ones[:, 0:1], start=True, stop=True)
+            nc.scalar.activation(out=winv_cols[:], in_=bank[:, 0 : TILES - C_ROWS_FROM], func=EXP, scale=-1.0)
 
         hop_bf, turned, hop_codes, hop_sc = {}, {}, {}, {}
 
         def widen(i, g0=0, g1=PASSES):
             if g0 == 0:
-                wide = work.tile([P, SITES], BF16, name="hop_bf", bufs=5)
-                hop_bf[i] = wide
+                values = work.tile([P, SITES], BF16, name="hop_bf", bufs=5)
+                hop_bf[i] = values
             k = slice(K_PASS * g0, K_PASS * g1)
             nc.vector.tensor_tensor(out=hop_bf[i][:, k], in0=hop_raw[i][:, k].bitcast(FP8), in1=scale_bc[:, k], op=MULT)
 
@@ -137,23 +147,23 @@ def tile_wrap_occupied_green_s11_kernel(tc, hop_bytes, hop_scale, left, right, h
             for i in range(a // PASSES, (b - 1) // PASSES + 1):
                 widen(i, max(a - PASSES * i, 0), min(b - PASSES * i, PASSES))
 
+        def copy_turned(bank, groups, target):
+            nc.scalar.copy(
+                out=target.bitcast(F32).rearrange("p (l r u) -> p l r u", r=P, u=2),
+                in_=bank[:, 0 : 2 * P * groups].rearrange("p (l u r) -> p l r u", u=2, r=P),
+            )
+
         def turn(rows, key):
-            grouped = work.tile([P, SITES], BF16, name="turned_sb", align_bytes=64, bufs=5)
+            grouped = work.tile([P, SITES], BF16, name="turned", align_bytes=64, bufs=5)
             turned[key] = grouped
             words = rows[:].bitcast(F32)
             for g0, g1 in ((0, 2), (2, 3)):
-                bank = psum.tile([P, 2, 2, P], F32, name="turned_ps", bufs=3)
+                bank = turn_bank()
                 for g in range(g0, g1):
                     for u in range(2):
-                        nc.tensor.transpose(bank[:, g - g0, u, :], words[:, 2 * P * g + u : 2 * P * (g + 1) : 2], ident[:])
-                nc.scalar.copy(
-                    out=grouped[:, K_PASS * g0 : K_PASS * g1].bitcast(F32).rearrange("p (l r u) -> p l r u", r=P, u=2),
-                    in_=bank[:, 0 : g1 - g0, :, :].rearrange("p l u r -> p l r u"),
-                )
-
-        def quantize_turned(key, codes, sc):
-            for a, b in ((0, 2 * P), (2 * P, 3 * P)):
-                nc.vector.quantize_mx(out=codes[:, a:b].bitcast(E4M3X4), scales=sc[:, a:b], in_=turned[key][:, PACK * a : PACK * b])
+                        col = P * (2 * (g - g0) + u)
+                        nc.tensor.transpose(bank[:, col : col + P], words[:, 2 * P * g + u : 2 * P * (g + 1) : 2], ident[:])
+                copy_turned(bank, g1 - g0, grouped[:, K_PASS * g0 : K_PASS * g1])
 
         def turn_hop(i):
             turn(hop_bf[i], ("hop", i))
@@ -165,7 +175,8 @@ def tile_wrap_occupied_green_s11_kernel(tc, hop_bytes, hop_scale, left, right, h
             codes = work.tile([P, PASSES * P], U32, name="hop_codes", align_bytes=64, bufs=4)
             sc = work.tile([P, PASSES * P], U8, name="hop_sc", align_bytes=64, bufs=4)
             hop_codes[i], hop_sc[i] = codes, sc
-            quantize_turned(("hop", i), codes, sc)
+            for a, b in ((0, 2 * P), (2 * P, 3 * P)):
+                nc.vector.quantize_mx(out=codes[:, a:b].bitcast(E4M3X4), scales=sc[:, a:b], in_=turned["hop", i][:, PACK * a : PACK * b])
 
         def quantize_right(t):
             m = slice(P * t, P * (t + 1))
@@ -176,113 +187,87 @@ def tile_wrap_occupied_green_s11_kernel(tc, hop_bytes, hop_scale, left, right, h
 
         left_grouped = {}
 
-        def interleave_left(g, h, copy):
-            if h == 0:
-                grouped = work.tile([P, ORB * PACK], BF16, name="left_grouped", align_bytes=64)
-                left_grouped[g] = grouped
-            m = slice(P // 2 * h, P // 2 * (h + 1))
-            copy(
-                out=left_grouped[g][:].rearrange("p (t m j) -> p m t j", t=PACK, j=PACK)[:, m, :, :],
-                in_=left_rows[g][:].rearrange("p j (m t) -> p m t j", t=PACK)[:, m, :, :],
+        def interleave_left(g):
+            grouped = work.tile([P, ORB * PACK], BF16, name="left_grouped", align_bytes=64)
+            left_grouped[g] = grouped
+            nc.scalar.copy(
+                out=grouped[:].rearrange("p (t m j) -> p m t j", t=PACK, j=PACK),
+                in_=left_rows[g][:].rearrange("p j (m t) -> p m t j", t=PACK),
             )
 
         def quantize_left(g):
             nc.vector.quantize_mx(out=left_codes[:, g, :].bitcast(E4M3X4), scales=left_sc[:, g, :], in_=left_grouped[g][:])
 
-        c_acc, c_grouped, a_acc, a_grouped, a_codes, a_sc = {}, {}, {}, {}, {}, {}
+        c_acc, c_rows, c_grouped, a_acc, a_grouped, a_codes, a_sc = {}, {}, {}, {}, {}, {}, {}
 
-        def mult_c(n, new_bank, slots=range(PACK)):
-            if slots[0] == 0:
-                c_acc[n] = new_bank()
-            acc = c_acc[n]
-            for t in slots:
+        def slots_product(acc, codes, sc, moving, moving_sc):
+            for t in range(PACK):
+                m = slice(P * t, P * (t + 1))
                 for g in range(PASSES):
                     nc.tensor.matmul_mx(
-                        out=acc[:, P * t : P * (t + 1)],
-                        lhsT=right_codes[:, g, P * t : P * (t + 1)].bitcast(E4M3X4),
-                        lhsT_scale=right_sc[:, g, P * t : P * (t + 1)],
-                        rhs=hinv_codes[n][:, g, :].bitcast(E2M1X4),
-                        rhs_scale=hinv_sc[n][:, g, :],
+                        out=acc[:, m],
+                        lhsT=codes[:, g, m].bitcast(E4M3X4),
+                        lhsT_scale=sc[:, g, m],
+                        rhs=moving(g),
+                        rhs_scale=moving_sc(g),
                         start=(g == 0),
                         stop=(g == PASSES - 1),
                     )
 
-        def field_columns(tiles, cols, sign):
-            bank = turn_bank()
-            for i in tiles:
-                nc.tensor.matmul(bank[:, 2 * i : 2 * i + 2], field_row[:, P * i : P * (i + 1)], ones[:, 0:2], start=True, stop=True)
-            lo, hi = tiles[0], tiles[-1] + 1
-            nc.scalar.activation(out=cols[:, lo:hi, :].rearrange("p i e -> p (i e)"), in_=bank[:, 2 * lo : 2 * hi], func=EXP, scale=sign)
+        def empty_slots(acc, factor, target):
+            nc.vector.tensor_tensor(
+                out=target,
+                in0=acc[:].rearrange("p (t n) -> p n t", t=PACK),
+                in1=factor.unsqueeze(2).to_broadcast([P, P, PACK]),
+                op=MULT,
+            )
 
-        rows_acc, rows_bf = {}, {}
+        def new_c_pair(pair):
+            grouped = work.tile([P, 2, P, PACK], BF16, name="c_grouped", align_bytes=64)
+            c_grouped[pair] = grouped
 
-        def mult_rows(key, new_bank, lhs, lhs_sc, lhs_type, codes, sc):
-            acc = new_bank()
-            rows_acc[key] = acc
+        def mult_c(n, acc):
+            c_acc[n] = acc
+            slots_product(acc, right_codes, right_sc, lambda g: hinv_codes[n][:, g, :].bitcast(E2M1X4), lambda g: hinv_sc[n][:, g, :])
+
+        def empty_c(n):
+            if n % 2 == 0:
+                new_c_pair(n // 2)
+            empty_slots(c_acc[n], winv_bc[:, P * n : P * (n + 1)], c_grouped[n // 2][:, n % 2, :, :])
+
+        def mult_c_rows(n, acc):
+            c_acc[n] = acc
             for g in range(PASSES):
                 nc.tensor.matmul_mx(
                     out=acc[:],
-                    lhsT=lhs(g).bitcast(lhs_type),
-                    lhsT_scale=lhs_sc(g),
-                    rhs=codes[:, g, :].bitcast(E4M3X4),
-                    rhs_scale=sc[:, g, :],
+                    lhsT=hinv_codes[n][:, g, :].bitcast(E2M1X4),
+                    lhsT_scale=hinv_sc[n][:, g, :],
+                    rhs=right_codes[:, g, :].bitcast(E4M3X4),
+                    rhs_scale=right_sc[:, g, :],
                     start=(g == 0),
                     stop=(g == PASSES - 1),
                 )
 
-        def scale_rows(key, column):
-            rows = work.tile([P, ORB], BF16, name="rows_bf", bufs=3)
-            rows_bf[key] = rows
+        def scale_c_rows(n):
+            rows = work.tile([P, ORB], BF16, name="c_rows", bufs=4)
+            c_rows[n] = rows
+            j = n - C_ROWS_FROM
             nc.scalar.activation(
                 out=rows[:].rearrange("p (u m e) -> p u m e", u=2, e=2),
-                in_=rows_acc[key][:].rearrange("p (u e m) -> p u m e", u=2, e=2),
+                in_=c_acc[n][:].rearrange("p (u e m) -> p u m e", u=2, e=2),
                 func=COPY,
-                scale=column,
+                scale=winv_cols[:, j : j + 1],
             )
-
-        def turn_rows(keys, grouped):
-            bank = psum.tile([P, 2, 2, P], F32, name="turned_ps", bufs=3)
-            for l, key in enumerate(keys):
-                words = rows_bf[key][:].bitcast(F32)
-                for u in range(2):
-                    nc.tensor.transpose(bank[:, l, u, :], words[:, P * u : P * (u + 1)], ident[:])
-            nc.scalar.copy(
-                out=grouped.bitcast(F32).rearrange("p (l r u) -> p l r u", r=P, u=2),
-                in_=bank[:, 0 : len(keys), :, :].rearrange("p l u r -> p l r u"),
-            )
-
-        def mult_c_rows(n, new_bank):
-            mult_rows(("c", n), new_bank, lambda g: hinv_codes[n][:, g, :], lambda g: hinv_sc[n][:, g, :], E2M1X4, right_codes, right_sc)
-
-        def scale_c_rows(n):
-            scale_rows(("c", n), winv_cols[:, n, 0:1])
 
         def turn_c_rows(pair):
-            grouped = work.tile([P, 2, P, PACK], BF16, name="c_grouped", align_bytes=64)
-            c_grouped[pair] = grouped
-            turn_rows([("c", 2 * pair), ("c", 2 * pair + 1)], grouped[:].rearrange("p s n t -> p (s n t)"))
-
-        def mult_a_rows(i):
-            mult_rows(("a", i), sum_bank, lambda g: hop_codes[i][:, P * g : P * (g + 1)], lambda g: hop_sc[i][:, P * g : P * (g + 1)], E4M3X4, left_codes, left_sc)
-
-        def scale_a_rows(i):
-            scale_rows(("a", i), w_cols[:, i, 0:1])
-
-        def turn_a_rows(i):
-            grouped = work.tile([P, P, PACK], BF16, name="a_grouped", align_bytes=64, bufs=3)
-            a_grouped[i] = grouped
-            turn_rows([("a", i)], grouped[:].rearrange("p n t -> p (n t)"))
-
-        def empty_c(n):
-            if n % 2 == 0:
-                grouped = work.tile([P, 2, P, PACK], BF16, name="c_grouped", align_bytes=64)
-                c_grouped[n // 2] = grouped
-            nc.vector.tensor_tensor(
-                out=c_grouped[n // 2][:, n % 2, :, :],
-                in0=c_acc[n][:].rearrange("p (t n) -> p n t", t=PACK),
-                in1=winv_bc[:, P * n : P * (n + 1)].unsqueeze(2).to_broadcast([P, P, PACK]),
-                op=MULT,
-            )
+            new_c_pair(pair)
+            bank = turn_bank()
+            for s in range(2):
+                words = c_rows[2 * pair + s][:].bitcast(F32)
+                for u in range(2):
+                    col = P * (2 * s + u)
+                    nc.tensor.transpose(bank[:, col : col + P], words[:, P * u : P * (u + 1)], ident[:])
+            copy_turned(bank, 2, c_grouped[pair][:].rearrange("p s n t -> p (s n t)"))
 
         def quantize_c(pair):
             cols = slice(2 * P * pair, 2 * P * (pair + 1))
@@ -293,30 +278,15 @@ def tile_wrap_occupied_green_s11_kernel(tc, hop_bytes, hop_scale, left, right, h
             )
 
         def mult_a(i):
-            acc = sum_bank()
-            a_acc[i] = acc
-            for t in range(PACK):
-                for g in range(PASSES):
-                    cols = slice(g * P, (g + 1) * P)
-                    nc.tensor.matmul_mx(
-                        out=acc[:, P * t : P * (t + 1)],
-                        lhsT=left_codes[:, g, P * t : P * (t + 1)].bitcast(E4M3X4),
-                        lhsT_scale=left_sc[:, g, P * t : P * (t + 1)],
-                        rhs=hop_codes[i][:, cols].bitcast(E4M3X4),
-                        rhs_scale=hop_sc[i][:, cols],
-                        start=(g == 0),
-                        stop=(g == PASSES - 1),
-                    )
+            a_acc[i] = sum_bank()
+            slots_product(
+                a_acc[i], left_codes, left_sc, lambda g: hop_codes[i][:, P * g : P * (g + 1)].bitcast(E4M3X4), lambda g: hop_sc[i][:, P * g : P * (g + 1)]
+            )
 
         def empty_a(i):
             grouped = work.tile([P, P, PACK], BF16, name="a_grouped", align_bytes=64, bufs=3)
             a_grouped[i] = grouped
-            nc.vector.tensor_tensor(
-                out=grouped[:],
-                in0=a_acc[i][:].rearrange("p (t n) -> p n t", t=PACK),
-                in1=w_bc[:, P * i : P * (i + 1)].unsqueeze(2).to_broadcast([P, P, PACK]),
-                op=MULT,
-            )
+            empty_slots(a_acc[i], w_bc[:, P * i : P * (i + 1)], grouped[:])
 
         def quantize_a(i):
             codes = work.tile([P, P], U32, name="a_codes", align_bytes=64, bufs=3)
@@ -326,12 +296,12 @@ def tile_wrap_occupied_green_s11_kernel(tc, hop_bytes, hop_scale, left, right, h
 
         out_banks, result = {}, {}
 
-        def mult_out(i, new_banks):
-            rows = results.tile([P, SITES], F32, name="result")
+        def mult_out(i):
+            rows = work.tile([P, SITES], F32, name="result", bufs=5)
             result[i] = rows
             for q in range(CHUNKS):
                 cols = slice(BANK * q, BANK * (q + 1))
-                bank = new_banks[q]()
+                bank = turn_bank() if i >= SHARE_FROM and q == 1 else wide_bank()
                 out_banks[i, q] = bank
                 nc.tensor.matmul_mx(
                     out=bank[:],
@@ -343,18 +313,13 @@ def tile_wrap_occupied_green_s11_kernel(tc, hop_bytes, hop_scale, left, right, h
                     stop=True,
                 )
 
-        def empty_out(i, q, copy, store):
+        def empty_out(i, q, copy):
             cols = slice(BANK * q, BANK * (q + 1))
             copy(out=result[i][:, cols], in_=out_banks[i, q][:])
-            if store:
+            if i >= STORE_BY_BANK_FROM:
                 nc.sync.dma_start(out=out[P * i : P * (i + 1), cols], in_=result[i][:, cols])
-
-        def store_rows(i, q0=0, q1=CHUNKS):
-            cols = slice(BANK * q0, BANK * q1)
-            nc.sync.dma_start(out=out[P * i : P * (i + 1), cols], in_=result[i][:, cols])
-
-        S = nc.scalar.copy
-        V = nc.vector.tensor_copy
+            elif q == CHUNKS - 1:
+                nc.sync.dma_start(out=out[P * i : P * (i + 1), :], in_=result[i][:])
 
         with tc.manual_schedule():
             nc.vector.memset(ones[:], 1.0)
@@ -362,7 +327,8 @@ def tile_wrap_occupied_green_s11_kernel(tc, hop_bytes, hop_scale, left, right, h
             nc.gpsimd.memset(table[:], 0.0)
             make_identity(nc, ident[:])
             clear_scales(0, 4)
-            clear_scales(4, 12)
+            clear_scales(4, TILES)
+
             nc.sync.dma_start(out=scale_cols[:], in_=hop_scale.rearrange("o (g n q) -> n (o g) q", n=P, q=PACK))
             load_hop(0, 1)
             nc.sync.dma_start(out=field_row[0:1, :], in_=field.rearrange("(o k) -> o k", o=1))
@@ -373,24 +339,25 @@ def tile_wrap_occupied_green_s11_kernel(tc, hop_bytes, hop_scale, left, right, h
             load_right(3)
             load_scales(0, 4)
             load_hinv(0, 4)
+            nc.sync.dma_start(out=field_cols[:], in_=field.rearrange("(p c) -> p c", c=PARK_COLS))
             load_hop(2, 4)
             load_left(0)
-            load_scales(4, 12)
+            load_scales(4, TILES)
             load_hinv(4, 8)
             load_left(1)
             load_hop(4, 6)
             load_left(2)
-            load_hinv(8, 12)
-            load_hop(6, 9)
-            load_hop(9, 12)
+            load_hinv(8, TILES)
 
             nc.scalar.activation(out=table[:], in_=table[:], func=EXP)
-            warm_up(4)
+            unread = wide_bank()
+            for repeat in range(4):
+                nc.tensor.matmul(unread[:], ones[:, 0:P], ones[:], start=True, stop=True)
+
             for g in range(PASSES):
                 spread_scale(g)
                 widen(0, g, g + 1)
-            spread_field(0, sum_bank())
-            spread_field(1, sum_bank())
+            field_banks = [spread_field(q) for q in range(2)]
             turn_right(0)
             turn_right(1)
             quantize_right(0)
@@ -402,32 +369,38 @@ def tile_wrap_occupied_green_s11_kernel(tc, hop_bytes, hop_scale, left, right, h
             quantize_right(2)
             quantize_hop(0)
             quantize_right(3)
-            exp_field(0, winv_bc, -1.0)
-            exp_field(0, w_bc, 1.0)
-            exp_field(1, winv_bc, -1.0)
-            field_columns(range(8, 12), winv_cols, -1.0)
+            exp_winv(0, field_banks[0])
+            exp_winv(1, field_banks[1])
+            make_winv_cols()
+            nc.scalar.activation(out=w_cols[:], in_=field_cols[:], func=EXP)
+            nc.sync.dma_start(out=out[SITES - 1, :].rearrange("(p c) -> p c", c=PARK_COLS), in_=w_cols[:])
+            nc.sync.dma_start(out=w_bc[:], in_=out[SITES - 1, :].partition_broadcast(P))
+            load_hop(6, 9)
+            load_hop(9, TILES)
             widen(2)
-            banks = (wide_bank, wide_bank, wide_bank, sum_bank, sum_bank)
-            for n in range(8):
-                mult_c(n, banks[n % 5])
-                if n in (2, 6):
-                    turn_hop(1 if n == 2 else 2)
-                if n in (5, 7):
-                    quantize_left((5, 7).index(n))
+
+            c_banks = (wide_bank, wide_bank, wide_bank, sum_bank, sum_bank)
+            for n in range(C_ROWS_FROM):
+                mult_c(n, c_banks[n % len(c_banks)]())
+                if n % 4 == 2:
+                    turn_hop(1 + n // 4)
+                if n > 4 and n % 2 == 1:
+                    quantize_left((n - 5) // 2)
                 empty_c(n)
-                if n < 6:
-                    interleave_left(n // 2, n % 2, S)
-                if n in (1, 4):
-                    widen(3 if n == 1 else 4)
-                if n == 6:
-                    quantize_hop(1)
-                if n >= 2 and n % 2 == 0:
+                if n < 2 * PASSES and n % 2 == 0:
+                    interleave_left(n // 2)
+                if n % 3 == 1 and n < 6:
+                    widen(3 + n // 3)
+                if n in (2, 4):
                     quantize_c(n // 2 - 1)
+            quantize_c(2)
+            quantize_left(PASSES - 1)
+            quantize_hop(1)
             quantize_c(3)
-            for n in range(8, 12):
-                mult_c_rows(n, banks[n % 5])
+
+            for n in range(C_ROWS_FROM, TILES):
+                mult_c_rows(n, c_banks[n % len(c_banks)]())
                 scale_c_rows(n)
-            quantize_left(2)
             quantize_hop(2)
             widen(5)
             turn_hop(3)
@@ -438,28 +411,29 @@ def tile_wrap_occupied_green_s11_kernel(tc, hop_bytes, hop_scale, left, right, h
             empty_a(0)
             quantize_c(4)
             quantize_a(0)
-            for q in (1, 2):
-                spread_field(q, wide_bank())
-                exp_field(q, w_bc, 1.0)
             quantize_c(5)
+
+            last_turn = TILES - 4
+
+            def widened(i):
+                return 6 * PASSES + (TILES - 6) * PASSES * max(2 * i - 1, 0) // (2 * last_turn - 1)
+
             for i in range(1, TILES + 1):
+                shared = i - 1 >= SHARE_FROM
                 if i < TILES:
                     mult_a(i)
-                if i <= 8:
-                    widen_passes(18 + 18 * (i - 1) // 8, 18 + 18 * i // 8)
+                if i <= last_turn:
+                    widen_passes(widened(i - 1), widened(i))
                 if i < TILES:
                     empty_a(i)
                 if i + 2 < TILES:
                     quantize_hop(i + 2)
-                mult_out(i - 1, (wide_bank, turn_bank if i > 9 else wide_bank, wide_bank))
-                shared = i > 9
+                mult_out(i - 1)
                 for q in (0, 2) if shared else range(CHUNKS):
-                    empty_out(i - 1, q, S, i > 7)
-                if i <= 7:
-                    store_rows(i - 1)
-                if 1 < i and i + 3 < TILES:
+                    empty_out(i - 1, q, on_scalar)
+                if 1 < i <= last_turn:
                     turn_hop(i + 3)
                 if i < TILES:
                     quantize_a(i)
                 if shared:
-                    empty_out(i - 1, 1, V, True)
+                    empty_out(i - 1, 1, on_vector)

@@ -44,7 +44,7 @@ def tile_wrap_occupied_green_s11_kernel(tc, hop_bytes, hop_scale, left, right, h
 
         ident = keep.tile([P, P], F32)
         table = keep.tile([P, 1], F32)
-        ones = keep.tile([P, BANK], BF16)
+        ones = keep.tile([P, P], BF16)
         field_row = keep.tile([P, SITES], BF16)
         field_cols = keep.tile([PARK_ROWS, PARK_COLS], BF16)
         w_cols = keep.tile([PARK_ROWS, PARK_COLS], F32)
@@ -121,7 +121,7 @@ def tile_wrap_occupied_green_s11_kernel(tc, hop_bytes, hop_scale, left, right, h
 
         def spread_field(q):
             bank = sum_bank()
-            nc.tensor.matmul(bank[:], ones[:, 0:P], field_row[:, BANK * q : BANK * (q + 1)], start=True, stop=True)
+            nc.tensor.matmul(bank[:], ones[:], field_row[:, BANK * q : BANK * (q + 1)], start=True, stop=True)
             return bank
 
         def exp_winv(q, bank):
@@ -147,13 +147,13 @@ def tile_wrap_occupied_green_s11_kernel(tc, hop_bytes, hop_scale, left, right, h
             for i in range(a // PASSES, (b - 1) // PASSES + 1):
                 widen(i, max(a - PASSES * i, 0), min(b - PASSES * i, PASSES))
 
-        def copy_turned(bank, groups, target):
-            nc.scalar.copy(
+        def copy_turned(bank, groups, target, copy):
+            copy(
                 out=target.bitcast(F32).rearrange("p (l r u) -> p l r u", r=P, u=2),
                 in_=bank[:, 0 : 2 * P * groups].rearrange("p (l u r) -> p l r u", u=2, r=P),
             )
 
-        def turn(rows, key):
+        def turn(rows, key, copy):
             grouped = work.tile([P, SITES], BF16, name="turned", align_bytes=64, bufs=5)
             turned[key] = grouped
             words = rows[:].bitcast(F32)
@@ -163,13 +163,13 @@ def tile_wrap_occupied_green_s11_kernel(tc, hop_bytes, hop_scale, left, right, h
                     for u in range(2):
                         col = P * (2 * (g - g0) + u)
                         nc.tensor.transpose(bank[:, col : col + P], words[:, 2 * P * g + u : 2 * P * (g + 1) : 2], ident[:])
-                copy_turned(bank, g1 - g0, grouped[:, K_PASS * g0 : K_PASS * g1])
+                copy_turned(bank, g1 - g0, grouped[:, K_PASS * g0 : K_PASS * g1], copy)
 
-        def turn_hop(i):
-            turn(hop_bf[i], ("hop", i))
+        def turn_hop(i, copy=on_scalar):
+            turn(hop_bf[i], ("hop", i), copy)
 
         def turn_right(t):
-            turn(right_rows[t], ("right", t))
+            turn(right_rows[t], ("right", t), on_scalar)
 
         def quantize_hop(i):
             codes = work.tile([P, PASSES * P], U32, name="hop_codes", align_bytes=64, bufs=4)
@@ -267,7 +267,7 @@ def tile_wrap_occupied_green_s11_kernel(tc, hop_bytes, hop_scale, left, right, h
                 for u in range(2):
                     col = P * (2 * s + u)
                     nc.tensor.transpose(bank[:, col : col + P], words[:, P * u : P * (u + 1)], ident[:])
-            copy_turned(bank, 2, c_grouped[pair][:].rearrange("p s n t -> p (s n t)"))
+            copy_turned(bank, 2, c_grouped[pair][:].rearrange("p s n t -> p (s n t)"), on_scalar)
 
         def quantize_c(pair):
             cols = slice(2 * P * pair, 2 * P * (pair + 1))
@@ -350,9 +350,6 @@ def tile_wrap_occupied_green_s11_kernel(tc, hop_bytes, hop_scale, left, right, h
             load_hinv(8, TILES)
 
             nc.scalar.activation(out=table[:], in_=table[:], func=EXP)
-            unread = wide_bank()
-            for repeat in range(4):
-                nc.tensor.matmul(unread[:], ones[:, 0:P], ones[:], start=True, stop=True)
 
             for g in range(PASSES):
                 spread_scale(g)
@@ -431,9 +428,11 @@ def tile_wrap_occupied_green_s11_kernel(tc, hop_bytes, hop_scale, left, right, h
                 mult_out(i - 1)
                 for q in (0, 2) if shared else range(CHUNKS):
                     empty_out(i - 1, q, on_scalar)
-                if 1 < i <= last_turn:
+                if 1 < i < last_turn:
                     turn_hop(i + 3)
                 if i < TILES:
                     quantize_a(i)
+                if i == last_turn:
+                    turn_hop(i + 3, on_vector)
                 if shared:
                     empty_out(i - 1, 1, on_vector)

@@ -25,7 +25,8 @@ TILES = SITES // P
 BANK = 512
 CHUNKS = SITES // BANK
 
-C_ROWS_FROM = 8
+A_LAG = 2
+C_ROWS_FROM = 10
 STORE_BY_BANK_FROM = 7
 SHARE_FROM = 9
 
@@ -44,7 +45,7 @@ def tile_wrap_occupied_green_s11_kernel(tc, hop_bytes, hop_scale, left, right, h
 
         ident = keep.tile([P, P], F32)
         table = keep.tile([P, 1], F32)
-        ones = keep.tile([P, P], BF16)
+        ones = keep.tile([P, BANK], BF16)
         field_row = keep.tile([P, SITES], BF16)
         field_cols = keep.tile([PARK_ROWS, PARK_COLS], BF16)
         w_cols = keep.tile([PARK_ROWS, PARK_COLS], F32)
@@ -53,6 +54,7 @@ def tile_wrap_occupied_green_s11_kernel(tc, hop_bytes, hop_scale, left, right, h
         w_bc = keep.tile([P, SITES], F32)
         winv_bc = keep.tile([P, P * C_ROWS_FROM], F32)
         winv_cols = keep.tile([P, TILES - C_ROWS_FROM], F32)
+        c_values = keep.tile([P, TILES * ORB], BF16, align_bytes=64)
         left_codes = keep.tile([P, PASSES, ORB], U32, align_bytes=64)
         left_sc = keep.tile([P, PASSES, ORB], U8, align_bytes=64)
         right_codes = keep.tile([P, PASSES, ORB], U32, align_bytes=64)
@@ -110,22 +112,27 @@ def tile_wrap_occupied_green_s11_kernel(tc, hop_bytes, hop_scale, left, right, h
                     in_=hinv_scales[:, 4 * q : 4 * q + 4, P * n0 : P * n1].rearrange("g q n -> q g n").bitcast(I32),
                 )
 
-        def spread_scale(g):
+        def spread_scale(g, copy):
             bank = wide_bank()
             for q in range(PACK):
                 nc.tensor.transpose(bank[:, P * q : P * (q + 1)], scale_cols[:, g, q : q + 1].to_broadcast([P, P]), ident[:])
-            nc.scalar.copy(
+            copy(
                 out=scale_bc[:, K_PASS * g : K_PASS * (g + 1)].rearrange("p (n q) -> p n q", q=PACK),
                 in_=bank[:].rearrange("p (q n) -> p n q", q=PACK),
             )
 
-        def spread_field(q):
-            bank = sum_bank()
-            nc.tensor.matmul(bank[:], ones[:], field_row[:, BANK * q : BANK * (q + 1)], start=True, stop=True)
+        def warm_up(bank, count):
+            for r in range(count):
+                nc.tensor.matmul(bank[:], ones[:, 0:P], ones[:], start=True, stop=True)
+
+        def spread_field(q, bank):
+            cols = slice(BANK * q, min(BANK * (q + 1), P * C_ROWS_FROM))
+            nc.tensor.matmul(bank[:, 0 : cols.stop - cols.start], ones[:, 0:P], field_row[:, cols], start=True, stop=True)
             return bank
 
         def exp_winv(q, bank):
-            nc.scalar.activation(out=winv_bc[:, BANK * q : BANK * (q + 1)], in_=bank[:], func=EXP, scale=-1.0)
+            cols = slice(BANK * q, min(BANK * (q + 1), P * C_ROWS_FROM))
+            nc.scalar.activation(out=winv_bc[:, cols], in_=bank[:, 0 : cols.stop - cols.start], func=EXP, scale=-1.0)
 
         def make_winv_cols():
             bank = turn_bank()
@@ -134,7 +141,7 @@ def tile_wrap_occupied_green_s11_kernel(tc, hop_bytes, hop_scale, left, right, h
                 nc.tensor.matmul(bank[:, j : j + 1], field_row[:, P * n : P * (n + 1)], ones[:, 0:1], start=True, stop=True)
             nc.scalar.activation(out=winv_cols[:], in_=bank[:, 0 : TILES - C_ROWS_FROM], func=EXP, scale=-1.0)
 
-        hop_bf, turned, hop_codes, hop_sc = {}, {}, {}, {}
+        hop_bf, staged, right_turned, hop_codes, hop_sc = {}, {}, {}, {}, {}
 
         def widen(i, g0=0, g1=PASSES):
             if g0 == 0:
@@ -149,13 +156,11 @@ def tile_wrap_occupied_green_s11_kernel(tc, hop_bytes, hop_scale, left, right, h
 
         def copy_turned(bank, groups, target, copy):
             copy(
-                out=target.bitcast(F32).rearrange("p (l r u) -> p l r u", r=P, u=2),
+                out=target.bitcast(F32).rearrange("p l (r u) -> p l r u", u=2),
                 in_=bank[:, 0 : 2 * P * groups].rearrange("p (l u r) -> p l r u", u=2, r=P),
             )
 
-        def turn(rows, key, copy):
-            grouped = work.tile([P, SITES], BF16, name="turned", align_bytes=64, bufs=5)
-            turned[key] = grouped
+        def turn(rows, grouped, copy):
             words = rows[:].bitcast(F32)
             for g0, g1 in ((0, 2), (2, 3)):
                 bank = turn_bank()
@@ -163,27 +168,32 @@ def tile_wrap_occupied_green_s11_kernel(tc, hop_bytes, hop_scale, left, right, h
                     for u in range(2):
                         col = P * (2 * (g - g0) + u)
                         nc.tensor.transpose(bank[:, col : col + P], words[:, 2 * P * g + u : 2 * P * (g + 1) : 2], ident[:])
-                copy_turned(bank, g1 - g0, grouped[:, K_PASS * g0 : K_PASS * g1], copy)
+                copy_turned(bank, g1 - g0, grouped[:, g0:g1, :], copy)
 
         def turn_hop(i, copy=on_scalar):
-            turn(hop_bf[i], ("hop", i), copy)
+            both = work.tile([P, SITES + ORB], BF16, name="staged", align_bytes=64, bufs=5)
+            staged[i] = both
+            turn(hop_bf[i], both[:].rearrange("p (g k) -> p g k", k=K_PASS), copy)
 
-        def turn_right(t):
-            turn(right_rows[t], ("right", t), on_scalar)
+        def turn_right(t, copy=on_scalar):
+            if t % 2 == 0:
+                pair = work.tile([P, PASSES, 2 * K_PASS], BF16, name="right_turned", align_bytes=64)
+                right_turned[t // 2] = pair
+            turn(right_rows[t], right_turned[t // 2][:, :, K_PASS * (t % 2) : K_PASS * (t % 2 + 1)], copy)
 
         def quantize_hop(i):
-            codes = work.tile([P, PASSES * P], U32, name="hop_codes", align_bytes=64, bufs=4)
-            sc = work.tile([P, PASSES * P], U8, name="hop_sc", align_bytes=64, bufs=4)
+            codes = work.tile([P, (PASSES + 1) * P], U32, name="hop_codes", align_bytes=64, bufs=4)
+            sc = work.tile([P, (PASSES + 1) * P], U8, name="hop_sc", align_bytes=64, bufs=4)
             hop_codes[i], hop_sc[i] = codes, sc
-            for a, b in ((0, 2 * P), (2 * P, 3 * P)):
-                nc.vector.quantize_mx(out=codes[:, a:b].bitcast(E4M3X4), scales=sc[:, a:b], in_=turned["hop", i][:, PACK * a : PACK * b])
+            for a, b in ((0, 4 * P),) if i >= A_LAG else ((0, 2 * P), (2 * P, 3 * P)):
+                nc.vector.quantize_mx(out=codes[:, a:b].bitcast(E4M3X4), scales=sc[:, a:b], in_=staged[i][:, PACK * a : PACK * b])
+            if i >= A_LAG:
+                a_codes[i - A_LAG], a_sc[i - A_LAG] = codes[:, 3 * P : 4 * P], sc[:, 3 * P : 4 * P]
 
-        def quantize_right(t):
-            m = slice(P * t, P * (t + 1))
+        def quantize_right(pair):
+            m = slice(2 * P * pair, 2 * P * (pair + 1))
             for g in range(PASSES):
-                nc.vector.quantize_mx(
-                    out=right_codes[:, g, m].bitcast(E4M3X4), scales=right_sc[:, g, m], in_=turned["right", t][:, K_PASS * g : K_PASS * (g + 1)]
-                )
+                nc.vector.quantize_mx(out=right_codes[:, g, m].bitcast(E4M3X4), scales=right_sc[:, g, m], in_=right_turned[pair][:, g, :])
 
         left_grouped = {}
 
@@ -198,42 +208,38 @@ def tile_wrap_occupied_green_s11_kernel(tc, hop_bytes, hop_scale, left, right, h
         def quantize_left(g):
             nc.vector.quantize_mx(out=left_codes[:, g, :].bitcast(E4M3X4), scales=left_sc[:, g, :], in_=left_grouped[g][:])
 
-        c_acc, c_rows, c_grouped, a_acc, a_grouped, a_codes, a_sc = {}, {}, {}, {}, {}, {}, {}
+        c_acc, c_rows, a_acc, a_grouped, a_codes, a_sc = {}, {}, {}, {}, {}, {}
 
-        def slots_product(acc, codes, sc, moving, moving_sc):
-            for t in range(PACK):
-                m = slice(P * t, P * (t + 1))
-                for g in range(PASSES):
-                    nc.tensor.matmul_mx(
-                        out=acc[:, m],
-                        lhsT=codes[:, g, m].bitcast(E4M3X4),
-                        lhsT_scale=sc[:, g, m],
-                        rhs=moving(g),
-                        rhs_scale=moving_sc(g),
-                        start=(g == 0),
-                        stop=(g == PASSES - 1),
-                    )
+        def slot_product(acc, t, operands):
+            for g in range(PASSES):
+                codes, sc, moving, moving_sc = operands(g)
+                nc.tensor.matmul_mx(
+                    out=acc[:, P * t : P * (t + 1)],
+                    lhsT=codes.bitcast(E4M3X4),
+                    lhsT_scale=sc,
+                    rhs=moving,
+                    rhs_scale=moving_sc,
+                    start=(g == 0),
+                    stop=(g == PASSES - 1),
+                )
 
         def empty_slots(acc, factor, target):
             nc.vector.tensor_tensor(
-                out=target,
+                out=target.rearrange("p (n t) -> p n t", t=PACK),
                 in0=acc[:].rearrange("p (t n) -> p n t", t=PACK),
                 in1=factor.unsqueeze(2).to_broadcast([P, P, PACK]),
                 op=MULT,
             )
 
-        def new_c_pair(pair):
-            grouped = work.tile([P, 2, P, PACK], BF16, name="c_grouped", align_bytes=64)
-            c_grouped[pair] = grouped
+        def mult_c(n, t):
+            def operands(g):
+                m = slice(P * t, P * (t + 1))
+                return right_codes[:, g, m], right_sc[:, g, m], hinv_codes[n][:, g, :].bitcast(E2M1X4), hinv_sc[n][:, g, :]
 
-        def mult_c(n, acc):
-            c_acc[n] = acc
-            slots_product(acc, right_codes, right_sc, lambda g: hinv_codes[n][:, g, :].bitcast(E2M1X4), lambda g: hinv_sc[n][:, g, :])
+            slot_product(c_acc[n], t, operands)
 
         def empty_c(n):
-            if n % 2 == 0:
-                new_c_pair(n // 2)
-            empty_slots(c_acc[n], winv_bc[:, P * n : P * (n + 1)], c_grouped[n // 2][:, n % 2, :, :])
+            empty_slots(c_acc[n], winv_bc[:, P * n : P * (n + 1)], c_values[:, ORB * n : ORB * (n + 1)])
 
         def mult_c_rows(n, acc):
             c_acc[n] = acc
@@ -260,39 +266,41 @@ def tile_wrap_occupied_green_s11_kernel(tc, hop_bytes, hop_scale, left, right, h
             )
 
         def turn_c_rows(pair):
-            new_c_pair(pair)
             bank = turn_bank()
             for s in range(2):
                 words = c_rows[2 * pair + s][:].bitcast(F32)
                 for u in range(2):
                     col = P * (2 * s + u)
                     nc.tensor.transpose(bank[:, col : col + P], words[:, P * u : P * (u + 1)], ident[:])
-            copy_turned(bank, 2, c_grouped[pair][:].rearrange("p s n t -> p (s n t)"), on_scalar)
+            copy_turned(bank, 2, c_values[:, 2 * ORB * pair : 2 * ORB * (pair + 1)].rearrange("p (s k) -> p s k", s=2), on_scalar)
 
-        def quantize_c(pair):
-            cols = slice(2 * P * pair, 2 * P * (pair + 1))
-            nc.vector.quantize_mx(
-                out=c_codes[:, cols].bitcast(E4M3X4),
-                scales=c_sc[:, cols],
-                in_=c_grouped[pair][:].rearrange("p s n t -> p (s n t)"),
-            )
+        def quantize_c(n0, n1):
+            cols = slice(P * n0, P * n1)
+            nc.vector.quantize_mx(out=c_codes[:, cols].bitcast(E4M3X4), scales=c_sc[:, cols], in_=c_values[:, ORB * n0 : ORB * n1])
 
         def mult_a(i):
             a_acc[i] = sum_bank()
-            slots_product(
-                a_acc[i], left_codes, left_sc, lambda g: hop_codes[i][:, P * g : P * (g + 1)].bitcast(E4M3X4), lambda g: hop_sc[i][:, P * g : P * (g + 1)]
-            )
+            for t in range(PACK):
+                m = slice(P * t, P * (t + 1))
+                slot_product(
+                    a_acc[i],
+                    t,
+                    lambda g: (left_codes[:, g, m], left_sc[:, g, m], hop_codes[i][:, P * g : P * (g + 1)].bitcast(E4M3X4), hop_sc[i][:, P * g : P * (g + 1)]),
+                )
 
         def empty_a(i):
-            grouped = work.tile([P, P, PACK], BF16, name="a_grouped", align_bytes=64, bufs=3)
-            a_grouped[i] = grouped
-            empty_slots(a_acc[i], w_bc[:, P * i : P * (i + 1)], grouped[:])
+            if i + A_LAG < TILES:
+                a_grouped[i] = staged[i + A_LAG][:, SITES : SITES + ORB]
+            else:
+                values = work.tile([P, ORB], BF16, name="a_values", align_bytes=64)
+                a_grouped[i] = values[:]
+            empty_slots(a_acc[i], w_bc[:, P * i : P * (i + 1)], a_grouped[i])
 
         def quantize_a(i):
-            codes = work.tile([P, P], U32, name="a_codes", align_bytes=64, bufs=3)
-            sc = work.tile([P, P], U8, name="a_sc", align_bytes=64, bufs=3)
-            a_codes[i], a_sc[i] = codes, sc
-            nc.vector.quantize_mx(out=codes[:].bitcast(E4M3X4), scales=sc[:], in_=a_grouped[i][:].rearrange("p n t -> p (n t)"))
+            codes = work.tile([P, P], U32, name="a_codes", align_bytes=64)
+            sc = work.tile([P, P], U8, name="a_sc", align_bytes=64)
+            a_codes[i], a_sc[i] = codes[:], sc[:]
+            nc.vector.quantize_mx(out=codes[:].bitcast(E4M3X4), scales=sc[:], in_=a_grouped[i])
 
         out_banks, result = {}, {}
 
@@ -305,8 +313,8 @@ def tile_wrap_occupied_green_s11_kernel(tc, hop_bytes, hop_scale, left, right, h
                 out_banks[i, q] = bank
                 nc.tensor.matmul_mx(
                     out=bank[:],
-                    lhsT=a_codes[i][:].bitcast(E4M3X4),
-                    lhsT_scale=a_sc[i][:],
+                    lhsT=a_codes[i].bitcast(E4M3X4),
+                    lhsT_scale=a_sc[i],
                     rhs=c_codes[:, cols].bitcast(E4M3X4),
                     rhs_scale=c_sc[:, cols],
                     start=True,
@@ -322,117 +330,133 @@ def tile_wrap_occupied_green_s11_kernel(tc, hop_bytes, hop_scale, left, right, h
                 nc.sync.dma_start(out=out[P * i : P * (i + 1), :], in_=result[i][:])
 
         with tc.manual_schedule():
+            nc.vector.memset(table[:], 0.0)
             nc.vector.memset(ones[:], 1.0)
             nc.vector.memset(field_row[:].bitcast(U32), 0)
-            nc.gpsimd.memset(table[:], 0.0)
             make_identity(nc, ident[:])
             clear_scales(0, 4)
             clear_scales(4, TILES)
+            nc.scalar.activation(out=table[:], in_=table[:], func=EXP)
 
             nc.sync.dma_start(out=scale_cols[:], in_=hop_scale.rearrange("o (g n q) -> n (o g) q", n=P, q=PACK))
-            load_hop(0, 1)
-            nc.sync.dma_start(out=field_row[0:1, :], in_=field.rearrange("(o k) -> o k", o=1))
             load_right(0)
+            load_hop(0, 1)
+            nc.sync.dma_start(out=field_cols[:], in_=field.rearrange("(p c) -> p c", c=PARK_COLS))
             load_right(1)
+            nc.sync.dma_start(out=field_row[0:1, :], in_=field.rearrange("(o k) -> o k", o=1))
             load_hop(1, 2)
             load_right(2)
             load_right(3)
+            load_hop(2, 3)
             load_scales(0, 4)
             load_hinv(0, 4)
-            nc.sync.dma_start(out=field_cols[:], in_=field.rearrange("(p c) -> p c", c=PARK_COLS))
-            load_hop(2, 4)
+            load_hop(3, 4)
             load_left(0)
             load_scales(4, TILES)
             load_hinv(4, 8)
             load_left(1)
-            load_hop(4, 6)
-            load_left(2)
-            load_hinv(8, TILES)
 
-            nc.scalar.activation(out=table[:], in_=table[:], func=EXP)
+            warm_up(sum_bank(), 4)
 
             for g in range(PASSES):
-                spread_scale(g)
+                spread_scale(g, on_vector if g == 0 else on_scalar)
                 widen(0, g, g + 1)
-            field_banks = [spread_field(q) for q in range(2)]
+            spare = wide_bank()
             turn_right(0)
+            warm_up(spare, 2)
             turn_right(1)
-            quantize_right(0)
-            widen(1)
-            quantize_right(1)
-            turn_hop(0)
-            turn_right(2)
-            turn_right(3)
-            quantize_right(2)
-            quantize_hop(0)
-            quantize_right(3)
-            exp_winv(0, field_banks[0])
-            exp_winv(1, field_banks[1])
-            make_winv_cols()
+            warm_up(spare, 1)
+            field_banks = [spread_field(0, sum_bank())]
             nc.scalar.activation(out=w_cols[:], in_=field_cols[:], func=EXP)
             nc.sync.dma_start(out=out[SITES - 1, :].rearrange("(p c) -> p c", c=PARK_COLS), in_=w_cols[:])
+            load_hinv(8, TILES)
+            load_left(2)
+            load_hop(4, 6)
             nc.sync.dma_start(out=w_bc[:], in_=out[SITES - 1, :].partition_broadcast(P))
             load_hop(6, 9)
             load_hop(9, TILES)
-            widen(2)
+            widen(1)
+            quantize_right(0)
+            turn_right(2)
+            field_banks.append(spread_field(1, sum_bank()))
+            warm_up(spare, 1)
+            turn_right(3)
+            field_banks.append(spread_field(2, wide_bank()))
+            widen(2, 0, 1)
+            quantize_right(1)
+            warm_up(spare, 1)
+            exp_winv(0, field_banks[0])
+            turn_hop(0)
+            exp_winv(1, field_banks[1])
+            exp_winv(2, field_banks[2])
+            make_winv_cols()
+            widen(2, 1, 3)
 
-            c_banks = (wide_bank, wide_bank, wide_bank, sum_bank, sum_bank)
+            c_banks = (wide_bank, wide_bank, sum_bank, sum_bank, wide_bank)
+            for n in range(2):
+                c_acc[n] = c_banks[n]()
+            for t in range(PACK):
+                for n in range(2):
+                    mult_c(n, t)
             for n in range(C_ROWS_FROM):
-                mult_c(n, c_banks[n % len(c_banks)]())
-                if n % 4 == 2:
-                    turn_hop(1 + n // 4)
-                if n > 4 and n % 2 == 1:
-                    quantize_left((n - 5) // 2)
+                if n >= 2:
+                    c_acc[n] = c_banks[n % len(c_banks)]()
+                    for t in range(PACK):
+                        mult_c(n, t)
+                if n in (4, 7):
+                    turn_hop(1 + n // 6)
+                if n in (0, 4, 7):
+                    interleave_left((n + 1) // 4)
                 empty_c(n)
-                if n < 2 * PASSES and n % 2 == 0:
-                    interleave_left(n // 2)
-                if n % 3 == 1 and n < 6:
-                    widen(3 + n // 3)
-                if n in (2, 4):
-                    quantize_c(n // 2 - 1)
-            quantize_c(2)
-            quantize_left(PASSES - 1)
-            quantize_hop(1)
-            quantize_c(3)
-
+                if n == 1:
+                    quantize_hop(0)
+                if n == 3:
+                    widen(3, 0, 2)
+                    quantize_left(0)
+                if n == 4:
+                    quantize_c(0, 4)
+                if n == 6:
+                    quantize_hop(1)
+                    widen(3, 2, 3)
+                if n == 7:
+                    quantize_left(1)
+                if n == 8:
+                    quantize_c(4, 8)
             for n in range(C_ROWS_FROM, TILES):
-                mult_c_rows(n, c_banks[n % len(c_banks)]())
+                mult_c_rows(n, wide_bank())
                 scale_c_rows(n)
-            quantize_hop(2)
-            widen(5)
+            quantize_left(2)
             turn_hop(3)
-            turn_c_rows(4)
+            widen(4, 0, 2)
             mult_a(0)
             turn_c_rows(5)
-            turn_hop(4)
             empty_a(0)
-            quantize_c(4)
-            quantize_a(0)
-            quantize_c(5)
+            quantize_c(8, 10)
+            quantize_hop(2)
 
-            last_turn = TILES - 4
+            last_turn = TILES - 3
 
             def widened(i):
-                return 6 * PASSES + (TILES - 6) * PASSES * max(2 * i - 1, 0) // (2 * last_turn - 1)
+                return min(14 + (TILES * PASSES - 14) * i // 8, TILES * PASSES)
 
             for i in range(1, TILES + 1):
                 shared = i - 1 >= SHARE_FROM
                 if i < TILES:
                     mult_a(i)
-                if i <= last_turn:
-                    widen_passes(widened(i - 1), widened(i))
+                if 1 < i <= last_turn:
+                    turn_hop(i + 2)
+                if i == 1:
+                    quantize_c(10, 12)
                 if i < TILES:
                     empty_a(i)
+                if widened(i) > widened(i - 1):
+                    widen_passes(widened(i - 1), widened(i))
                 if i + 2 < TILES:
                     quantize_hop(i + 2)
                 mult_out(i - 1)
                 for q in (0, 2) if shared else range(CHUNKS):
                     empty_out(i - 1, q, on_scalar)
-                if 1 < i < last_turn:
-                    turn_hop(i + 3)
-                if i < TILES:
+                if i + 2 >= TILES and i < TILES:
                     quantize_a(i)
-                if i == last_turn:
-                    turn_hop(i + 3, on_vector)
                 if shared:
                     empty_out(i - 1, 1, on_vector)

@@ -27,7 +27,7 @@ CHUNKS = SITES // BANK
 
 A_LAG = 2
 C_ROWS_FROM = 10
-STORE_BY_BANK_FROM = 7
+LAST_TURN = 9
 SHARE_FROM = 9
 
 PARK_ROWS, PARK_COLS = 64, 24
@@ -170,9 +170,14 @@ def tile_wrap_occupied_green_s11_kernel(tc, hop_bytes, hop_scale, left, right, h
                         nc.tensor.transpose(bank[:, col : col + P], words[:, 2 * P * g + u : 2 * P * (g + 1) : 2], ident[:])
                 copy_turned(bank, g1 - g0, grouped[:, g0:g1, :], copy)
 
+        def staged_tile(i):
+            if i not in staged:
+                both = work.tile([P, SITES + ORB], BF16, name="staged", align_bytes=64, bufs=6)
+                staged[i] = both
+            return staged[i]
+
         def turn_hop(i, copy=on_scalar):
-            both = work.tile([P, SITES + ORB], BF16, name="staged", align_bytes=64, bufs=5)
-            staged[i] = both
+            both = staged_tile(i)
             turn(hop_bf[i], both[:].rearrange("p (g k) -> p g k", k=K_PASS), copy)
 
         def turn_right(t, copy=on_scalar):
@@ -290,7 +295,7 @@ def tile_wrap_occupied_green_s11_kernel(tc, hop_bytes, hop_scale, left, right, h
 
         def empty_a(i):
             if i + A_LAG < TILES:
-                a_grouped[i] = staged[i + A_LAG][:, SITES : SITES + ORB]
+                a_grouped[i] = staged_tile(i + A_LAG)[:, SITES : SITES + ORB]
             else:
                 values = work.tile([P, ORB], BF16, name="a_values", align_bytes=64)
                 a_grouped[i] = values[:]
@@ -309,7 +314,7 @@ def tile_wrap_occupied_green_s11_kernel(tc, hop_bytes, hop_scale, left, right, h
             result[i] = rows
             for q in range(CHUNKS):
                 cols = slice(BANK * q, BANK * (q + 1))
-                bank = turn_bank() if i >= SHARE_FROM and q == 1 else wide_bank()
+                bank = turn_bank() if i > LAST_TURN - 1 and q == CHUNKS - 1 else wide_bank()
                 out_banks[i, q] = bank
                 nc.tensor.matmul_mx(
                     out=bank[:],
@@ -322,16 +327,15 @@ def tile_wrap_occupied_green_s11_kernel(tc, hop_bytes, hop_scale, left, right, h
                 )
 
         def empty_out(i, q, copy):
-            cols = slice(BANK * q, BANK * (q + 1))
-            copy(out=result[i][:, cols], in_=out_banks[i, q][:])
-            if i >= STORE_BY_BANK_FROM:
-                nc.sync.dma_start(out=out[P * i : P * (i + 1), cols], in_=result[i][:, cols])
-            elif q == CHUNKS - 1:
-                nc.sync.dma_start(out=out[P * i : P * (i + 1), :], in_=result[i][:])
+            copy(out=result[i][:, BANK * q : BANK * (q + 1)], in_=out_banks[i, q][:])
+
+        def store(i, q0, q1):
+            cols = slice(BANK * q0, BANK * q1)
+            nc.sync.dma_start(out=out[P * i : P * (i + 1), cols], in_=result[i][:, cols])
 
         with tc.manual_schedule():
-            nc.vector.memset(table[:], 0.0)
             nc.vector.memset(ones[:], 1.0)
+            nc.vector.memset(table[:], 0.0)
             nc.vector.memset(field_row[:].bitcast(U32), 0)
             make_identity(nc, ident[:])
             clear_scales(0, 4)
@@ -339,8 +343,8 @@ def tile_wrap_occupied_green_s11_kernel(tc, hop_bytes, hop_scale, left, right, h
             nc.scalar.activation(out=table[:], in_=table[:], func=EXP)
 
             nc.sync.dma_start(out=scale_cols[:], in_=hop_scale.rearrange("o (g n q) -> n (o g) q", n=P, q=PACK))
-            load_right(0)
             load_hop(0, 1)
+            load_right(0)
             nc.sync.dma_start(out=field_cols[:], in_=field.rearrange("(p c) -> p c", c=PARK_COLS))
             load_right(1)
             nc.sync.dma_start(out=field_row[0:1, :], in_=field.rearrange("(o k) -> o k", o=1))
@@ -356,16 +360,14 @@ def tile_wrap_occupied_green_s11_kernel(tc, hop_bytes, hop_scale, left, right, h
             load_hinv(4, 8)
             load_left(1)
 
-            warm_up(sum_bank(), 4)
-
+            spare = sum_bank()
+            warm_up(spare, 3)
             for g in range(PASSES):
                 spread_scale(g, on_vector if g == 0 else on_scalar)
                 widen(0, g, g + 1)
-            spare = wide_bank()
             turn_right(0)
-            warm_up(spare, 2)
-            turn_right(1)
             warm_up(spare, 1)
+            turn_right(1)
             field_banks = [spread_field(0, sum_bank())]
             nc.scalar.activation(out=w_cols[:], in_=field_cols[:], func=EXP)
             nc.sync.dma_start(out=out[SITES - 1, :].rearrange("(p c) -> p c", c=PARK_COLS), in_=w_cols[:])
@@ -378,13 +380,12 @@ def tile_wrap_occupied_green_s11_kernel(tc, hop_bytes, hop_scale, left, right, h
             widen(1)
             quantize_right(0)
             turn_right(2)
-            field_banks.append(spread_field(1, sum_bank()))
             warm_up(spare, 1)
             turn_right(3)
+            field_banks.append(spread_field(1, sum_bank()))
             field_banks.append(spread_field(2, wide_bank()))
             widen(2, 0, 1)
             quantize_right(1)
-            warm_up(spare, 1)
             exp_winv(0, field_banks[0])
             turn_hop(0)
             exp_winv(1, field_banks[1])
@@ -434,8 +435,6 @@ def tile_wrap_occupied_green_s11_kernel(tc, hop_bytes, hop_scale, left, right, h
             quantize_c(8, 10)
             quantize_hop(2)
 
-            last_turn = TILES - 3
-
             def widened(i):
                 return min(14 + (TILES * PASSES - 14) * i // 8, TILES * PASSES)
 
@@ -443,20 +442,22 @@ def tile_wrap_occupied_green_s11_kernel(tc, hop_bytes, hop_scale, left, right, h
                 shared = i - 1 >= SHARE_FROM
                 if i < TILES:
                     mult_a(i)
-                if 1 < i <= last_turn:
-                    turn_hop(i + 2)
-                if i == 1:
-                    quantize_c(10, 12)
-                if i < TILES:
+                    if i == 1:
+                        quantize_c(10, 12)
                     empty_a(i)
                 if widened(i) > widened(i - 1):
                     widen_passes(widened(i - 1), widened(i))
+                if 1 < i < LAST_TURN:
+                    turn_hop(i + 2)
+                if i == LAST_TURN:
+                    turn_hop(i + 2, copy=on_vector)
                 if i + 2 < TILES:
                     quantize_hop(i + 2)
                 mult_out(i - 1)
-                for q in (0, 2) if shared else range(CHUNKS):
-                    empty_out(i - 1, q, on_scalar)
                 if i + 2 >= TILES and i < TILES:
                     quantize_a(i)
-                if shared:
-                    empty_out(i - 1, 1, on_vector)
+                for q in range(CHUNKS):
+                    empty_out(i - 1, q, on_vector if shared and q == CHUNKS - 1 else on_scalar)
+                    for q0, q1 in (((0, 3),) if i - 1 < 7 else ((0, 1), (1, 3)) if i < TILES else ((0, 1), (1, 2), (2, 3))):
+                        if q1 == q + 1:
+                            store(i - 1, q0, q1)

@@ -14,6 +14,7 @@ FP8 = mybir.dt.float8_e4m3fn
 E4M3X4 = mybir.dt.float8_e4m3fn_x4
 E2M1X4 = mybir.dt.float4_e2m1fn_x4
 MULT = mybir.AluOpType.mult
+ADD = mybir.AluOpType.add
 EXP = mybir.ActivationFunctionType.Exp
 COPY = mybir.ActivationFunctionType.Copy
 
@@ -26,8 +27,10 @@ BANK = 512
 CHUNKS = SITES // BANK
 
 A_LAG = 2
-C_ROWS_FROM = 10
+C_ROWS_FROM = 8
 LAST_TURN = 9
+WCOL = 128
+PAIR_FIRST = (1, 4, 6, 8)
 SHARE_FROM = 9
 
 PARK_ROWS, PARK_COLS = 64, 24
@@ -65,14 +68,11 @@ def tile_wrap_occupied_green_s11_kernel(tc, hop_bytes, hop_scale, left, right, h
         on_scalar = nc.scalar.copy
         on_vector = nc.vector.tensor_copy
 
-        def wide_bank():
-            return psum.tile([P, BANK], F32, name="wide", bufs=3)
+        def ring_bank():
+            return psum.tile([P, BANK], F32, name="ring", bufs=6)
 
         def sum_bank():
             return psum.tile([P, BANK], F32, name="sums", bufs=2)
-
-        def turn_bank():
-            return psum.tile([P, BANK], F32, name="turns", bufs=3)
 
         hop_raw, left_rows, right_rows, hinv_codes, hinv_sc, scale_tiles = {}, {}, {}, {}, {}, {}
 
@@ -113,7 +113,7 @@ def tile_wrap_occupied_green_s11_kernel(tc, hop_bytes, hop_scale, left, right, h
                 )
 
         def spread_scale(g, copy):
-            bank = wide_bank()
+            bank = ring_bank()
             for q in range(PACK):
                 nc.tensor.transpose(bank[:, P * q : P * (q + 1)], scale_cols[:, g, q : q + 1].to_broadcast([P, P]), ident[:])
             copy(
@@ -135,11 +135,11 @@ def tile_wrap_occupied_green_s11_kernel(tc, hop_bytes, hop_scale, left, right, h
             nc.scalar.activation(out=winv_bc[:, cols], in_=bank[:, 0 : cols.stop - cols.start], func=EXP, scale=-1.0)
 
         def make_winv_cols():
-            bank = turn_bank()
+            bank = ring_bank()
             for n in range(C_ROWS_FROM, TILES):
                 j = n - C_ROWS_FROM
-                nc.tensor.matmul(bank[:, j : j + 1], field_row[:, P * n : P * (n + 1)], ones[:, 0:1], start=True, stop=True)
-            nc.scalar.activation(out=winv_cols[:], in_=bank[:, 0 : TILES - C_ROWS_FROM], func=EXP, scale=-1.0)
+                nc.tensor.matmul(bank[:, WCOL * j : WCOL * (j + 1)], field_row[:, P * n : P * (n + 1)], ones[:, 0:WCOL], start=True, stop=True)
+            nc.scalar.activation(out=winv_cols[:], in_=bank[:, 0 : WCOL * (TILES - C_ROWS_FROM) : WCOL], func=EXP, scale=-1.0)
 
         hop_bf, staged, right_turned, hop_codes, hop_sc = {}, {}, {}, {}, {}
 
@@ -160,40 +160,50 @@ def tile_wrap_occupied_green_s11_kernel(tc, hop_bytes, hop_scale, left, right, h
                 in_=bank[:, 0 : 2 * P * groups].rearrange("p (l u r) -> p l r u", u=2, r=P),
             )
 
-        def turn(rows, grouped, copy):
-            words = rows[:].bitcast(F32)
-            for g0, g1 in ((0, 2), (2, 3)):
-                bank = turn_bank()
-                for g in range(g0, g1):
-                    for u in range(2):
-                        col = P * (2 * (g - g0) + u)
-                        nc.tensor.transpose(bank[:, col : col + P], words[:, 2 * P * g + u : 2 * P * (g + 1) : 2], ident[:])
-                copy_turned(bank, g1 - g0, grouped[:, g0:g1, :], copy)
+        def turn_bank_full(groups, target, copy):
+            bank = ring_bank()
+            for s, (rows, g) in enumerate(groups):
+                words = rows[:].bitcast(F32)
+                for u in range(2):
+                    col = P * (2 * s + u)
+                    nc.tensor.transpose(bank[:, col : col + P], words[:, 2 * P * g + u : 2 * P * (g + 1) : 2], ident[:])
+            copy_turned(bank, len(groups), target, copy)
 
-        def staged_tile(i):
-            if i not in staged:
-                both = work.tile([P, SITES + ORB], BF16, name="staged", align_bytes=64, bufs=6)
-                staged[i] = both
-            return staged[i]
+        def staged_pair(j):
+            if j not in staged:
+                both = work.tile([P, 2 * (SITES + ORB)], BF16, name="staged", align_bytes=64, bufs=3)
+                staged[j] = both
+            return staged[j]
 
-        def turn_hop(i, copy=on_scalar):
-            both = staged_tile(i)
-            turn(hop_bf[i], both[:].rearrange("p (g k) -> p g k", k=K_PASS), copy)
+        def staged_half(i):
+            return staged_pair(i - i % 2)[:, (SITES + ORB) * (i % 2) : (SITES + ORB) * (i % 2 + 1)]
+
+        def turn_hop(b0, b1, copy=on_scalar):
+            for b in range(b0, b1):
+                j = 2 * (b // PASSES)
+                first = ORB + 2 * K_PASS * (b % PASSES)
+                groups = [(hop_bf[k // PASSES], k % PASSES) for k in (2 * b, 2 * b + 1)]
+                turn_bank_full(groups, staged_pair(j)[:, first : first + 2 * K_PASS].rearrange("p (g k) -> p g k", k=K_PASS), copy)
 
         def turn_right(t, copy=on_scalar):
             if t % 2 == 0:
                 pair = work.tile([P, PASSES, 2 * K_PASS], BF16, name="right_turned", align_bytes=64)
                 right_turned[t // 2] = pair
-            turn(right_rows[t], right_turned[t // 2][:, :, K_PASS * (t % 2) : K_PASS * (t % 2 + 1)], copy)
+            target = right_turned[t // 2][:, :, K_PASS * (t % 2) : K_PASS * (t % 2 + 1)]
+            for g0, g1 in ((0, 2), (2, 3)):
+                turn_bank_full([(right_rows[t], g) for g in range(g0, g1)], target[:, g0:g1, :], copy)
 
         def quantize_hop(i):
             codes = work.tile([P, (PASSES + 1) * P], U32, name="hop_codes", align_bytes=64, bufs=4)
             sc = work.tile([P, (PASSES + 1) * P], U8, name="hop_sc", align_bytes=64, bufs=4)
-            hop_codes[i], hop_sc[i] = codes, sc
-            for a, b in ((0, 4 * P),) if i >= A_LAG else ((0, 2 * P), (2 * P, 3 * P)):
-                nc.vector.quantize_mx(out=codes[:, a:b].bitcast(E4M3X4), scales=sc[:, a:b], in_=staged[i][:, PACK * a : PACK * b])
-            if i >= A_LAG:
-                a_codes[i - A_LAG], a_sc[i - A_LAG] = codes[:, 3 * P : 4 * P], sc[:, 3 * P : 4 * P]
+            hop_cols, a_cols = (slice(P, 4 * P), slice(0, P)) if i % 2 == 0 else (slice(0, 3 * P), slice(3 * P, 4 * P))
+            first = hop_cols.start
+            joint = A_LAG <= i < TILES - 1
+            for a, b in ((0, 4 * P),) if joint else ((first, first + 2 * P), (first + 2 * P, first + 3 * P)):
+                nc.vector.quantize_mx(out=codes[:, a:b].bitcast(E4M3X4), scales=sc[:, a:b], in_=staged_half(i)[:, PACK * a : PACK * b])
+            hop_codes[i], hop_sc[i] = codes[:, hop_cols], sc[:, hop_cols]
+            if joint:
+                a_codes[i - A_LAG], a_sc[i - A_LAG] = codes[:, a_cols], sc[:, a_cols]
 
         def quantize_right(pair):
             m = slice(2 * P * pair, 2 * P * (pair + 1))
@@ -204,14 +214,25 @@ def tile_wrap_occupied_green_s11_kernel(tc, hop_bytes, hop_scale, left, right, h
 
         def interleave_left(g):
             grouped = work.tile([P, ORB * PACK], BF16, name="left_grouped", align_bytes=64)
-            left_grouped[g] = grouped
+            left_grouped[g] = grouped[:]
             nc.scalar.copy(
                 out=grouped[:].rearrange("p (t m j) -> p m t j", t=PACK, j=PACK),
                 in_=left_rows[g][:].rearrange("p j (m t) -> p m t j", t=PACK),
             )
 
+        def interleave_left_aside(g, grouped):
+            left_grouped[g] = grouped
+            nc.gpsimd.tensor_scalar(
+                out=grouped.rearrange("p (t m j) -> p m t j", t=PACK, j=PACK),
+                in0=left_rows[g][:].rearrange("p j (m t) -> p m t j", t=PACK),
+                scalar1=1.0,
+                scalar2=0.0,
+                op0=MULT,
+                op1=ADD,
+            )
+
         def quantize_left(g):
-            nc.vector.quantize_mx(out=left_codes[:, g, :].bitcast(E4M3X4), scales=left_sc[:, g, :], in_=left_grouped[g][:])
+            nc.vector.quantize_mx(out=left_codes[:, g, :].bitcast(E4M3X4), scales=left_sc[:, g, :], in_=left_grouped[g])
 
         c_acc, c_rows, a_acc, a_grouped, a_codes, a_sc = {}, {}, {}, {}, {}, {}
 
@@ -260,7 +281,7 @@ def tile_wrap_occupied_green_s11_kernel(tc, hop_bytes, hop_scale, left, right, h
                 )
 
         def scale_c_rows(n):
-            rows = work.tile([P, ORB], BF16, name="c_rows", bufs=4)
+            rows = work.tile([P, ORB], BF16, name="c_rows", bufs=6)
             c_rows[n] = rows
             j = n - C_ROWS_FROM
             nc.scalar.activation(
@@ -270,14 +291,14 @@ def tile_wrap_occupied_green_s11_kernel(tc, hop_bytes, hop_scale, left, right, h
                 scale=winv_cols[:, j : j + 1],
             )
 
-        def turn_c_rows(pair):
-            bank = turn_bank()
-            for s in range(2):
-                words = c_rows[2 * pair + s][:].bitcast(F32)
+        def turn_c_rows(n0, n1, new_bank=ring_bank):
+            bank = new_bank()
+            for s in range(n1 - n0):
+                words = c_rows[n0 + s][:].bitcast(F32)
                 for u in range(2):
                     col = P * (2 * s + u)
                     nc.tensor.transpose(bank[:, col : col + P], words[:, P * u : P * (u + 1)], ident[:])
-            copy_turned(bank, 2, c_values[:, 2 * ORB * pair : 2 * ORB * (pair + 1)].rearrange("p (s k) -> p s k", s=2), on_scalar)
+            copy_turned(bank, n1 - n0, c_values[:, ORB * n0 : ORB * n1].rearrange("p (s k) -> p s k", k=ORB), on_scalar)
 
         def quantize_c(n0, n1):
             cols = slice(P * n0, P * n1)
@@ -295,15 +316,15 @@ def tile_wrap_occupied_green_s11_kernel(tc, hop_bytes, hop_scale, left, right, h
 
         def empty_a(i):
             if i + A_LAG < TILES:
-                a_grouped[i] = staged_tile(i + A_LAG)[:, SITES : SITES + ORB]
+                a_grouped[i] = staged_half(i + A_LAG)[:, 0:ORB] if i % 2 == 0 else staged_half(i + A_LAG)[:, SITES:]
             else:
                 values = work.tile([P, ORB], BF16, name="a_values", align_bytes=64)
                 a_grouped[i] = values[:]
             empty_slots(a_acc[i], w_bc[:, P * i : P * (i + 1)], a_grouped[i])
 
         def quantize_a(i):
-            codes = work.tile([P, P], U32, name="a_codes", align_bytes=64)
-            sc = work.tile([P, P], U8, name="a_sc", align_bytes=64)
+            codes = work.tile([P, P], U32, name="a_codes", align_bytes=64, bufs=3)
+            sc = work.tile([P, P], U8, name="a_sc", align_bytes=64, bufs=3)
             a_codes[i], a_sc[i] = codes[:], sc[:]
             nc.vector.quantize_mx(out=codes[:].bitcast(E4M3X4), scales=sc[:], in_=a_grouped[i])
 
@@ -314,7 +335,7 @@ def tile_wrap_occupied_green_s11_kernel(tc, hop_bytes, hop_scale, left, right, h
             result[i] = rows
             for q in range(CHUNKS):
                 cols = slice(BANK * q, BANK * (q + 1))
-                bank = turn_bank() if i > LAST_TURN - 1 and q == CHUNKS - 1 else wide_bank()
+                bank = ring_bank()
                 out_banks[i, q] = bank
                 nc.tensor.matmul_mx(
                     out=bank[:],
@@ -338,8 +359,8 @@ def tile_wrap_occupied_green_s11_kernel(tc, hop_bytes, hop_scale, left, right, h
             nc.vector.memset(table[:], 0.0)
             nc.vector.memset(field_row[:].bitcast(U32), 0)
             make_identity(nc, ident[:])
-            clear_scales(0, 4)
-            clear_scales(4, TILES)
+            clear_scales(0, 5)
+            clear_scales(5, TILES)
             nc.scalar.activation(out=table[:], in_=table[:], func=EXP)
 
             nc.sync.dma_start(out=scale_cols[:], in_=hop_scale.rearrange("o (g n q) -> n (o g) q", n=P, q=PACK))
@@ -352,13 +373,13 @@ def tile_wrap_occupied_green_s11_kernel(tc, hop_bytes, hop_scale, left, right, h
             load_right(2)
             load_right(3)
             load_hop(2, 3)
-            load_scales(0, 4)
-            load_hinv(0, 4)
+            load_scales(0, 5)
+            load_hinv(0, 5)
             load_hop(3, 4)
             load_left(0)
-            load_scales(4, TILES)
-            load_hinv(4, 8)
             load_left(1)
+            load_scales(5, TILES)
+            load_hinv(5, 8)
 
             spare = sum_bank()
             warm_up(spare, 3)
@@ -371,8 +392,8 @@ def tile_wrap_occupied_green_s11_kernel(tc, hop_bytes, hop_scale, left, right, h
             field_banks = [spread_field(0, sum_bank())]
             nc.scalar.activation(out=w_cols[:], in_=field_cols[:], func=EXP)
             nc.sync.dma_start(out=out[SITES - 1, :].rearrange("(p c) -> p c", c=PARK_COLS), in_=w_cols[:])
-            load_hinv(8, TILES)
             load_left(2)
+            load_hinv(8, TILES)
             load_hop(4, 6)
             nc.sync.dma_start(out=w_bc[:], in_=out[SITES - 1, :].partition_broadcast(P))
             load_hop(6, 9)
@@ -383,81 +404,104 @@ def tile_wrap_occupied_green_s11_kernel(tc, hop_bytes, hop_scale, left, right, h
             warm_up(spare, 1)
             turn_right(3)
             field_banks.append(spread_field(1, sum_bank()))
-            field_banks.append(spread_field(2, wide_bank()))
             widen(2, 0, 1)
             quantize_right(1)
             exp_winv(0, field_banks[0])
-            turn_hop(0)
+            turn_hop(0, 2)
             exp_winv(1, field_banks[1])
-            exp_winv(2, field_banks[2])
             make_winv_cols()
             widen(2, 1, 3)
 
-            c_banks = (wide_bank, wide_bank, sum_bank, sum_bank, wide_bank)
+            c_banks = (ring_bank, ring_bank, sum_bank, sum_bank, ring_bank)
             for n in range(2):
                 c_acc[n] = c_banks[n]()
             for t in range(PACK):
                 for n in range(2):
                     mult_c(n, t)
-            for n in range(C_ROWS_FROM):
-                if n >= 2:
-                    c_acc[n] = c_banks[n % len(c_banks)]()
-                    for t in range(PACK):
-                        mult_c(n, t)
-                if n in (4, 7):
-                    turn_hop(1 + n // 6)
-                if n in (0, 4, 7):
-                    interleave_left((n + 1) // 4)
-                empty_c(n)
-                if n == 1:
-                    quantize_hop(0)
-                if n == 3:
-                    widen(3, 0, 2)
-                    quantize_left(0)
-                if n == 4:
-                    quantize_c(0, 4)
-                if n == 6:
-                    quantize_hop(1)
-                    widen(3, 2, 3)
-                if n == 7:
-                    quantize_left(1)
-                if n == 8:
-                    quantize_c(4, 8)
-            for n in range(C_ROWS_FROM, TILES):
-                mult_c_rows(n, wide_bank())
+
+            def c_slots(n):
+                c_acc[n] = c_banks[n % len(c_banks)]()
+                for t in range(PACK):
+                    mult_c(n, t)
+
+            def c_by_rows(n):
+                mult_c_rows(n, c_banks[n % len(c_banks)]())
                 scale_c_rows(n)
+
+            widen(3, 0, 2)
+            quantize_hop(0)
+            interleave_left_aside(1, staged_half(0))
+            interleave_left(0)
+            interleave_left(2)
+            for n in range(2, 6):
+                c_slots(n)
+            for n in range(6):
+                empty_c(n)
+            turn_hop(2, 4)
+            quantize_left(0)
+            quantize_left(1)
+            widen(3, 2, 3)
+            c_slots(6)
+            c_slots(7)
+            turn_hop(4, 6)
+            quantize_c(0, 4)
+            empty_c(6)
+            empty_c(7)
             quantize_left(2)
-            turn_hop(3)
+            quantize_hop(1)
             widen(4, 0, 2)
+            quantize_c(4, 8)
+            widen_passes(14, 17)
+            for n in range(C_ROWS_FROM, TILES):
+                mult_c_rows(n, (sum_bank, ring_bank, ring_bank, ring_bank)[n - C_ROWS_FROM]())
+                scale_c_rows(n)
             mult_a(0)
-            turn_c_rows(5)
+            turn_c_rows(8, 10)
+            turn_c_rows(10, 12)
+            turn_hop(6, 7)
             empty_a(0)
-            quantize_c(8, 10)
+            widen_passes(17, 18)
             quantize_hop(2)
 
-            def widened(i):
-                return min(14 + (TILES * PASSES - 14) * i // 8, TILES * PASSES)
-
-            for i in range(1, TILES + 1):
-                shared = i - 1 >= SHARE_FROM
-                if i < TILES:
-                    mult_a(i)
-                    if i == 1:
-                        quantize_c(10, 12)
-                    empty_a(i)
-                if widened(i) > widened(i - 1):
-                    widen_passes(widened(i - 1), widened(i))
-                if 1 < i < LAST_TURN:
-                    turn_hop(i + 2)
-                if i == LAST_TURN:
-                    turn_hop(i + 2, copy=on_vector)
-                if i + 2 < TILES:
-                    quantize_hop(i + 2)
-                mult_out(i - 1)
-                if i + 2 >= TILES and i < TILES:
-                    quantize_a(i)
+            def empty_and_store(i, stores, on_vector_too=()):
                 for q in range(CHUNKS):
-                    empty_out(i - 1, q, on_vector if shared and q == CHUNKS - 1 else on_scalar)
-                    for q0, q1 in (((0, 3),) if i - 1 < 7 else ((0, 1), (1, 3)) if i < TILES else ((0, 1), (1, 2), (2, 3))):
+                    empty_out(i, q, on_vector if q in on_vector_too else on_scalar)
+                    for q0, q1 in stores:
                         if q1 == q + 1:
-                            store(i - 1, q0, q1)
+                            store(i, q0, q1)
+
+            whole, split, by_bank = ((0, 3),), ((0, 1), (1, 3)), ((0, 1), (1, 2), (2, 3))
+            TURNED = (7, 7, 9, 9, 11, 13, 15, 15, 17)
+            BEFORE, AFTER = (0, 19, 21, 23, 26, 29, 31, 34, 35), (18, 19, 22, 24, 27, 30, 32, 34, 36)
+            for i in range(1, 9):
+                mult_a(i)
+                if i == 1:
+                    quantize_c(8, 12)
+                empty_a(i)
+                if BEFORE[i] > AFTER[i - 1]:
+                    widen_passes(AFTER[i - 1], BEFORE[i])
+                turn_hop(TURNED[i - 1], TURNED[i])
+                quantize_hop(i + 2)
+                if AFTER[i] > BEFORE[i]:
+                    widen_passes(BEFORE[i], AFTER[i])
+                mult_out(i - 1)
+                empty_and_store(i - 1, whole if i - 1 < 7 else split)
+            mult_a(9)
+            empty_a(9)
+            mult_out(8)
+            quantize_a(9)
+            empty_and_store(8, split)
+            turn_hop(17, 18, on_vector)
+            mult_a(10)
+            quantize_hop(11)
+            empty_a(10)
+            mult_out(9)
+            quantize_a(10)
+            empty_and_store(9, by_bank)
+            mult_a(11)
+            empty_a(11)
+            mult_out(10)
+            quantize_a(11)
+            empty_and_store(10, split, (1,))
+            mult_out(11)
+            empty_and_store(11, by_bank, (1,))

@@ -26,12 +26,15 @@ TILES = SITES // P
 BANK = 512
 CHUNKS = SITES // BANK
 
+HOP_PASSES = TILES * PASSES
+HOP_BANKS = HOP_PASSES // 2
+
 A_LAG = 2
+ALONE_FROM = 10
 C_ROWS_FROM = 8
-LAST_TURN = 9
-WCOL = 128
-PAIR_FIRST = (1, 4, 6, 8)
-SHARE_FROM = 9
+C_IN_A_ROW = 6
+HINV_FIRST = 5
+RUN_BANKS = 2
 
 PARK_ROWS, PARK_COLS = 64, 24
 
@@ -48,7 +51,7 @@ def tile_wrap_occupied_green_s11_kernel(tc, hop_bytes, hop_scale, left, right, h
 
         ident = keep.tile([P, P], F32)
         table = keep.tile([P, 1], F32)
-        ones = keep.tile([P, BANK], BF16)
+        ones = keep.tile([P, P], BF16)
         field_row = keep.tile([P, SITES], BF16)
         field_cols = keep.tile([PARK_ROWS, PARK_COLS], BF16)
         w_cols = keep.tile([PARK_ROWS, PARK_COLS], F32)
@@ -121,53 +124,61 @@ def tile_wrap_occupied_green_s11_kernel(tc, hop_bytes, hop_scale, left, right, h
                 in_=bank[:].rearrange("p (q n) -> p n q", q=PACK),
             )
 
-        def warm_up(bank, count):
-            for r in range(count):
-                nc.tensor.matmul(bank[:], ones[:, 0:P], ones[:], start=True, stop=True)
-
-        def spread_field(q, bank):
-            cols = slice(BANK * q, min(BANK * (q + 1), P * C_ROWS_FROM))
-            nc.tensor.matmul(bank[:, 0 : cols.stop - cols.start], ones[:, 0:P], field_row[:, cols], start=True, stop=True)
+        def spread_field(q):
+            bank = sum_bank()
+            nc.tensor.matmul(bank[:], ones[:], field_row[:, BANK * q : BANK * (q + 1)], start=True, stop=True)
             return bank
 
         def exp_winv(q, bank):
-            cols = slice(BANK * q, min(BANK * (q + 1), P * C_ROWS_FROM))
-            nc.scalar.activation(out=winv_bc[:, cols], in_=bank[:, 0 : cols.stop - cols.start], func=EXP, scale=-1.0)
+            nc.scalar.activation(out=winv_bc[:, BANK * q : BANK * (q + 1)], in_=bank[:], func=EXP, scale=-1.0)
 
         def make_winv_cols():
             bank = ring_bank()
             for n in range(C_ROWS_FROM, TILES):
                 j = n - C_ROWS_FROM
-                nc.tensor.matmul(bank[:, WCOL * j : WCOL * (j + 1)], field_row[:, P * n : P * (n + 1)], ones[:, 0:WCOL], start=True, stop=True)
-            nc.scalar.activation(out=winv_cols[:], in_=bank[:, 0 : WCOL * (TILES - C_ROWS_FROM) : WCOL], func=EXP, scale=-1.0)
+                nc.tensor.matmul(bank[:, P * j : P * (j + 1)], field_row[:, P * n : P * (n + 1)], ones[:], start=True, stop=True)
+            nc.scalar.activation(out=winv_cols[:], in_=bank[:, 0 : P * (TILES - C_ROWS_FROM) : P], func=EXP, scale=-1.0)
 
-        hop_bf, staged, right_turned, hop_codes, hop_sc = {}, {}, {}, {}, {}
+        def park_w():
+            nc.scalar.activation(out=w_cols[:], in_=field_cols[:], func=EXP)
+            nc.sync.dma_start(out=out[SITES - 1, :].rearrange("(p c) -> p c", c=PARK_COLS), in_=w_cols[:])
 
-        def widen(i, g0=0, g1=PASSES):
-            if g0 == 0:
-                values = work.tile([P, SITES], BF16, name="hop_bf", bufs=5)
-                hop_bf[i] = values
-            k = slice(K_PASS * g0, K_PASS * g1)
-            nc.vector.tensor_tensor(out=hop_bf[i][:, k], in0=hop_raw[i][:, k].bitcast(FP8), in1=scale_bc[:, k], op=MULT)
+        def spread_w():
+            nc.sync.dma_start(out=w_bc[:], in_=out[SITES - 1, :].partition_broadcast(P))
 
-        def widen_passes(a, b):
+        hop_bf, sorted_words, staged, right_turned, hop_codes, hop_sc = {}, {}, {}, {}, {}, {}
+
+        def widen(a, b):
             for i in range(a // PASSES, (b - 1) // PASSES + 1):
-                widen(i, max(a - PASSES * i, 0), min(b - PASSES * i, PASSES))
+                g0, g1 = max(a - PASSES * i, 0), min(b - PASSES * i, PASSES)
+                if g0 == 0:
+                    values = work.tile([P, SITES], BF16, name="hop_bf", bufs=5)
+                    hop_bf[i] = values
+                k = slice(K_PASS * g0, K_PASS * g1)
+                nc.vector.tensor_tensor(out=hop_bf[i][:, k], in0=hop_raw[i][:, k].bitcast(FP8), in1=scale_bc[:, k], op=MULT)
 
-        def copy_turned(bank, groups, target, copy):
-            copy(
-                out=target.bitcast(F32).rearrange("p l (r u) -> p l r u", u=2),
-                in_=bank[:, 0 : 2 * P * groups].rearrange("p (l u r) -> p l r u", u=2, r=P),
-            )
+        def every_second_word(rows, g):
+            words = rows[:].bitcast(F32)
+            return [words[:, 2 * P * g + u : 2 * P * (g + 1) : 2] for u in range(2)]
 
-        def turn_bank_full(groups, target, copy):
+        def sort_words(a, b):
+            i, g0 = divmod(a, PASSES)
+            halves = work.tile([P, b - a, 2, P], F32, name="sorted_words", bufs=3)
+            words = hop_bf[i][:].bitcast(F32)[:, 2 * P * g0 : 2 * P * (g0 + b - a)]
+            nc.scalar.copy(out=halves[:], in_=words.rearrange("p (g n u) -> p g u n", n=P, u=2))
+            for k in range(a, b):
+                sorted_words[k] = [halves[:, k - a, u, :] for u in range(2)]
+
+        def turn(groups, target, copy):
             bank = ring_bank()
-            for s, (rows, g) in enumerate(groups):
-                words = rows[:].bitcast(F32)
+            for s, halves in enumerate(groups):
                 for u in range(2):
                     col = P * (2 * s + u)
-                    nc.tensor.transpose(bank[:, col : col + P], words[:, 2 * P * g + u : 2 * P * (g + 1) : 2], ident[:])
-            copy_turned(bank, len(groups), target, copy)
+                    nc.tensor.transpose(bank[:, col : col + P], halves[u], ident[:])
+            copy(
+                out=target.bitcast(F32).rearrange("p l (r u) -> p l r u", u=2),
+                in_=bank[:, 0 : 2 * P * len(groups)].rearrange("p (l u r) -> p l r u", u=2, r=P),
+            )
 
         def staged_pair(j):
             if j not in staged:
@@ -178,27 +189,27 @@ def tile_wrap_occupied_green_s11_kernel(tc, hop_bytes, hop_scale, left, right, h
         def staged_half(i):
             return staged_pair(i - i % 2)[:, (SITES + ORB) * (i % 2) : (SITES + ORB) * (i % 2 + 1)]
 
-        def turn_hop(b0, b1, copy=on_scalar):
+        def turn_hop(b0, b1, last_copy=on_scalar):
             for b in range(b0, b1):
-                j = 2 * (b // PASSES)
                 first = ORB + 2 * K_PASS * (b % PASSES)
-                groups = [(hop_bf[k // PASSES], k % PASSES) for k in (2 * b, 2 * b + 1)]
-                turn_bank_full(groups, staged_pair(j)[:, first : first + 2 * K_PASS].rearrange("p (g k) -> p g k", k=K_PASS), copy)
+                target = staged_pair(2 * (b // PASSES))[:, first : first + 2 * K_PASS].rearrange("p (g k) -> p g k", k=K_PASS)
+                groups = [sorted_words[k] if k in sorted_words else every_second_word(hop_bf[k // PASSES], k % PASSES) for k in (2 * b, 2 * b + 1)]
+                turn(groups, target, last_copy if b == b1 - 1 else on_scalar)
 
-        def turn_right(t, copy=on_scalar):
+        def turn_right(t):
             if t % 2 == 0:
                 pair = work.tile([P, PASSES, 2 * K_PASS], BF16, name="right_turned", align_bytes=64)
                 right_turned[t // 2] = pair
             target = right_turned[t // 2][:, :, K_PASS * (t % 2) : K_PASS * (t % 2 + 1)]
             for g0, g1 in ((0, 2), (2, 3)):
-                turn_bank_full([(right_rows[t], g) for g in range(g0, g1)], target[:, g0:g1, :], copy)
+                turn([every_second_word(right_rows[t], g) for g in range(g0, g1)], target[:, g0:g1, :], on_scalar)
 
         def quantize_hop(i):
             codes = work.tile([P, (PASSES + 1) * P], U32, name="hop_codes", align_bytes=64, bufs=4)
             sc = work.tile([P, (PASSES + 1) * P], U8, name="hop_sc", align_bytes=64, bufs=4)
             hop_cols, a_cols = (slice(P, 4 * P), slice(0, P)) if i % 2 == 0 else (slice(0, 3 * P), slice(3 * P, 4 * P))
             first = hop_cols.start
-            joint = A_LAG <= i < TILES - 1
+            joint = A_LAG <= i < ALONE_FROM
             for a, b in ((0, 4 * P),) if joint else ((first, first + 2 * P), (first + 2 * P, first + 3 * P)):
                 nc.vector.quantize_mx(out=codes[:, a:b].bitcast(E4M3X4), scales=sc[:, a:b], in_=staged_half(i)[:, PACK * a : PACK * b])
             hop_codes[i], hop_sc[i] = codes[:, hop_cols], sc[:, hop_cols]
@@ -212,24 +223,18 @@ def tile_wrap_occupied_green_s11_kernel(tc, hop_bytes, hop_scale, left, right, h
 
         left_grouped = {}
 
+        def left_views(g, grouped):
+            left_grouped[g] = grouped
+            return grouped.rearrange("p (t m j) -> p m t j", t=PACK, j=PACK), left_rows[g][:].rearrange("p j (m t) -> p m t j", t=PACK)
+
         def interleave_left(g):
             grouped = work.tile([P, ORB * PACK], BF16, name="left_grouped", align_bytes=64)
-            left_grouped[g] = grouped[:]
-            nc.scalar.copy(
-                out=grouped[:].rearrange("p (t m j) -> p m t j", t=PACK, j=PACK),
-                in_=left_rows[g][:].rearrange("p j (m t) -> p m t j", t=PACK),
-            )
+            target, source = left_views(g, grouped[:])
+            nc.scalar.copy(out=target, in_=source)
 
         def interleave_left_aside(g, grouped):
-            left_grouped[g] = grouped
-            nc.gpsimd.tensor_scalar(
-                out=grouped.rearrange("p (t m j) -> p m t j", t=PACK, j=PACK),
-                in0=left_rows[g][:].rearrange("p j (m t) -> p m t j", t=PACK),
-                scalar1=1.0,
-                scalar2=0.0,
-                op0=MULT,
-                op1=ADD,
-            )
+            target, source = left_views(g, grouped)
+            nc.gpsimd.tensor_scalar(out=target, in0=source, scalar1=1.0, scalar2=0.0, op0=MULT, op1=ADD)
 
         def quantize_left(g):
             nc.vector.quantize_mx(out=left_codes[:, g, :].bitcast(E4M3X4), scales=left_sc[:, g, :], in_=left_grouped[g])
@@ -281,7 +286,7 @@ def tile_wrap_occupied_green_s11_kernel(tc, hop_bytes, hop_scale, left, right, h
                 )
 
         def scale_c_rows(n):
-            rows = work.tile([P, ORB], BF16, name="c_rows", bufs=6)
+            rows = work.tile([P, ORB], BF16, name="c_rows", bufs=TILES - C_ROWS_FROM)
             c_rows[n] = rows
             j = n - C_ROWS_FROM
             nc.scalar.activation(
@@ -291,14 +296,9 @@ def tile_wrap_occupied_green_s11_kernel(tc, hop_bytes, hop_scale, left, right, h
                 scale=winv_cols[:, j : j + 1],
             )
 
-        def turn_c_rows(n0, n1, new_bank=ring_bank):
-            bank = new_bank()
-            for s in range(n1 - n0):
-                words = c_rows[n0 + s][:].bitcast(F32)
-                for u in range(2):
-                    col = P * (2 * s + u)
-                    nc.tensor.transpose(bank[:, col : col + P], words[:, P * u : P * (u + 1)], ident[:])
-            copy_turned(bank, n1 - n0, c_values[:, ORB * n0 : ORB * n1].rearrange("p (s k) -> p s k", k=ORB), on_scalar)
+        def turn_c_rows(n):
+            groups = [[c_rows[j][:].bitcast(F32)[:, P * u : P * (u + 1)] for u in range(2)] for j in (n, n + 1)]
+            turn(groups, c_values[:, ORB * n : ORB * (n + 2)].rearrange("p (s k) -> p s k", k=ORB), on_scalar)
 
         def quantize_c(n0, n1):
             cols = slice(P * n0, P * n1)
@@ -323,8 +323,8 @@ def tile_wrap_occupied_green_s11_kernel(tc, hop_bytes, hop_scale, left, right, h
             empty_slots(a_acc[i], w_bc[:, P * i : P * (i + 1)], a_grouped[i])
 
         def quantize_a(i):
-            codes = work.tile([P, P], U32, name="a_codes", align_bytes=64, bufs=3)
-            sc = work.tile([P, P], U8, name="a_sc", align_bytes=64, bufs=3)
+            codes = work.tile([P, P], U32, name="a_codes", align_bytes=64, bufs=4)
+            sc = work.tile([P, P], U8, name="a_sc", align_bytes=64, bufs=4)
             a_codes[i], a_sc[i] = codes[:], sc[:]
             nc.vector.quantize_mx(out=codes[:].bitcast(E4M3X4), scales=sc[:], in_=a_grouped[i])
 
@@ -347,20 +347,22 @@ def tile_wrap_occupied_green_s11_kernel(tc, hop_bytes, hop_scale, left, right, h
                     stop=True,
                 )
 
-        def empty_out(i, q, copy):
-            copy(out=result[i][:, BANK * q : BANK * (q + 1)], in_=out_banks[i, q][:])
-
-        def store(i, q0, q1):
-            cols = slice(BANK * q0, BANK * q1)
-            nc.sync.dma_start(out=out[P * i : P * (i + 1), cols], in_=result[i][:, cols])
+        def empty_and_store(i, stores, vector_bank=None):
+            for q in range(CHUNKS):
+                copy = on_vector if q == vector_bank else on_scalar
+                copy(out=result[i][:, BANK * q : BANK * (q + 1)], in_=out_banks[i, q][:])
+                for q0, q1 in stores:
+                    if q1 == q + 1:
+                        cols = slice(BANK * q0, BANK * q1)
+                        nc.sync.dma_start(out=out[P * i : P * (i + 1), cols], in_=result[i][:, cols])
 
         with tc.manual_schedule():
             nc.vector.memset(ones[:], 1.0)
             nc.vector.memset(table[:], 0.0)
             nc.vector.memset(field_row[:].bitcast(U32), 0)
             make_identity(nc, ident[:])
-            clear_scales(0, 5)
-            clear_scales(5, TILES)
+            clear_scales(0, HINV_FIRST)
+            clear_scales(HINV_FIRST, TILES)
             nc.scalar.activation(out=table[:], in_=table[:], func=EXP)
 
             nc.sync.dma_start(out=scale_cols[:], in_=hop_scale.rearrange("o (g n q) -> n (o g) q", n=P, q=PACK))
@@ -373,135 +375,135 @@ def tile_wrap_occupied_green_s11_kernel(tc, hop_bytes, hop_scale, left, right, h
             load_right(2)
             load_right(3)
             load_hop(2, 3)
-            load_scales(0, 5)
-            load_hinv(0, 5)
+            load_scales(0, HINV_FIRST)
+            load_hinv(0, HINV_FIRST)
             load_hop(3, 4)
             load_left(0)
             load_left(1)
-            load_scales(5, TILES)
-            load_hinv(5, 8)
+            load_scales(HINV_FIRST, TILES)
+            load_hinv(HINV_FIRST, C_ROWS_FROM)
 
-            spare = sum_bank()
-            warm_up(spare, 3)
             for g in range(PASSES):
                 spread_scale(g, on_vector if g == 0 else on_scalar)
-                widen(0, g, g + 1)
+                widen(g, g + 1)
             turn_right(0)
-            warm_up(spare, 1)
             turn_right(1)
-            field_banks = [spread_field(0, sum_bank())]
-            nc.scalar.activation(out=w_cols[:], in_=field_cols[:], func=EXP)
-            nc.sync.dma_start(out=out[SITES - 1, :].rearrange("(p c) -> p c", c=PARK_COLS), in_=w_cols[:])
+            turn_hop(0, 1)
+            park_w()
             load_left(2)
-            load_hinv(8, TILES)
+            load_hinv(C_ROWS_FROM, TILES)
             load_hop(4, 6)
-            nc.sync.dma_start(out=w_bc[:], in_=out[SITES - 1, :].partition_broadcast(P))
+            spread_w()
             load_hop(6, 9)
             load_hop(9, TILES)
-            widen(1)
+            widen(3, 6)
             quantize_right(0)
             turn_right(2)
-            warm_up(spare, 1)
             turn_right(3)
-            field_banks.append(spread_field(1, sum_bank()))
-            widen(2, 0, 1)
+            field_banks = [spread_field(q) for q in range(P * C_ROWS_FROM // BANK)]
+            widen(6, 7)
             quantize_right(1)
-            exp_winv(0, field_banks[0])
-            turn_hop(0, 2)
-            exp_winv(1, field_banks[1])
             make_winv_cols()
-            widen(2, 1, 3)
+            exp_winv(0, field_banks[0])
+            turn_hop(1, 2)
+            exp_winv(1, field_banks[1])
+            widen(7, 9)
 
             c_banks = (ring_bank, ring_bank, sum_bank, sum_bank, ring_bank)
+
+            def mult_c_slots(n):
+                c_acc[n] = c_banks[n % len(c_banks)]()
+                for t in range(PACK):
+                    mult_c(n, t)
+
             for n in range(2):
                 c_acc[n] = c_banks[n]()
             for t in range(PACK):
                 for n in range(2):
                     mult_c(n, t)
-
-            def c_slots(n):
-                c_acc[n] = c_banks[n % len(c_banks)]()
-                for t in range(PACK):
-                    mult_c(n, t)
-
-            def c_by_rows(n):
-                mult_c_rows(n, c_banks[n % len(c_banks)]())
-                scale_c_rows(n)
-
-            widen(3, 0, 2)
+            widen(9, 11)
             quantize_hop(0)
             interleave_left_aside(1, staged_half(0))
             interleave_left(0)
+            sort_words(6, 9)
             interleave_left(2)
-            for n in range(2, 6):
-                c_slots(n)
-            for n in range(6):
+            for n in range(2, C_IN_A_ROW):
+                mult_c_slots(n)
+            for n in range(C_IN_A_ROW):
                 empty_c(n)
             turn_hop(2, 4)
             quantize_left(0)
             quantize_left(1)
-            widen(3, 2, 3)
-            c_slots(6)
-            c_slots(7)
+            widen(11, 12)
+            mult_c_slots(6)
+            mult_c_slots(7)
             turn_hop(4, 6)
-            quantize_c(0, 4)
             empty_c(6)
-            empty_c(7)
             quantize_left(2)
+            empty_c(7)
+            widen(12, 15)
+            quantize_c(0, C_ROWS_FROM)
             quantize_hop(1)
-            widen(4, 0, 2)
-            quantize_c(4, 8)
-            widen_passes(14, 17)
+            widen(15, 17)
             for n in range(C_ROWS_FROM, TILES):
-                mult_c_rows(n, (sum_bank, ring_bank, ring_bank, ring_bank)[n - C_ROWS_FROM]())
+                mult_c_rows(n, sum_bank() if n == C_ROWS_FROM else ring_bank())
                 scale_c_rows(n)
+                if n == C_ROWS_FROM + 1:
+                    sort_words(12, 14)
             mult_a(0)
-            turn_c_rows(8, 10)
-            turn_c_rows(10, 12)
+            for n in range(C_ROWS_FROM, TILES, 2):
+                turn_c_rows(n)
             turn_hop(6, 7)
+            sort_words(15, 17)
             empty_a(0)
-            widen_passes(17, 18)
+            widen(17, 18)
             quantize_hop(2)
 
-            def empty_and_store(i, stores, on_vector_too=()):
-                for q in range(CHUNKS):
-                    empty_out(i, q, on_vector if q in on_vector_too else on_scalar)
-                    for q0, q1 in stores:
-                        if q1 == q + 1:
-                            store(i, q0, q1)
-
-            whole, split, by_bank = ((0, 3),), ((0, 1), (1, 3)), ((0, 1), (1, 2), (2, 3))
-            TURNED = (7, 7, 9, 9, 11, 13, 15, 15, 17)
-            BEFORE, AFTER = (0, 19, 21, 23, 26, 29, 31, 34, 35), (18, 19, 22, 24, 27, 30, 32, 34, 36)
-            for i in range(1, 9):
+            whole, split = ((0, CHUNKS),), ((0, 1), (1, CHUNKS))
+            widened, turned = 18, 7
+            for i in range(1, ALONE_FROM - A_LAG):
                 mult_a(i)
                 if i == 1:
-                    quantize_c(8, 12)
+                    quantize_c(C_ROWS_FROM, TILES)
                 empty_a(i)
-                if BEFORE[i] > AFTER[i - 1]:
-                    widen_passes(AFTER[i - 1], BEFORE[i])
-                turn_hop(TURNED[i - 1], TURNED[i])
-                quantize_hop(i + 2)
-                if AFTER[i] > BEFORE[i]:
-                    widen_passes(BEFORE[i], AFTER[i])
+                passes = 1 if i == 1 else 2
+                widen(widened, widened + passes)
+                widened = widened + passes
+                runs = 2 * turned < PASSES * (i + A_LAG + 1)
+                if runs:
+                    turn_hop(turned, turned + RUN_BANKS)
+                    turned = turned + RUN_BANKS
+                quantize_hop(i + A_LAG)
+                if runs:
+                    widen(widened, widened + 1)
+                    widened = widened + 1
                 mult_out(i - 1)
-                empty_and_store(i - 1, whole if i - 1 < 7 else split)
+                empty_and_store(i - 1, whole)
+
+            mult_a(8)
+            empty_a(8)
+            widen(widened, HOP_PASSES)
+            quantize_a(8)
+            turn_hop(turned, HOP_BANKS - 1, on_vector)
+            mult_out(7)
+            quantize_hop(10)
+            empty_and_store(7, split)
             mult_a(9)
             empty_a(9)
             mult_out(8)
             quantize_a(9)
             empty_and_store(8, split)
-            turn_hop(17, 18, on_vector)
+            turn_hop(HOP_BANKS - 1, HOP_BANKS, on_vector)
             mult_a(10)
             quantize_hop(11)
             empty_a(10)
             mult_out(9)
             quantize_a(10)
-            empty_and_store(9, by_bank)
+            empty_and_store(9, split, vector_bank=2)
             mult_a(11)
             empty_a(11)
             mult_out(10)
             quantize_a(11)
-            empty_and_store(10, split, (1,))
+            empty_and_store(10, split, vector_bank=1)
             mult_out(11)
-            empty_and_store(11, by_bank, (1,))
+            empty_and_store(11, split, vector_bank=1)

@@ -32,7 +32,7 @@ HOP_BANKS = HOP_PASSES // 2
 A_LAG = 2
 ALONE_FROM = 10
 C_ROWS_FROM = 8
-C_IN_A_ROW = 6
+C_IN_A_ROW = 7
 HINV_FIRST = 5
 RUN_BANKS = 2
 
@@ -401,18 +401,18 @@ def tile_wrap_occupied_green_s11_kernel(tc, hop_bytes, hop_scale, left, right, h
             turn_right(2)
             turn_right(3)
             field_banks = [spread_field(q) for q in range(P * C_ROWS_FROM // BANK)]
-            widen(6, 7)
+            widen(6, 8)
             quantize_right(1)
             make_winv_cols()
             exp_winv(0, field_banks[0])
             turn_hop(1, 2)
             exp_winv(1, field_banks[1])
-            widen(7, 9)
+            widen(8, 9)
 
-            c_banks = (ring_bank, ring_bank, sum_bank, sum_bank, ring_bank)
+            c_banks = {n: sum_bank if n in (2, 3, 7) else ring_bank for n in range(C_ROWS_FROM)}
 
             def mult_c_slots(n):
-                c_acc[n] = c_banks[n % len(c_banks)]()
+                c_acc[n] = c_banks[n]()
                 for t in range(PACK):
                     mult_c(n, t)
 
@@ -421,7 +421,7 @@ def tile_wrap_occupied_green_s11_kernel(tc, hop_bytes, hop_scale, left, right, h
             for t in range(PACK):
                 for n in range(2):
                     mult_c(n, t)
-            widen(9, 11)
+            widen(9, 12)
             quantize_hop(0)
             interleave_left_aside(1, staged_half(0))
             interleave_left(0)
@@ -434,11 +434,8 @@ def tile_wrap_occupied_green_s11_kernel(tc, hop_bytes, hop_scale, left, right, h
             turn_hop(2, 4)
             quantize_left(0)
             quantize_left(1)
-            widen(11, 12)
-            mult_c_slots(6)
             mult_c_slots(7)
             turn_hop(4, 6)
-            empty_c(6)
             quantize_left(2)
             empty_c(7)
             widen(12, 15)

@@ -25,20 +25,20 @@ PASSES = SITES // K_PASS
 TILES = SITES // P
 BANK = 512
 CHUNKS = SITES // BANK
+HOP_BANKS = TILES * PASSES // 2
 
-HOP_PASSES = TILES * PASSES
-HOP_BANKS = HOP_PASSES // 2
-
-A_LAG = 2
-ALONE_FROM = 10
-C_ROWS_FROM = 8
-C_IN_A_ROW = 7
+C_ROWS_FROM = 4
+FIELD_ROWS, FIELD_COLS = 4, 384
 HINV_FIRST = 5
-RUN_BANKS = 2
 
 PARK_ROWS, PARK_COLS = 64, 24
 
 FLOPS = 3 * 2 * SITES * SITES * ORB
+
+
+def bank_passes(b):
+    even = 2 * (b // PASSES)
+    return (((even, 0), (even, 1)), ((even, 2), (even + 1, 2)), ((even + 1, 0), (even + 1, 1)))[b % PASSES]
 
 
 def tile_wrap_occupied_green_s11_kernel(tc, hop_bytes, hop_scale, left, right, hinv_words, hinv_scales, field, out):
@@ -51,16 +51,17 @@ def tile_wrap_occupied_green_s11_kernel(tc, hop_bytes, hop_scale, left, right, h
 
         ident = keep.tile([P, P], F32)
         table = keep.tile([P, 1], F32)
-        ones = keep.tile([P, P], BF16)
-        field_row = keep.tile([P, SITES], BF16)
+        one = keep.tile([P, 1], F32)
+        ident_bf = keep.tile([P, P], BF16)
+        field_rows = keep.tile([P, FIELD_COLS], BF16)
         field_cols = keep.tile([PARK_ROWS, PARK_COLS], BF16)
         w_cols = keep.tile([PARK_ROWS, PARK_COLS], F32)
         scale_cols = keep.tile([P, PASSES, PACK], F32)
-        scale_bc = keep.tile([P, SITES], F32)
         w_bc = keep.tile([P, SITES], F32)
         winv_bc = keep.tile([P, P * C_ROWS_FROM], F32)
-        winv_cols = keep.tile([P, TILES - C_ROWS_FROM], F32)
+        winv_cols = keep.tile([P, TILES], F32)
         c_values = keep.tile([P, TILES * ORB], BF16, align_bytes=64)
+        right_turned = keep.tile([P, PASSES * PACK * K_PASS], BF16, align_bytes=64)
         left_codes = keep.tile([P, PASSES, ORB], U32, align_bytes=64)
         left_sc = keep.tile([P, PASSES, ORB], U8, align_bytes=64)
         right_codes = keep.tile([P, PASSES, ORB], U32, align_bytes=64)
@@ -71,19 +72,16 @@ def tile_wrap_occupied_green_s11_kernel(tc, hop_bytes, hop_scale, left, right, h
         on_scalar = nc.scalar.copy
         on_vector = nc.vector.tensor_copy
 
-        def ring_bank():
-            return psum.tile([P, BANK], F32, name="ring", bufs=6)
-
-        def sum_bank():
-            return psum.tile([P, BANK], F32, name="sums", bufs=2)
+        def psum_bank(k):
+            return psum.tile([P, BANK], F32, name=f"bank{k}")
 
         hop_raw, left_rows, right_rows, hinv_codes, hinv_sc, scale_tiles = {}, {}, {}, {}, {}, {}
 
         def load_hop(i0, i1):
-            rows = keep.tile([P, i1 - i0, SITES], U8, name=f"hop_raw{i0}")
-            nc.sync.dma_start(out=rows[:], in_=hop_bytes[P * i0 : P * i1, :].rearrange("(s p) k -> p s k", p=P))
+            rows = keep.tile([P, (i1 - i0) * SITES], U8, name=f"hop_raw{i0}")
+            nc.sync.dma_start(out=rows[:].rearrange("p (s k) -> p s k", k=SITES), in_=hop_bytes[P * i0 : P * i1, :].rearrange("(s p) k -> p s k", p=P))
             for i in range(i0, i1):
-                hop_raw[i] = rows[:, i - i0, :]
+                hop_raw[i] = (rows, SITES * (i - i0))
 
         def load_left(g):
             rows = keep.tile([P, PACK, ORB], BF16, name=f"left_rows{g}")
@@ -101,9 +99,9 @@ def tile_wrap_occupied_green_s11_kernel(tc, hop_bytes, hop_scale, left, right, h
             for n in range(n0, n1):
                 hinv_codes[n] = words[:, :, 2 * P * (n - n0) : 2 * P * (n - n0 + 1)]
 
-        def clear_scales(n0, n1):
+        def clear_scales(n0, n1, engine):
             sc = keep.tile([P, PASSES, P * (n1 - n0)], U8, name=f"hinv_sc{n0}", align_bytes=64)
-            nc.gpsimd.memset(sc[:].rearrange("p g n -> p (g n)").bitcast(U32), 0)
+            engine.memset(sc[:].rearrange("p g n -> p (g n)").bitcast(U32), 0)
             scale_tiles[n0] = sc
             for n in range(n0, n1):
                 hinv_sc[n] = sc[:, :, P * (n - n0) : P * (n - n0 + 1)]
@@ -115,29 +113,23 @@ def tile_wrap_occupied_green_s11_kernel(tc, hop_bytes, hop_scale, left, right, h
                     in_=hinv_scales[:, 4 * q : 4 * q + 4, P * n0 : P * n1].rearrange("g q n -> q g n").bitcast(I32),
                 )
 
-        def spread_scale(g, copy):
-            bank = ring_bank()
-            for q in range(PACK):
-                nc.tensor.transpose(bank[:, P * q : P * (q + 1)], scale_cols[:, g, q : q + 1].to_broadcast([P, P]), ident[:])
-            copy(
-                out=scale_bc[:, K_PASS * g : K_PASS * (g + 1)].rearrange("p (n q) -> p n q", q=PACK),
-                in_=bank[:].rearrange("p (q n) -> p n q", q=PACK),
+        def spread_field(k0, k1):
+            wide, cols = psum_bank(k0), psum_bank(k1)
+            for c0 in range(0, P * C_ROWS_FROM, FIELD_COLS):
+                j, n = c0 // FIELD_COLS, min(FIELD_COLS, P * C_ROWS_FROM - c0)
+                nc.tensor.matmul(wide[:, c0 : c0 + n], ident_bf[:, j : j + 1].to_broadcast([P, P]), field_rows[:, 0:n], start=True, stop=True)
+            for s in range(FIELD_COLS // P):
+                nc.tensor.matmul(cols[:, P * s : P * (s + 1)], field_rows[:, P * s : P * (s + 1)], ident_bf[:], start=True, stop=True)
+            return wide, cols
+
+        def exp_field(wide, cols):
+            nc.scalar.activation(out=winv_bc[:], in_=wide[:, 0 : P * C_ROWS_FROM], func=EXP, scale=-1.0)
+            nc.scalar.activation(
+                out=winv_cols[:].rearrange("p (j s) -> p s j", j=FIELD_ROWS),
+                in_=cols[:, 0:FIELD_COLS].rearrange("p (s c) -> p s c", c=P)[:, :, 0:FIELD_ROWS],
+                func=EXP,
+                scale=-1.0,
             )
-
-        def spread_field(q):
-            bank = sum_bank()
-            nc.tensor.matmul(bank[:], ones[:], field_row[:, BANK * q : BANK * (q + 1)], start=True, stop=True)
-            return bank
-
-        def exp_winv(q, bank):
-            nc.scalar.activation(out=winv_bc[:, BANK * q : BANK * (q + 1)], in_=bank[:], func=EXP, scale=-1.0)
-
-        def make_winv_cols():
-            bank = ring_bank()
-            for n in range(C_ROWS_FROM, TILES):
-                j = n - C_ROWS_FROM
-                nc.tensor.matmul(bank[:, P * j : P * (j + 1)], field_row[:, P * n : P * (n + 1)], ones[:], start=True, stop=True)
-            nc.scalar.activation(out=winv_cols[:], in_=bank[:, 0 : P * (TILES - C_ROWS_FROM) : P], func=EXP, scale=-1.0)
 
         def park_w():
             nc.scalar.activation(out=w_cols[:], in_=field_cols[:], func=EXP)
@@ -146,100 +138,131 @@ def tile_wrap_occupied_green_s11_kernel(tc, hop_bytes, hop_scale, left, right, h
         def spread_w():
             nc.sync.dma_start(out=w_bc[:], in_=out[SITES - 1, :].partition_broadcast(P))
 
-        hop_bf, sorted_words, staged, right_turned, hop_codes, hop_sc = {}, {}, {}, {}, {}, {}
+        hop_pairs, halves, hop_banks, codes_of = {}, {}, {}, {}
 
-        def widen(a, b):
-            for i in range(a // PASSES, (b - 1) // PASSES + 1):
-                g0, g1 = max(a - PASSES * i, 0), min(b - PASSES * i, PASSES)
-                if g0 == 0:
-                    values = work.tile([P, SITES], BF16, name="hop_bf", bufs=5)
-                    hop_bf[i] = values
-                k = slice(K_PASS * g0, K_PASS * g1)
-                nc.vector.tensor_tensor(out=hop_bf[i][:, k], in0=hop_raw[i][:, k].bitcast(FP8), in1=scale_bc[:, k], op=MULT)
+        def every_second_word(words, first):
+            return [words[:, first + u : first + 2 * P : 2] for u in range(2)]
 
-        def every_second_word(rows, g):
-            words = rows[:].bitcast(F32)
-            return [words[:, 2 * P * g + u : 2 * P * (g + 1) : 2] for u in range(2)]
+        def cast(i0, i1, copy):
+            if i0 // 2 not in hop_pairs:
+                values = work.tile([P, 2 * SITES], BF16, name="hop_pair", bufs=3)
+                hop_pairs[i0 // 2] = values
+            values = hop_pairs[i0 // 2]
+            rows, first = hop_raw[i0]
+            copy(out=values[:, SITES * (i0 % 2) : SITES * (i0 % 2 + i1 - i0)], in_=rows[:, first : first + SITES * (i1 - i0)].bitcast(FP8))
+            for i in range(i0, i1):
+                for g in range(PASSES):
+                    halves[i, g] = every_second_word(values[:].bitcast(F32), 2 * P * (PASSES * (i % 2) + g))
 
-        def sort_words(a, b):
-            i, g0 = divmod(a, PASSES)
-            halves = work.tile([P, b - a, 2, P], F32, name="sorted_words", bufs=3)
-            words = hop_bf[i][:].bitcast(F32)[:, 2 * P * g0 : 2 * P * (g0 + b - a)]
-            nc.scalar.copy(out=halves[:], in_=words.rearrange("p (g n u) -> p g u n", n=P, u=2))
-            for k in range(a, b):
-                sorted_words[k] = [halves[:, k - a, u, :] for u in range(2)]
+        def cast_sorted(i):
+            values = work.tile([P, SITES], BF16, name="hop_sorted", bufs=1)
+            rows, first = hop_raw[i]
+            nc.vector.tensor_scalar(
+                out=values[:].rearrange("p (u n e) -> p n u e", u=2, e=2),
+                in0=rows[:, first : first + SITES].bitcast(FP8).rearrange("p (n u e) -> p n u e", u=2, e=2),
+                scalar1=one[:],
+                scalar2=None,
+                op0=MULT,
+            )
+            for g in range(PASSES):
+                halves[i, g] = [values[:].bitcast(F32)[:, P * (PASSES * u + g) : P * (PASSES * u + g + 1)] for u in range(2)]
 
-        def turn(groups, target, copy):
-            bank = ring_bank()
-            for s, halves in enumerate(groups):
+        def sort_words(b, target, copy):
+            (i0, g0), (i1, g1) = bank_passes(b)
+            first, step = PASSES * (i0 % 2) + g0, PASSES * (i1 - i0) + g1 - g0
+            words = hop_pairs[i0 // 2][:].bitcast(F32).rearrange("p (l n u) -> p l u n", n=P, u=2)[:, first : first + step + 1 : step]
+            target = target.bitcast(F32).rearrange("p (l u n) -> p l u n", n=P, u=2)
+            copy(out=target, in_=words)
+            for s, key in enumerate(bank_passes(b)):
+                halves[key] = [target[:, s, u, :] for u in range(2)]
+
+        def sort_pair(j, target):
+            target = target.bitcast(F32).rearrange("p (l u n) -> p l u n", n=P, u=2)
+            nc.gpsimd.tensor_copy(out=target, in_=hop_pairs[j][:].bitcast(F32).rearrange("p (l n u) -> p l u n", n=P, u=2))
+            for s in range(2 * PASSES):
+                halves[2 * j + s // PASSES, s % PASSES] = [target[:, s, u, :] for u in range(2)]
+
+        def new_sorted():
+            target = work.tile([P, 2 * K_PASS], BF16, name="sorted_words", bufs=4)
+            return target[:]
+
+        def sort_banks(b, target):
+            if b < HOP_BANKS:
+                sort_words(b, target, nc.gpsimd.tensor_copy)
+            if b + 1 < HOP_BANKS:
+                sort_words(b + 1, new_sorted(), nc.gpsimd.tensor_copy)
+
+        def turn(groups, k):
+            bank = psum_bank(k)
+            for s, pair in enumerate(groups):
                 for u in range(2):
-                    col = P * (2 * s + u)
-                    nc.tensor.transpose(bank[:, col : col + P], halves[u], ident[:])
+                    col = P * (len(groups) * u + s)
+                    nc.tensor.transpose(bank[:, col : col + P], pair[u], ident[:])
+            return bank
+
+        def copy_turned(bank, target, copy):
+            n = target.shape[1]
             copy(
                 out=target.bitcast(F32).rearrange("p l (r u) -> p l r u", u=2),
-                in_=bank[:, 0 : 2 * P * len(groups)].rearrange("p (l u r) -> p l r u", u=2, r=P),
+                in_=bank[:, 0 : 2 * P * n].rearrange("p (u l r) -> p l r u", u=2, r=P),
             )
 
-        def staged_pair(j):
-            if j not in staged:
-                both = work.tile([P, 2 * (SITES + ORB)], BF16, name="staged", align_bytes=64, bufs=3)
-                staged[j] = both
-            return staged[j]
+        def turn_hop(b, k):
+            hop_banks[b] = turn([halves[key] for key in bank_passes(b)], k)
 
-        def staged_half(i):
-            return staged_pair(i - i % 2)[:, (SITES + ORB) * (i % 2) : (SITES + ORB) * (i % 2 + 1)]
+        def scale_hop(b, target):
+            (i0, g0), (i1, g1) = bank_passes(b)
+            nc.vector.tensor_tensor(
+                out=target.rearrange("p (l r u e) -> p l r u e", l=2, u=2, e=2),
+                in0=hop_banks[b][:].bitcast(BF16).rearrange("p (u l r e) -> p l r u e", l=2, u=2, e=2),
+                in1=scale_cols[:, g0 : g1 + 1, :].rearrange("p l (u e) -> p l u e", u=2).unsqueeze(2).to_broadcast([P, 2, P, 2, 2]),
+                op=MULT,
+            )
 
-        def turn_hop(b0, b1, last_copy=on_scalar):
-            for b in range(b0, b1):
-                first = ORB + 2 * K_PASS * (b % PASSES)
-                target = staged_pair(2 * (b // PASSES))[:, first : first + 2 * K_PASS].rearrange("p (g k) -> p g k", k=K_PASS)
-                groups = [sorted_words[k] if k in sorted_words else every_second_word(hop_bf[k // PASSES], k % PASSES) for k in (2 * b, 2 * b + 1)]
-                turn(groups, target, last_copy if b == b1 - 1 else on_scalar)
+        def turn_right(items, k):
+            bank = turn([every_second_word(right_rows[t][:].bitcast(F32), 2 * P * g) for t, g in items], k)
+            places = [PACK * g + t for t, g in items]
+            step = max(places[-1] - places[0], 1)
+            copy_turned(bank, right_turned[:].rearrange("p (l k) -> p l k", k=K_PASS)[:, places[0] : places[-1] + 1 : step, :], on_scalar)
 
-        def turn_right(t):
-            if t % 2 == 0:
-                pair = work.tile([P, PASSES, 2 * K_PASS], BF16, name="right_turned", align_bytes=64)
-                right_turned[t // 2] = pair
-            target = right_turned[t // 2][:, :, K_PASS * (t % 2) : K_PASS * (t % 2 + 1)]
-            for g0, g1 in ((0, 2), (2, 3)):
-                turn([every_second_word(right_rows[t], g) for g in range(g0, g1)], target[:, g0:g1, :], on_scalar)
-
-        def quantize_hop(i):
-            codes = work.tile([P, (PASSES + 1) * P], U32, name="hop_codes", align_bytes=64, bufs=4)
-            sc = work.tile([P, (PASSES + 1) * P], U8, name="hop_sc", align_bytes=64, bufs=4)
-            hop_cols, a_cols = (slice(P, 4 * P), slice(0, P)) if i % 2 == 0 else (slice(0, 3 * P), slice(3 * P, 4 * P))
-            first = hop_cols.start
-            joint = A_LAG <= i < ALONE_FROM
-            for a, b in ((0, 4 * P),) if joint else ((first, first + 2 * P), (first + 2 * P, first + 3 * P)):
-                nc.vector.quantize_mx(out=codes[:, a:b].bitcast(E4M3X4), scales=sc[:, a:b], in_=staged_half(i)[:, PACK * a : PACK * b])
-            hop_codes[i], hop_sc[i] = codes[:, hop_cols], sc[:, hop_cols]
-            if joint:
-                a_codes[i - A_LAG], a_sc[i - A_LAG] = codes[:, a_cols], sc[:, a_cols]
-
-        def quantize_right(pair):
-            m = slice(2 * P * pair, 2 * P * (pair + 1))
+        def quantize_right(t0, t1):
             for g in range(PASSES):
-                nc.vector.quantize_mx(out=right_codes[:, g, m].bitcast(E4M3X4), scales=right_sc[:, g, m], in_=right_turned[pair][:, g, :])
+                m = slice(P * t0, P * t1)
+                nc.vector.quantize_mx(
+                    out=right_codes[:, g, m].bitcast(E4M3X4),
+                    scales=right_sc[:, g, m],
+                    in_=right_turned[:, K_PASS * (PACK * g + t0) : K_PASS * (PACK * g + t1)],
+                )
+
+        def new_stage(units):
+            size = len(units)
+            values = work.tile([P, size * K_PASS], BF16, name=f"stage{size}", align_bytes=64, bufs={1: 2, 3: 4, 4: 3, 6: 1}[size])
+            codes = keep.tile([P, size * P], U32, name=f"codes{len(codes_of)}", align_bytes=64)
+            sc = keep.tile([P, size * P], U8, name=f"scales{len(codes_of)}", align_bytes=64)
+            for s, key in enumerate(units):
+                codes_of[key] = (codes[:, P * s : P * (s + 1)], sc[:, P * s : P * (s + 1)])
+            return values, codes, sc
+
+        def units_of(stage, s0, s1):
+            return stage[0][:, K_PASS * s0 : K_PASS * s1]
+
+        def quantize(stage, s0, s1):
+            values, codes, sc = stage
+            nc.vector.quantize_mx(out=codes[:, P * s0 : P * s1].bitcast(E4M3X4), scales=sc[:, P * s0 : P * s1], in_=units_of(stage, s0, s1))
 
         left_grouped = {}
 
-        def left_views(g, grouped):
+        def interleave_left(g, grouped, copy, m=slice(0, P)):
             left_grouped[g] = grouped
-            return grouped.rearrange("p (t m j) -> p m t j", t=PACK, j=PACK), left_rows[g][:].rearrange("p j (m t) -> p m t j", t=PACK)
+            copy(out=grouped.rearrange("p (t m j) -> p m t j", t=PACK, j=PACK)[:, m], in_=left_rows[g][:].rearrange("p j (m t) -> p m t j", t=PACK)[:, m])
 
-        def interleave_left(g):
-            grouped = work.tile([P, ORB * PACK], BF16, name="left_grouped", align_bytes=64)
-            target, source = left_views(g, grouped[:])
-            nc.scalar.copy(out=target, in_=source)
-
-        def interleave_left_aside(g, grouped):
-            target, source = left_views(g, grouped)
-            nc.gpsimd.tensor_scalar(out=target, in0=source, scalar1=1.0, scalar2=0.0, op0=MULT, op1=ADD)
+        def on_gpsimd(out, in_):
+            nc.gpsimd.tensor_scalar(out=out, in0=in_, scalar1=1.0, scalar2=0.0, op0=MULT, op1=ADD)
 
         def quantize_left(g):
             nc.vector.quantize_mx(out=left_codes[:, g, :].bitcast(E4M3X4), scales=left_sc[:, g, :], in_=left_grouped[g])
 
-        c_acc, c_rows, a_acc, a_grouped, a_codes, a_sc = {}, {}, {}, {}, {}, {}
+        c_acc, scaled_rows, a_acc = {}, {}, {}
 
         def slot_product(acc, t, operands):
             for g in range(PASSES):
@@ -272,7 +295,8 @@ def tile_wrap_occupied_green_s11_kernel(tc, hop_bytes, hop_scale, left, right, h
         def empty_c(n):
             empty_slots(c_acc[n], winv_bc[:, P * n : P * (n + 1)], c_values[:, ORB * n : ORB * (n + 1)])
 
-        def mult_c_rows(n, acc):
+        def mult_c_rows(n, k):
+            acc = psum_bank(k)
             c_acc[n] = acc
             for g in range(PASSES):
                 nc.tensor.matmul_mx(
@@ -285,62 +309,53 @@ def tile_wrap_occupied_green_s11_kernel(tc, hop_bytes, hop_scale, left, right, h
                     stop=(g == PASSES - 1),
                 )
 
-        def scale_c_rows(n):
-            rows = work.tile([P, ORB], BF16, name="c_rows", bufs=TILES - C_ROWS_FROM)
-            c_rows[n] = rows
-            j = n - C_ROWS_FROM
+        def scale_rows(key, acc, j):
+            rows = work.tile([P, ORB], BF16, name="rows", bufs=6)
+            scaled_rows[key] = rows
             nc.scalar.activation(
                 out=rows[:].rearrange("p (u m e) -> p u m e", u=2, e=2),
-                in_=c_acc[n][:].rearrange("p (u e m) -> p u m e", u=2, e=2),
+                in_=acc[:].rearrange("p (u e m) -> p u m e", u=2, e=2),
                 func=COPY,
                 scale=winv_cols[:, j : j + 1],
             )
 
-        def turn_c_rows(n):
-            groups = [[c_rows[j][:].bitcast(F32)[:, P * u : P * (u + 1)] for u in range(2)] for j in (n, n + 1)]
-            turn(groups, c_values[:, ORB * n : ORB * (n + 2)].rearrange("p (s k) -> p s k", k=ORB), on_scalar)
+        def turn_rows(keys, target, k):
+            bank = turn([[scaled_rows[key][:].bitcast(F32)[:, P * u : P * (u + 1)] for u in range(2)] for key in keys], k)
+            copy_turned(bank, target.rearrange("p (s k) -> p s k", k=ORB), on_scalar)
+
+        def make_c_rows(n, k):
+            mult_c_rows(n, k)
+            scale_rows(("c", n), c_acc[n], n)
+
+        def turn_c_rows(n0, n1, k):
+            turn_rows([("c", n) for n in range(n0, n1)], c_values[:, ORB * n0 : ORB * n1], k)
 
         def quantize_c(n0, n1):
             cols = slice(P * n0, P * n1)
             nc.vector.quantize_mx(out=c_codes[:, cols].bitcast(E4M3X4), scales=c_sc[:, cols], in_=c_values[:, ORB * n0 : ORB * n1])
 
         def mult_a(i):
-            a_acc[i] = sum_bank()
+            a_acc[i] = psum_bank(i % 2)
             for t in range(PACK):
                 m = slice(P * t, P * (t + 1))
-                slot_product(
-                    a_acc[i],
-                    t,
-                    lambda g: (left_codes[:, g, m], left_sc[:, g, m], hop_codes[i][:, P * g : P * (g + 1)].bitcast(E4M3X4), hop_sc[i][:, P * g : P * (g + 1)]),
-                )
+                slot_product(a_acc[i], t, lambda g: (left_codes[:, g, m], left_sc[:, g, m], codes_of[i, g][0].bitcast(E4M3X4), codes_of[i, g][1]))
 
-        def empty_a(i):
-            if i + A_LAG < TILES:
-                a_grouped[i] = staged_half(i + A_LAG)[:, 0:ORB] if i % 2 == 0 else staged_half(i + A_LAG)[:, SITES:]
-            else:
-                values = work.tile([P, ORB], BF16, name="a_values", align_bytes=64)
-                a_grouped[i] = values[:]
-            empty_slots(a_acc[i], w_bc[:, P * i : P * (i + 1)], a_grouped[i])
-
-        def quantize_a(i):
-            codes = work.tile([P, P], U32, name="a_codes", align_bytes=64, bufs=4)
-            sc = work.tile([P, P], U8, name="a_sc", align_bytes=64, bufs=4)
-            a_codes[i], a_sc[i] = codes[:], sc[:]
-            nc.vector.quantize_mx(out=codes[:].bitcast(E4M3X4), scales=sc[:], in_=a_grouped[i])
+        def empty_a(i, target):
+            empty_slots(a_acc[i], w_bc[:, P * i : P * (i + 1)], target)
 
         out_banks, result = {}, {}
 
         def mult_out(i):
-            rows = work.tile([P, SITES], F32, name="result", bufs=5)
+            rows = work.tile([P, SITES], F32, name="result", bufs=4)
             result[i] = rows
             for q in range(CHUNKS):
                 cols = slice(BANK * q, BANK * (q + 1))
-                bank = ring_bank()
+                bank = psum_bank(4 + (CHUNKS * i + q) % 4)
                 out_banks[i, q] = bank
                 nc.tensor.matmul_mx(
                     out=bank[:],
-                    lhsT=a_codes[i].bitcast(E4M3X4),
-                    lhsT_scale=a_sc[i],
+                    lhsT=codes_of["a", i][0].bitcast(E4M3X4),
+                    lhsT_scale=codes_of["a", i][1],
                     rhs=c_codes[:, cols].bitcast(E4M3X4),
                     rhs_scale=c_sc[:, cols],
                     start=True,
@@ -357,150 +372,160 @@ def tile_wrap_occupied_green_s11_kernel(tc, hop_bytes, hop_scale, left, right, h
                         nc.sync.dma_start(out=out[P * i : P * (i + 1), cols], in_=result[i][:, cols])
 
         with tc.manual_schedule():
-            nc.vector.memset(ones[:], 1.0)
             nc.vector.memset(table[:], 0.0)
-            nc.vector.memset(field_row[:].bitcast(U32), 0)
+            nc.vector.memset(field_rows[:].bitcast(U32), 0)
+            nc.vector.memset(one[:], 1.0)
             make_identity(nc, ident[:])
-            clear_scales(0, HINV_FIRST)
-            clear_scales(HINV_FIRST, TILES)
+            clear_scales(0, HINV_FIRST, nc.vector)
+            clear_scales(HINV_FIRST, TILES, nc.vector)
+            on_vector(out=ident_bf[:], in_=ident[:])
             nc.scalar.activation(out=table[:], in_=table[:], func=EXP)
 
-            nc.sync.dma_start(out=scale_cols[:], in_=hop_scale.rearrange("o (g n q) -> n (o g) q", n=P, q=PACK))
             load_hop(0, 1)
-            load_right(0)
-            nc.sync.dma_start(out=field_cols[:], in_=field.rearrange("(p c) -> p c", c=PARK_COLS))
-            load_right(1)
-            nc.sync.dma_start(out=field_row[0:1, :], in_=field.rearrange("(o k) -> o k", o=1))
             load_hop(1, 2)
-            load_right(2)
-            load_right(3)
-            load_hop(2, 3)
+            nc.sync.dma_start(out=scale_cols[:], in_=hop_scale.rearrange("o (g n q) -> n (o g) q", n=P, q=PACK))
+            load_left(0)
+            for t in range(PACK):
+                load_right(t)
+            nc.sync.dma_start(out=field_rows[0:FIELD_ROWS, :], in_=field.rearrange("(j c) -> j c", c=FIELD_COLS))
             load_scales(0, HINV_FIRST)
             load_hinv(0, HINV_FIRST)
-            load_hop(3, 4)
-            load_left(0)
+            load_hop(2, 4)
+            nc.sync.dma_start(out=field_cols[:], in_=field.rearrange("(p c) -> p c", c=PARK_COLS))
             load_left(1)
-            load_scales(HINV_FIRST, TILES)
-            load_hinv(HINV_FIRST, C_ROWS_FROM)
-
-            for g in range(PASSES):
-                spread_scale(g, on_vector if g == 0 else on_scalar)
-                widen(g, g + 1)
-            turn_right(0)
-            turn_right(1)
-            turn_hop(0, 1)
-            park_w()
-            load_left(2)
-            load_hinv(C_ROWS_FROM, TILES)
             load_hop(4, 6)
-            spread_w()
-            load_hop(6, 9)
-            load_hop(9, TILES)
-            widen(3, 6)
-            quantize_right(0)
-            turn_right(2)
-            turn_right(3)
-            field_banks = [spread_field(q) for q in range(P * C_ROWS_FROM // BANK)]
-            widen(6, 8)
-            quantize_right(1)
-            make_winv_cols()
-            exp_winv(0, field_banks[0])
-            turn_hop(1, 2)
-            exp_winv(1, field_banks[1])
-            widen(8, 9)
+            load_scales(HINV_FIRST, TILES)
+            load_hinv(HINV_FIRST, 9)
+            load_hop(6, 8)
+            load_hinv(9, TILES)
+            load_left(2)
 
-            c_banks = {n: sum_bank if n in (2, 3, 7) else ring_bank for n in range(C_ROWS_FROM)}
-
-            def mult_c_slots(n):
-                c_acc[n] = c_banks[n]()
-                for t in range(PACK):
-                    mult_c(n, t)
-
-            for n in range(2):
-                c_acc[n] = c_banks[n]()
-            for t in range(PACK):
-                for n in range(2):
-                    mult_c(n, t)
-            widen(9, 12)
-            quantize_hop(0)
-            interleave_left_aside(1, staged_half(0))
-            interleave_left(0)
-            sort_words(6, 9)
-            interleave_left(2)
-            for n in range(2, C_IN_A_ROW):
-                mult_c_slots(n)
-            for n in range(C_IN_A_ROW):
-                empty_c(n)
-            turn_hop(2, 4)
+            first = new_stage(bank_passes(0) + bank_passes(1) + bank_passes(2))
+            grouped = work.tile([P, PACK * ORB], BF16, name="left_grouped", align_bytes=64, bufs=1)
+            interleave_left(0, grouped[:], on_gpsimd)
+            cast_sorted(0)
+            cast(1, 2, on_scalar)
+            turn_hop(0, 2)
+            turn_hop(1, 5)
+            turn_hop(2, 6)
+            turn_right([(0, 0), (0, 1)], 0)
+            turn_right([(0, 2)], 1)
+            turn_right([(1, 0), (1, 1)], 3)
+            turn_right([(1, 2)], 4)
+            scale_hop(0, units_of(first, 0, 2))
+            scale_hop(1, units_of(first, 2, 4))
+            scale_hop(2, units_of(first, 4, 6))
+            quantize_right(0, 2)
             quantize_left(0)
+            quantize(first, 0, 4)
+            turn_right([(2, 0), (3, 0)], 7)
+            turn_right([(2, 1), (3, 1)], 0)
+            turn_right([(2, 2), (3, 2)], 2)
+            spread = spread_field(1, 3)
+            quantize_right(2, 4)
+            quantize(first, 4, 6)
+            interleave_left(1, units_of(first, 2, 6), on_gpsimd)
+            cast(2, 3, on_scalar)
+            exp_field(*spread)
+            cast(3, 4, on_scalar)
+            for n in range(C_ROWS_FROM):
+                c_acc[n] = psum_bank((4, 5, 7, 0)[n])
+            for n in range(3):
+                for t in range(2):
+                    mult_c(n, t)
+            second = new_stage(bank_passes(3) + bank_passes(4))
+            turn_hop(3, 6)
+            scale_hop(3, units_of(second, 0, 2))
+            park_w()
+            load_hop(8, 10)
+            load_hop(10, 12)
+            spread_w()
+            sort_words(4, new_sorted(), on_scalar)
+            sort_words(5, new_sorted(), on_scalar)
+            cast(4, 6, on_scalar)
+            sort_words(6, new_sorted(), on_scalar)
+            for n in range(C_ROWS_FROM):
+                for t in range(2 if n < 3 else 0, PACK):
+                    mult_c(n, t)
+            empty_c(0)
+            empty_c(1)
+            turn_hop(4, 2)
+            turn_hop(5, 6)
+            scale_hop(4, units_of(second, 2, 4))
+            make_c_rows(4, 1)
+            make_c_rows(5, 3)
+            cast(6, 8, on_scalar)
             quantize_left(1)
-            mult_c_slots(7)
-            turn_hop(4, 6)
-            quantize_left(2)
-            empty_c(7)
-            widen(12, 15)
-            quantize_c(0, C_ROWS_FROM)
-            quantize_hop(1)
-            widen(15, 17)
-            for n in range(C_ROWS_FROM, TILES):
-                mult_c_rows(n, sum_bank() if n == C_ROWS_FROM else ring_bank())
-                scale_c_rows(n)
-                if n == C_ROWS_FROM + 1:
-                    sort_words(12, 14)
-            mult_a(0)
-            for n in range(C_ROWS_FROM, TILES, 2):
-                turn_c_rows(n)
-            turn_hop(6, 7)
-            sort_words(15, 17)
-            empty_a(0)
-            widen(17, 18)
-            quantize_hop(2)
+            quantize(second, 0, 4)
+            sort_words(7, units_of(second, 0, 2), nc.gpsimd.tensor_copy)
+            sort_words(8, units_of(second, 2, 4), nc.gpsimd.tensor_copy)
+            sort_words(9, new_sorted(), nc.gpsimd.tensor_copy)
+            interleave_left(2, grouped[:], on_gpsimd)
+            empty_c(2)
+            empty_c(3)
+            third = new_stage(bank_passes(5) + bank_passes(6))
+            scale_hop(5, units_of(third, 0, 2))
+            make_c_rows(6, 4)
+            turn_hop(6, 5)
+            turn_c_rows(4, 6, 7)
+            turn_hop(7, 2)
+            scale_hop(6, units_of(third, 2, 4))
+            fourth = new_stage(bank_passes(7) + bank_passes(8))
+            scale_hop(7, units_of(fourth, 0, 2))
+            make_c_rows(7, 0)
+            make_c_rows(8, 1)
+            turn_hop(8, 3)
+            turn_hop(9, 6)
+            turn_c_rows(6, 8, 4)
+            scale_hop(8, units_of(fourth, 2, 4))
+            make_c_rows(9, 7)
+            make_c_rows(10, 5)
+            make_c_rows(11, 2)
+            cast(8, 9, on_scalar)
 
             whole, split = ((0, CHUNKS),), ((0, 1), (1, CHUNKS))
-            widened, turned = 18, 7
-            for i in range(1, ALONE_FROM - A_LAG):
+            lead = 9
+            stage = new_stage(bank_passes(lead) + (("a", 1),))
+            scale_hop(lead, units_of(stage, 0, 2))
+            quantize_left(2)
+            quantize_c(0, 4)
+            quantize_c(4, 8)
+            mult_a(0)
+            turn_c_rows(8, 10, 7)
+            turn_c_rows(10, 12, 4)
+            cast(9, 10, on_scalar)
+            alone = new_stage((("a", 0),))
+            empty_a(0, units_of(alone, 0, 1))
+            quantize(third, 0, 4)
+            quantize(alone, 0, 1)
+            quantize(fourth, 0, 4)
+            quantize_c(8, 12)
+            for i in range(1, TILES):
+                b = i + lead
                 mult_a(i)
                 if i == 1:
-                    quantize_c(C_ROWS_FROM, TILES)
-                empty_a(i)
-                passes = 1 if i == 1 else 2
-                widen(widened, widened + passes)
-                widened = widened + passes
-                runs = 2 * turned < PASSES * (i + A_LAG + 1)
-                if runs:
-                    turn_hop(turned, turned + RUN_BANKS)
-                    turned = turned + RUN_BANKS
-                quantize_hop(i + A_LAG)
-                if runs:
-                    widen(widened, widened + 1)
-                    widened = widened + 1
+                    turn_hop(b, 3)
+                    turn_hop(b + 1, 2)
+                a_unit = 2 if b <= HOP_BANKS else 0
+                empty_a(i, units_of(stage, a_unit, a_unit + 1))
                 mult_out(i - 1)
-                empty_and_store(i - 1, whole)
-
-            mult_a(8)
-            empty_a(8)
-            widen(widened, HOP_PASSES)
-            quantize_a(8)
-            turn_hop(turned, HOP_BANKS - 1, on_vector)
-            mult_out(7)
-            quantize_hop(10)
-            empty_and_store(7, split)
-            mult_a(9)
-            empty_a(9)
-            mult_out(8)
-            quantize_a(9)
-            empty_and_store(8, split)
-            turn_hop(HOP_BANKS - 1, HOP_BANKS, on_vector)
-            mult_a(10)
-            quantize_hop(11)
-            empty_a(10)
-            mult_out(9)
-            quantize_a(10)
-            empty_and_store(9, split, vector_bank=2)
-            mult_a(11)
-            empty_a(11)
-            mult_out(10)
-            quantize_a(11)
-            empty_and_store(10, split, vector_bank=1)
+                if i % 2 == 1 and 1 < i and b < HOP_BANKS:
+                    turn_hop(b, 3)
+                    turn_hop(b + 1, 2)
+                if b < HOP_BANKS:
+                    quantize(stage, 0, 2)
+                quantize(stage, a_unit, a_unit + 1)
+                if b == HOP_BANKS:
+                    quantize(stage, 0, 2)
+                if b + 2 < HOP_BANKS:
+                    sort_words(b + 2, units_of(stage, 1, 3), nc.gpsimd.tensor_copy)
+                if b < HOP_BANKS:
+                    stage = new_stage(bank_passes(b) + (("a", i + 1),))
+                    scale_hop(b, units_of(stage, 0, 2))
+                elif i + 1 < TILES:
+                    stage = new_stage((("a", i + 1),))
+                empty_and_store(i - 1, whole if i < 7 else split, vector_bank={10: 2, 11: 1}.get(i))
+                if i in (2, 4):
+                    cast(9 + i // 2, 10 + i // 2, on_scalar)
             mult_out(11)
             empty_and_store(11, split, vector_bank=1)

@@ -14,7 +14,6 @@ FP8 = mybir.dt.float8_e4m3fn
 E4M3X4 = mybir.dt.float8_e4m3fn_x4
 E2M1X4 = mybir.dt.float4_e2m1fn_x4
 MULT = mybir.AluOpType.mult
-ADD = mybir.AluOpType.add
 EXP = mybir.ActivationFunctionType.Exp
 COPY = mybir.ActivationFunctionType.Copy
 
@@ -252,12 +251,12 @@ def tile_wrap_occupied_green_s11_kernel(tc, hop_bytes, hop_scale, left, right, h
 
         left_grouped = {}
 
-        def interleave_left(g, grouped, copy, m=slice(0, P)):
+        def interleave_left(g, grouped):
             left_grouped[g] = grouped
-            copy(out=grouped.rearrange("p (t m j) -> p m t j", t=PACK, j=PACK)[:, m], in_=left_rows[g][:].rearrange("p j (m t) -> p m t j", t=PACK)[:, m])
-
-        def on_gpsimd(out, in_):
-            nc.gpsimd.tensor_scalar(out=out, in0=in_, scalar1=1.0, scalar2=0.0, op0=MULT, op1=ADD)
+            nc.gpsimd.tensor_copy(
+                out=grouped.rearrange("p (t h l j) -> p h t l j", t=PACK, l=2, j=PACK),
+                in_=left_rows[g][:].rearrange("p j (h l t) -> p h t l j", l=2, t=PACK),
+            )
 
         def quantize_left(g):
             nc.vector.quantize_mx(out=left_codes[:, g, :].bitcast(E4M3X4), scales=left_sc[:, g, :], in_=left_grouped[g])
@@ -384,13 +383,14 @@ def tile_wrap_occupied_green_s11_kernel(tc, hop_bytes, hop_scale, left, right, h
             load_hop(0, 1)
             load_hop(1, 2)
             nc.sync.dma_start(out=scale_cols[:], in_=hop_scale.rearrange("o (g n q) -> n (o g) q", n=P, q=PACK))
+            load_hop(2, 3)
             load_left(0)
             for t in range(PACK):
                 load_right(t)
             nc.sync.dma_start(out=field_rows[0:FIELD_ROWS, :], in_=field.rearrange("(j c) -> j c", c=FIELD_COLS))
             load_scales(0, HINV_FIRST)
             load_hinv(0, HINV_FIRST)
-            load_hop(2, 4)
+            load_hop(3, 4)
             nc.sync.dma_start(out=field_cols[:], in_=field.rearrange("(p c) -> p c", c=PARK_COLS))
             load_left(1)
             load_hop(4, 6)
@@ -401,13 +401,16 @@ def tile_wrap_occupied_green_s11_kernel(tc, hop_bytes, hop_scale, left, right, h
             load_left(2)
 
             first = new_stage(bank_passes(0) + bank_passes(1) + bank_passes(2))
+            second = new_stage(bank_passes(3) + bank_passes(4))
             grouped = work.tile([P, PACK * ORB], BF16, name="left_grouped", align_bytes=64, bufs=1)
-            interleave_left(0, grouped[:], on_gpsimd)
+            interleave_left(0, grouped[:])
             cast_sorted(0)
             cast(1, 2, on_scalar)
+            cast(2, 3, on_scalar)
             turn_hop(0, 2)
             turn_hop(1, 5)
             turn_hop(2, 6)
+            turn_hop(3, 7)
             turn_right([(0, 0), (0, 1)], 0)
             turn_right([(0, 2)], 1)
             turn_right([(1, 0), (1, 1)], 3)
@@ -415,27 +418,24 @@ def tile_wrap_occupied_green_s11_kernel(tc, hop_bytes, hop_scale, left, right, h
             scale_hop(0, units_of(first, 0, 2))
             scale_hop(1, units_of(first, 2, 4))
             scale_hop(2, units_of(first, 4, 6))
+            scale_hop(3, units_of(second, 0, 2))
             quantize_right(0, 2)
             quantize_left(0)
             quantize(first, 0, 4)
-            turn_right([(2, 0), (3, 0)], 7)
+            turn_right([(2, 0), (3, 0)], 2)
             turn_right([(2, 1), (3, 1)], 0)
-            turn_right([(2, 2), (3, 2)], 2)
+            turn_right([(2, 2), (3, 2)], 5)
             spread = spread_field(1, 3)
             quantize_right(2, 4)
             quantize(first, 4, 6)
-            interleave_left(1, units_of(first, 2, 6), on_gpsimd)
-            cast(2, 3, on_scalar)
-            exp_field(*spread)
+            interleave_left(1, units_of(first, 2, 6))
             cast(3, 4, on_scalar)
+            exp_field(*spread)
             for n in range(C_ROWS_FROM):
-                c_acc[n] = psum_bank((4, 5, 7, 0)[n])
-            for n in range(3):
+                c_acc[n] = psum_bank((4, 6, 7, 2)[n])
+            for n in range(C_ROWS_FROM):
                 for t in range(2):
                     mult_c(n, t)
-            second = new_stage(bank_passes(3) + bank_passes(4))
-            turn_hop(3, 6)
-            scale_hop(3, units_of(second, 0, 2))
             park_w()
             load_hop(8, 10)
             load_hop(10, 12)
@@ -444,42 +444,44 @@ def tile_wrap_occupied_green_s11_kernel(tc, hop_bytes, hop_scale, left, right, h
             sort_words(5, new_sorted(), on_scalar)
             cast(4, 6, on_scalar)
             sort_words(6, new_sorted(), on_scalar)
-            for n in range(C_ROWS_FROM):
-                for t in range(2 if n < 3 else 0, PACK):
+            sort_words(7, new_sorted(), on_scalar)
+            for n in range(2):
+                for t in range(2, PACK):
+                    mult_c(n, t)
+            turn_hop(4, 0)
+            turn_hop(5, 5)
+            for n in range(2, C_ROWS_FROM):
+                for t in range(2, PACK):
                     mult_c(n, t)
             empty_c(0)
             empty_c(1)
-            turn_hop(4, 2)
-            turn_hop(5, 6)
             scale_hop(4, units_of(second, 2, 4))
+            empty_c(2)
+            empty_c(3)
             make_c_rows(4, 1)
             make_c_rows(5, 3)
             cast(6, 8, on_scalar)
             quantize_left(1)
             quantize(second, 0, 4)
-            sort_words(7, units_of(second, 0, 2), nc.gpsimd.tensor_copy)
             sort_words(8, units_of(second, 2, 4), nc.gpsimd.tensor_copy)
-            sort_words(9, new_sorted(), nc.gpsimd.tensor_copy)
-            interleave_left(2, grouped[:], on_gpsimd)
-            empty_c(2)
-            empty_c(3)
+            interleave_left(2, grouped[:])
             third = new_stage(bank_passes(5) + bank_passes(6))
             scale_hop(5, units_of(third, 0, 2))
             make_c_rows(6, 4)
-            turn_hop(6, 5)
+            turn_hop(6, 6)
             turn_c_rows(4, 6, 7)
-            turn_hop(7, 2)
+            turn_hop(7, 0)
             scale_hop(6, units_of(third, 2, 4))
             fourth = new_stage(bank_passes(7) + bank_passes(8))
             scale_hop(7, units_of(fourth, 0, 2))
-            make_c_rows(7, 0)
+            make_c_rows(7, 2)
             make_c_rows(8, 1)
             turn_hop(8, 3)
-            turn_hop(9, 6)
+            turn_hop(9, 5)
             turn_c_rows(6, 8, 4)
             scale_hop(8, units_of(fourth, 2, 4))
             make_c_rows(9, 7)
-            make_c_rows(10, 5)
+            make_c_rows(10, 6)
             make_c_rows(11, 2)
             cast(8, 9, on_scalar)
 
@@ -524,7 +526,7 @@ def tile_wrap_occupied_green_s11_kernel(tc, hop_bytes, hop_scale, left, right, h
                     scale_hop(b, units_of(stage, 0, 2))
                 elif i + 1 < TILES:
                     stage = new_stage((("a", i + 1),))
-                empty_and_store(i - 1, whole if i < 7 else split, vector_bank={10: 2, 11: 1}.get(i))
+                empty_and_store(i - 1, whole if i < 5 else split, vector_bank={10: 2, 11: 1}.get(i))
                 if i in (2, 4):
                     cast(9 + i // 2, 10 + i // 2, on_scalar)
             mult_out(11)

@@ -130,6 +130,10 @@ def tile_wrap_occupied_green_s11_kernel(tc, hop_bytes, hop_scale, left, right, h
                 scale=-1.0,
             )
 
+        def warm_up(k):
+            bank = psum_bank(k)
+            nc.tensor.matmul(bank[:], ident_bf[:], right_rows[0][:, 0:BANK], start=True, stop=True)
+
         def park_w():
             nc.scalar.activation(out=w_cols[:], in_=field_cols[:], func=EXP)
             nc.sync.dma_start(out=out[SITES - 1, :].rearrange("(p c) -> p c", c=PARK_COLS), in_=w_cols[:])
@@ -142,29 +146,31 @@ def tile_wrap_occupied_green_s11_kernel(tc, hop_bytes, hop_scale, left, right, h
         def every_second_word(words, first):
             return [words[:, first + u : first + 2 * P : 2] for u in range(2)]
 
-        def cast(i0, i1, copy):
-            if i0 // 2 not in hop_pairs:
+        def cast(k0, k1):
+            pair = k0 // (2 * PASSES)
+            if pair not in hop_pairs:
                 values = work.tile([P, 2 * SITES], BF16, name="hop_pair", bufs=3)
-                hop_pairs[i0 // 2] = values
-            values = hop_pairs[i0 // 2]
-            rows, first = hop_raw[i0]
-            copy(out=values[:, SITES * (i0 % 2) : SITES * (i0 % 2 + i1 - i0)], in_=rows[:, first : first + SITES * (i1 - i0)].bitcast(FP8))
-            for i in range(i0, i1):
-                for g in range(PASSES):
-                    halves[i, g] = every_second_word(values[:].bitcast(F32), 2 * P * (PASSES * (i % 2) + g))
+                hop_pairs[pair] = values
+            values = hop_pairs[pair]
+            rows, first = hop_raw[k0 // PASSES]
+            first = first + K_PASS * (k0 % PASSES)
+            target = K_PASS * (k0 % (2 * PASSES))
+            width = K_PASS * (k1 - k0)
+            on_scalar(out=values[:, target : target + width], in_=rows[:, first : first + width].bitcast(FP8))
+            for k in range(k0, k1):
+                halves[divmod(k, PASSES)] = every_second_word(values[:].bitcast(F32), 2 * P * (k % (2 * PASSES)))
 
-        def cast_sorted(i):
-            values = work.tile([P, SITES], BF16, name="hop_sorted", bufs=1)
-            rows, first = hop_raw[i]
+        def cast_first_bank():
+            values = keep.tile([P, 2 * K_PASS], BF16)
             nc.vector.tensor_scalar(
                 out=values[:].rearrange("p (u n e) -> p n u e", u=2, e=2),
-                in0=rows[:, first : first + SITES].bitcast(FP8).rearrange("p (n u e) -> p n u e", u=2, e=2),
+                in0=hop_raw[0][0][:, 0 : 2 * K_PASS].bitcast(FP8).rearrange("p (n u e) -> p n u e", u=2, e=2),
                 scalar1=one[:],
                 scalar2=None,
                 op0=MULT,
             )
-            for g in range(PASSES):
-                halves[i, g] = [values[:].bitcast(F32)[:, P * (PASSES * u + g) : P * (PASSES * u + g + 1)] for u in range(2)]
+            for g in range(2):
+                halves[0, g] = [values[:].bitcast(F32)[:, P * (2 * u + g) : P * (2 * u + g + 1)] for u in range(2)]
 
         def sort_words(b, target, copy):
             (i0, g0), (i1, g1) = bank_passes(b)
@@ -175,21 +181,9 @@ def tile_wrap_occupied_green_s11_kernel(tc, hop_bytes, hop_scale, left, right, h
             for s, key in enumerate(bank_passes(b)):
                 halves[key] = [target[:, s, u, :] for u in range(2)]
 
-        def sort_pair(j, target):
-            target = target.bitcast(F32).rearrange("p (l u n) -> p l u n", n=P, u=2)
-            nc.gpsimd.tensor_copy(out=target, in_=hop_pairs[j][:].bitcast(F32).rearrange("p (l n u) -> p l u n", n=P, u=2))
-            for s in range(2 * PASSES):
-                halves[2 * j + s // PASSES, s % PASSES] = [target[:, s, u, :] for u in range(2)]
-
         def new_sorted():
             target = work.tile([P, 2 * K_PASS], BF16, name="sorted_words", bufs=4)
             return target[:]
-
-        def sort_banks(b, target):
-            if b < HOP_BANKS:
-                sort_words(b, target, nc.gpsimd.tensor_copy)
-            if b + 1 < HOP_BANKS:
-                sort_words(b + 1, new_sorted(), nc.gpsimd.tensor_copy)
 
         def turn(groups, k):
             bank = psum_bank(k)
@@ -371,13 +365,14 @@ def tile_wrap_occupied_green_s11_kernel(tc, hop_bytes, hop_scale, left, right, h
                         nc.sync.dma_start(out=out[P * i : P * (i + 1), cols], in_=result[i][:, cols])
 
         with tc.manual_schedule():
-            nc.vector.memset(table[:], 0.0)
             nc.vector.memset(field_rows[:].bitcast(U32), 0)
+            nc.vector.memset(table[:], 0.0)
             nc.vector.memset(one[:], 1.0)
             make_identity(nc, ident[:])
             clear_scales(0, HINV_FIRST, nc.vector)
-            clear_scales(HINV_FIRST, TILES, nc.vector)
             on_vector(out=ident_bf[:], in_=ident[:])
+            clear_scales(HINV_FIRST, TILES, nc.vector)
+            nc.scalar.dma_start(out=field_rows[0:FIELD_ROWS, :], in_=field.rearrange("(j c) -> j c", c=FIELD_COLS))
             nc.scalar.activation(out=table[:], in_=table[:], func=EXP)
 
             load_hop(0, 1)
@@ -387,7 +382,6 @@ def tile_wrap_occupied_green_s11_kernel(tc, hop_bytes, hop_scale, left, right, h
             load_left(0)
             for t in range(PACK):
                 load_right(t)
-            nc.sync.dma_start(out=field_rows[0:FIELD_ROWS, :], in_=field.rearrange("(j c) -> j c", c=FIELD_COLS))
             load_scales(0, HINV_FIRST)
             load_hinv(0, HINV_FIRST)
             load_hop(3, 4)
@@ -397,16 +391,18 @@ def tile_wrap_occupied_green_s11_kernel(tc, hop_bytes, hop_scale, left, right, h
             load_scales(HINV_FIRST, TILES)
             load_hinv(HINV_FIRST, 9)
             load_hop(6, 8)
-            load_hinv(9, TILES)
             load_left(2)
+            load_hinv(9, TILES)
 
             first = new_stage(bank_passes(0) + bank_passes(1) + bank_passes(2))
             second = new_stage(bank_passes(3) + bank_passes(4))
             grouped = work.tile([P, PACK * ORB], BF16, name="left_grouped", align_bytes=64, bufs=1)
             interleave_left(0, grouped[:])
-            cast_sorted(0)
-            cast(1, 2, on_scalar)
-            cast(2, 3, on_scalar)
+            cast_first_bank()
+            cast(2, 3)
+            cast(3, 6)
+            cast(6, 9)
+            exp_field(*spread_field(0, 1))
             turn_hop(0, 2)
             turn_hop(1, 5)
             turn_hop(2, 6)
@@ -422,15 +418,15 @@ def tile_wrap_occupied_green_s11_kernel(tc, hop_bytes, hop_scale, left, right, h
             quantize_right(0, 2)
             quantize_left(0)
             quantize(first, 0, 4)
+            warm_up(2)
             turn_right([(2, 0), (3, 0)], 2)
             turn_right([(2, 1), (3, 1)], 0)
             turn_right([(2, 2), (3, 2)], 5)
-            spread = spread_field(1, 3)
+            warm_up(1)
             quantize_right(2, 4)
             quantize(first, 4, 6)
             interleave_left(1, units_of(first, 2, 6))
-            cast(3, 4, on_scalar)
-            exp_field(*spread)
+            cast(9, 12)
             for n in range(C_ROWS_FROM):
                 c_acc[n] = psum_bank((4, 6, 7, 2)[n])
             for n in range(C_ROWS_FROM):
@@ -442,7 +438,7 @@ def tile_wrap_occupied_green_s11_kernel(tc, hop_bytes, hop_scale, left, right, h
             spread_w()
             sort_words(4, new_sorted(), on_scalar)
             sort_words(5, new_sorted(), on_scalar)
-            cast(4, 6, on_scalar)
+            cast(12, 18)
             sort_words(6, new_sorted(), on_scalar)
             sort_words(7, new_sorted(), on_scalar)
             for n in range(2):
@@ -460,7 +456,7 @@ def tile_wrap_occupied_green_s11_kernel(tc, hop_bytes, hop_scale, left, right, h
             empty_c(3)
             make_c_rows(4, 1)
             make_c_rows(5, 3)
-            cast(6, 8, on_scalar)
+            cast(18, 24)
             quantize_left(1)
             quantize(second, 0, 4)
             sort_words(8, units_of(second, 2, 4), nc.gpsimd.tensor_copy)
@@ -483,9 +479,9 @@ def tile_wrap_occupied_green_s11_kernel(tc, hop_bytes, hop_scale, left, right, h
             make_c_rows(9, 7)
             make_c_rows(10, 6)
             make_c_rows(11, 2)
-            cast(8, 9, on_scalar)
+            cast(24, 27)
 
-            whole, split = ((0, CHUNKS),), ((0, 1), (1, CHUNKS))
+            whole, split, by_bank = ((0, CHUNKS),), ((0, 1), (1, CHUNKS)), ((0, 1), (1, 2), (2, CHUNKS))
             lead = 9
             stage = new_stage(bank_passes(lead) + (("a", 1),))
             scale_hop(lead, units_of(stage, 0, 2))
@@ -495,7 +491,7 @@ def tile_wrap_occupied_green_s11_kernel(tc, hop_bytes, hop_scale, left, right, h
             mult_a(0)
             turn_c_rows(8, 10, 7)
             turn_c_rows(10, 12, 4)
-            cast(9, 10, on_scalar)
+            cast(27, 30)
             alone = new_stage((("a", 0),))
             empty_a(0, units_of(alone, 0, 1))
             quantize(third, 0, 4)
@@ -526,8 +522,8 @@ def tile_wrap_occupied_green_s11_kernel(tc, hop_bytes, hop_scale, left, right, h
                     scale_hop(b, units_of(stage, 0, 2))
                 elif i + 1 < TILES:
                     stage = new_stage((("a", i + 1),))
-                empty_and_store(i - 1, whole if i < 5 else split, vector_bank={10: 2, 11: 1}.get(i))
+                empty_and_store(i - 1, whole if i < 5 else by_bank if i in (8, 9) else split, vector_bank={10: 2, 11: 1}.get(i))
                 if i in (2, 4):
-                    cast(9 + i // 2, 10 + i // 2, on_scalar)
+                    cast(PASSES * (9 + i // 2), PASSES * (10 + i // 2))
             mult_out(11)
             empty_and_store(11, split, vector_bank=1)

@@ -522,8 +522,8 @@ def tile_wrap_occupied_green_s11_kernel(tc, hop_bytes, hop_scale, left, right, h
                     scale_hop(b, units_of(stage, 0, 2))
                 elif i + 1 < TILES:
                     stage = new_stage((("a", i + 1),))
-                empty_and_store(i - 1, whole if i < 5 else by_bank if i in (8, 9) else split, vector_bank={10: 2, 11: 1}.get(i))
+                empty_and_store(i - 1, whole if i < 5 or i > 9 else split, vector_bank={10: 2, 11: 1}.get(i))
                 if i in (2, 4):
                     cast(PASSES * (9 + i // 2), PASSES * (10 + i // 2))
             mult_out(11)
-            empty_and_store(11, split, vector_bank=1)
+            empty_and_store(11, whole, vector_bank=1)

@@ -476,7 +476,9 @@ def tile_wrap_occupied_green_s11_kernel(tc, hop_bytes, hop_scale, left, right, h
             turn_hop(9, 5)
             turn_c_rows(6, 8, 4)
             scale_hop(8, units_of(fourth, 2, 4))
+            sort_words(10, new_sorted(), on_scalar)
             make_c_rows(9, 7)
+            sort_words(11, new_sorted(), on_scalar)
             make_c_rows(10, 6)
             make_c_rows(11, 2)
             cast(24, 27)
@@ -491,19 +493,19 @@ def tile_wrap_occupied_green_s11_kernel(tc, hop_bytes, hop_scale, left, right, h
             mult_a(0)
             turn_c_rows(8, 10, 7)
             turn_c_rows(10, 12, 4)
+            turn_hop(lead + 1, 3)
+            turn_hop(lead + 2, 2)
             cast(27, 30)
             alone = new_stage((("a", 0),))
-            empty_a(0, units_of(alone, 0, 1))
             quantize(third, 0, 4)
-            quantize(alone, 0, 1)
+            empty_a(0, units_of(alone, 0, 1))
             quantize(fourth, 0, 4)
-            quantize_c(8, 12)
+            quantize(alone, 0, 1)
+            quantize_c(8, 10)
+            quantize_c(10, 12)
             for i in range(1, TILES):
                 b = i + lead
                 mult_a(i)
-                if i == 1:
-                    turn_hop(b, 3)
-                    turn_hop(b + 1, 2)
                 a_unit = 2 if b <= HOP_BANKS else 0
                 empty_a(i, units_of(stage, a_unit, a_unit + 1))
                 mult_out(i - 1)

@@ -130,10 +130,6 @@ def tile_wrap_occupied_green_s11_kernel(tc, hop_bytes, hop_scale, left, right, h
                 scale=-1.0,
             )
 
-        def warm_up(k):
-            bank = psum_bank(k)
-            nc.tensor.matmul(bank[:], ident_bf[:], right_rows[0][:, 0:BANK], start=True, stop=True)
-
         def park_w():
             nc.scalar.activation(out=w_cols[:], in_=field_cols[:], func=EXP)
             nc.sync.dma_start(out=out[SITES - 1, :].rearrange("(p c) -> p c", c=PARK_COLS), in_=w_cols[:])
@@ -418,11 +414,9 @@ def tile_wrap_occupied_green_s11_kernel(tc, hop_bytes, hop_scale, left, right, h
             quantize_right(0, 2)
             quantize_left(0)
             quantize(first, 0, 4)
-            warm_up(2)
             turn_right([(2, 0), (3, 0)], 2)
             turn_right([(2, 1), (3, 1)], 0)
             turn_right([(2, 2), (3, 2)], 5)
-            warm_up(1)
             quantize_right(2, 4)
             quantize(first, 4, 6)
             interleave_left(1, units_of(first, 2, 6))

from contextlib import ExitStack

import concourse.mybir as mybir
from concourse.masks import make_identity

SITES, ORB = 1536, 512

F32 = mybir.dt.float32
BF16 = mybir.dt.bfloat16
U32 = mybir.dt.uint32
I32 = mybir.dt.int32
U8 = mybir.dt.uint8
FP8 = mybir.dt.float8_e4m3fn
E4M3X4 = mybir.dt.float8_e4m3fn_x4
E2M1X4 = mybir.dt.float4_e2m1fn_x4
MULT = mybir.AluOpType.mult
EXP = mybir.ActivationFunctionType.Exp
COPY = mybir.ActivationFunctionType.Copy

P = 128
PACK = 4
K_PASS = P * PACK
PASSES = SITES // K_PASS
TILES = SITES // P
BANK = 512
CHUNKS = SITES // BANK
HOP_BANKS = TILES * PASSES // 2

C_ROWS_FROM = 4
FIELD_ROWS, FIELD_COLS = 4, 384
HINV_FIRST = 5

PARK_ROWS, PARK_COLS = 64, 24

FLOPS = 3 * 2 * SITES * SITES * ORB


def bank_passes(b):
    even = 2 * (b // PASSES)
    return (((even, 0), (even, 1)), ((even, 2), (even + 1, 2)), ((even + 1, 0), (even + 1, 1)))[b % PASSES]


def tile_wrap_occupied_green_s11_kernel(tc, hop_bytes, hop_scale, left, right, hinv_words, hinv_scales, field, out):
    nc = tc.nc

    with ExitStack() as ctx:
        keep = ctx.enter_context(tc.tile_pool(name="keep", bufs=1))
        work = ctx.enter_context(tc.tile_pool(name="work", bufs=2))
        psum = ctx.enter_context(tc.psum_pool(name="psum", bufs=1))

        ident = keep.tile([P, P], F32)
        table = keep.tile([P, 1], F32)
        one = keep.tile([P, 1], F32)
        ident_bf = keep.tile([P, P], BF16)
        field_rows = keep.tile([P, FIELD_COLS], BF16)
        field_cols = keep.tile([PARK_ROWS, PARK_COLS], BF16)
        w_cols = keep.tile([PARK_ROWS, PARK_COLS], F32)
        scale_cols = keep.tile([P, PASSES, PACK], F32)
        w_bc = keep.tile([P, SITES], F32)
        winv_bc = keep.tile([P, P * C_ROWS_FROM], F32)
        winv_cols = keep.tile([P, TILES], F32)
        c_values = keep.tile([P, TILES * ORB], BF16, align_bytes=64)
        right_turned = keep.tile([P, PASSES * PACK * K_PASS], BF16, align_bytes=64)
        left_codes = keep.tile([P, PASSES, ORB], U32, align_bytes=64)
        left_sc = keep.tile([P, PASSES, ORB], U8, align_bytes=64)
        right_codes = keep.tile([P, PASSES, ORB], U32, align_bytes=64)
        right_sc = keep.tile([P, PASSES, ORB], U8, align_bytes=64)
        c_codes = keep.tile([P, SITES], U32, align_bytes=64)
        c_sc = keep.tile([P, SITES], U8, align_bytes=64)

        on_scalar = nc.scalar.copy
        on_vector = nc.vector.tensor_copy

        def psum_bank(k):
            return psum.tile([P, BANK], F32, name=f"bank{k}")

        hop_raw, left_rows, right_rows, hinv_codes, hinv_sc, scale_tiles = {}, {}, {}, {}, {}, {}

        def load_hop(i0, i1):
            rows = keep.tile([P, (i1 - i0) * SITES], U8, name=f"hop_raw{i0}")
            nc.sync.dma_start(out=rows[:].rearrange("p (s k) -> p s k", k=SITES), in_=hop_bytes[P * i0 : P * i1, :].rearrange("(s p) k -> p s k", p=P))
            for i in range(i0, i1):
                hop_raw[i] = (rows, SITES * (i - i0))

        def load_left(g):
            rows = keep.tile([P, PACK, ORB], BF16, name=f"left_rows{g}")
            nc.sync.dma_start(out=rows[:], in_=left.rearrange("(g p j) r -> g p j r", p=P, j=PACK)[g])
            left_rows[g] = rows

        def load_right(t):
            rows = keep.tile([P, SITES], BF16, name=f"right_rows{t}")
            nc.sync.dma_start(out=rows[:], in_=right.rearrange("(m t) k -> t m k", t=PACK)[t])
            right_rows[t] = rows

        def load_hinv(n0, n1):
            words = keep.tile([P, PASSES, 2 * P * (n1 - n0)], U8, name=f"hinv_codes{n0}", align_bytes=64)
            nc.sync.dma_start(out=words[:], in_=hinv_words[:, :, 2 * P * n0 : 2 * P * n1].rearrange("g p n -> p g n"))
            for n in range(n0, n1):
                hinv_codes[n] = words[:, :, 2 * P * (n - n0) : 2 * P * (n - n0 + 1)]

        def clear_scales(n0, n1, engine):
            sc = keep.tile([P, PASSES, P * (n1 - n0)], U8, name=f"hinv_sc{n0}", align_bytes=64)
            engine.memset(sc[:].rearrange("p g n -> p (g n)").bitcast(U32), 0)
            scale_tiles[n0] = sc
            for n in range(n0, n1):
                hinv_sc[n] = sc[:, :, P * (n - n0) : P * (n - n0 + 1)]

        def load_scales(n0, n1):
            for q in range(4):
                nc.sync.dma_start(
                    out=scale_tiles[n0][32 * q : 32 * q + 4, :, :].bitcast(I32),
                    in_=hinv_scales[:, 4 * q : 4 * q + 4, P * n0 : P * n1].rearrange("g q n -> q g n").bitcast(I32),
                )

        def spread_field(k0, k1):
            wide, cols = psum_bank(k0), psum_bank(k1)
            for c0 in range(0, P * C_ROWS_FROM, FIELD_COLS):
                j, n = c0 // FIELD_COLS, min(FIELD_COLS, P * C_ROWS_FROM - c0)
                nc.tensor.matmul(wide[:, c0 : c0 + n], ident_bf[:, j : j + 1].to_broadcast([P, P]), field_rows[:, 0:n], start=True, stop=True)
            for s in range(FIELD_COLS // P):
                nc.tensor.matmul(cols[:, P * s : P * (s + 1)], field_rows[:, P * s : P * (s + 1)], ident_bf[:], start=True, stop=True)
            return wide, cols

        def exp_field(wide, cols):
            nc.scalar.activation(out=winv_bc[:], in_=wide[:, 0 : P * C_ROWS_FROM], func=EXP, scale=-1.0)
            nc.scalar.activation(
                out=winv_cols[:].rearrange("p (j s) -> p s j", j=FIELD_ROWS),
                in_=cols[:, 0:FIELD_COLS].rearrange("p (s c) -> p s c", c=P)[:, :, 0:FIELD_ROWS],
                func=EXP,
                scale=-1.0,
            )

        def park_w():
            nc.scalar.activation(out=w_cols[:], in_=field_cols[:], func=EXP)
            nc.sync.dma_start(out=out[SITES - 1, :].rearrange("(p c) -> p c", c=PARK_COLS), in_=w_cols[:])

        def spread_w():
            nc.sync.dma_start(out=w_bc[:], in_=out[SITES - 1, :].partition_broadcast(P))

        hop_pairs, halves, hop_banks, codes_of = {}, {}, {}, {}

        def every_second_word(words, first):
            return [words[:, first + u : first + 2 * P : 2] for u in range(2)]

        def cast(k0, k1):
            pair = k0 // (2 * PASSES)
            if pair not in hop_pairs:
                values = work.tile([P, 2 * SITES], BF16, name="hop_pair", bufs=3)
                hop_pairs[pair] = values
            values = hop_pairs[pair]
            rows, first = hop_raw[k0 // PASSES]
            first = first + K_PASS * (k0 % PASSES)
            target = K_PASS * (k0 % (2 * PASSES))
            width = K_PASS * (k1 - k0)
            on_scalar(out=values[:, target : target + width], in_=rows[:, first : first + width].bitcast(FP8))
            for k in range(k0, k1):
                halves[divmod(k, PASSES)] = every_second_word(values[:].bitcast(F32), 2 * P * (k % (2 * PASSES)))

        def cast_first_bank():
            values = keep.tile([P, 2 * K_PASS], BF16)
            nc.vector.tensor_scalar(
                out=values[:].rearrange("p (u n e) -> p n u e", u=2, e=2),
                in0=hop_raw[0][0][:, 0 : 2 * K_PASS].bitcast(FP8).rearrange("p (n u e) -> p n u e", u=2, e=2),
                scalar1=one[:],
                scalar2=None,
                op0=MULT,
            )
            for g in range(2):
                halves[0, g] = [values[:].bitcast(F32)[:, P * (2 * u + g) : P * (2 * u + g + 1)] for u in range(2)]

        def sort_words(b, target, copy):
            (i0, g0), (i1, g1) = bank_passes(b)
            first, step = PASSES * (i0 % 2) + g0, PASSES * (i1 - i0) + g1 - g0
            words = hop_pairs[i0 // 2][:].bitcast(F32).rearrange("p (l n u) -> p l u n", n=P, u=2)[:, first : first + step + 1 : step]
            target = target.bitcast(F32).rearrange("p (l u n) -> p l u n", n=P, u=2)
            copy(out=target, in_=words)
            for s, key in enumerate(bank_passes(b)):
                halves[key] = [target[:, s, u, :] for u in range(2)]

        def new_sorted():
            target = work.tile([P, 2 * K_PASS], BF16, name="sorted_words", bufs=4)
            return target[:]

        def turn(groups, k):
            bank = psum_bank(k)
            for s, pair in enumerate(groups):
                for u in range(2):
                    col = P * (len(groups) * u + s)
                    nc.tensor.transpose(bank[:, col : col + P], pair[u], ident[:])
            return bank

        def copy_turned(bank, target, copy):
            n = target.shape[1]
            copy(
                out=target.bitcast(F32).rearrange("p l (r u) -> p l r u", u=2),
                in_=bank[:, 0 : 2 * P * n].rearrange("p (u l r) -> p l r u", u=2, r=P),
            )

        def turn_hop(b, k):
            hop_banks[b] = turn([halves[key] for key in bank_passes(b)], k)

        def scale_hop(b, target):
            (i0, g0), (i1, g1) = bank_passes(b)
            nc.vector.tensor_tensor(
                out=target.rearrange("p (l r u e) -> p l r u e", l=2, u=2, e=2),
                in0=hop_banks[b][:].bitcast(BF16).rearrange("p (u l r e) -> p l r u e", l=2, u=2, e=2),
                in1=scale_cols[:, g0 : g1 + 1, :].rearrange("p l (u e) -> p l u e", u=2).unsqueeze(2).to_broadcast([P, 2, P, 2, 2]),
                op=MULT,
            )

        def turn_right(items, k):
            bank = turn([every_second_word(right_rows[t][:].bitcast(F32), 2 * P * g) for t, g in items], k)
            places = [PACK * g + t for t, g in items]
            step = max(places[-1] - places[0], 1)
            copy_turned(bank, right_turned[:].rearrange("p (l k) -> p l k", k=K_PASS)[:, places[0] : places[-1] + 1 : step, :], on_scalar)

        def quantize_right(t0, t1):
            for g in range(PASSES):
                m = slice(P * t0, P * t1)
                nc.vector.quantize_mx(
                    out=right_codes[:, g, m].bitcast(E4M3X4),
                    scales=right_sc[:, g, m],
                    in_=right_turned[:, K_PASS * (PACK * g + t0) : K_PASS * (PACK * g + t1)],
                )

        def new_stage(units):
            size = len(units)
            values = work.tile([P, size * K_PASS], BF16, name=f"stage{size}", align_bytes=64, bufs={1: 2, 3: 4, 4: 3, 6: 1}[size])
            codes = keep.tile([P, size * P], U32, name=f"codes{len(codes_of)}", align_bytes=64)
            sc = keep.tile([P, size * P], U8, name=f"scales{len(codes_of)}", align_bytes=64)
            for s, key in enumerate(units):
                codes_of[key] = (codes[:, P * s : P * (s + 1)], sc[:, P * s : P * (s + 1)])
            return values, codes, sc

        def units_of(stage, s0, s1):
            return stage[0][:, K_PASS * s0 : K_PASS * s1]

        def quantize(stage, s0, s1):
            values, codes, sc = stage
            nc.vector.quantize_mx(out=codes[:, P * s0 : P * s1].bitcast(E4M3X4), scales=sc[:, P * s0 : P * s1], in_=units_of(stage, s0, s1))

        left_grouped = {}

        def interleave_left(g, grouped):
            left_grouped[g] = grouped
            nc.gpsimd.tensor_copy(
                out=grouped.rearrange("p (t h l j) -> p h t l j", t=PACK, l=2, j=PACK),
                in_=left_rows[g][:].rearrange("p j (h l t) -> p h t l j", l=2, t=PACK),
            )

        def quantize_left(g):
            nc.vector.quantize_mx(out=left_codes[:, g, :].bitcast(E4M3X4), scales=left_sc[:, g, :], in_=left_grouped[g])

        c_acc, scaled_rows, a_acc = {}, {}, {}

        def slot_product(acc, t, operands):
            for g in range(PASSES):
                codes, sc, moving, moving_sc = operands(g)
                nc.tensor.matmul_mx(
                    out=acc[:, P * t : P * (t + 1)],
                    lhsT=codes.bitcast(E4M3X4),
                    lhsT_scale=sc,
                    rhs=moving,
                    rhs_scale=moving_sc,
                    start=(g == 0),
                    stop=(g == PASSES - 1),
                )

        def empty_slots(acc, factor, target):
            nc.vector.tensor_tensor(
                out=target.rearrange("p (n t) -> p n t", t=PACK),
                in0=acc[:].rearrange("p (t n) -> p n t", t=PACK),
                in1=factor.unsqueeze(2).to_broadcast([P, P, PACK]),
                op=MULT,
            )

        def mult_c(n, t):
            def operands(g):
                m = slice(P * t, P * (t + 1))
                return right_codes[:, g, m], right_sc[:, g, m], hinv_codes[n][:, g, :].bitcast(E2M1X4), hinv_sc[n][:, g, :]

            slot_product(c_acc[n], t, operands)

        def empty_c(n):
            empty_slots(c_acc[n], winv_bc[:, P * n : P * (n + 1)], c_values[:, ORB * n : ORB * (n + 1)])

        def mult_c_rows(n, k):
            acc = psum_bank(k)
            c_acc[n] = acc
            for g in range(PASSES):
                nc.tensor.matmul_mx(
                    out=acc[:],
                    lhsT=hinv_codes[n][:, g, :].bitcast(E2M1X4),
                    lhsT_scale=hinv_sc[n][:, g, :],
                    rhs=right_codes[:, g, :].bitcast(E4M3X4),
                    rhs_scale=right_sc[:, g, :],
                    start=(g == 0),
                    stop=(g == PASSES - 1),
                )

        def scale_rows(key, acc, j):
            rows = work.tile([P, ORB], BF16, name="rows", bufs=6)
            scaled_rows[key] = rows
            nc.scalar.activation(
                out=rows[:].rearrange("p (u m e) -> p u m e", u=2, e=2),
                in_=acc[:].rearrange("p (u e m) -> p u m e", u=2, e=2),
                func=COPY,
                scale=winv_cols[:, j : j + 1],
            )

        def turn_rows(keys, target, k):
            bank = turn([[scaled_rows[key][:].bitcast(F32)[:, P * u : P * (u + 1)] for u in range(2)] for key in keys], k)
            copy_turned(bank, target.rearrange("p (s k) -> p s k", k=ORB), on_scalar)

        def make_c_rows(n, k):
            mult_c_rows(n, k)
            scale_rows(("c", n), c_acc[n], n)

        def turn_c_rows(n0, n1, k):
            turn_rows([("c", n) for n in range(n0, n1)], c_values[:, ORB * n0 : ORB * n1], k)

        def quantize_c(n0, n1):
            cols = slice(P * n0, P * n1)
            nc.vector.quantize_mx(out=c_codes[:, cols].bitcast(E4M3X4), scales=c_sc[:, cols], in_=c_values[:, ORB * n0 : ORB * n1])

        def mult_a(i):
            a_acc[i] = psum_bank(i % 2)
            for t in range(PACK):
                m = slice(P * t, P * (t + 1))
                slot_product(a_acc[i], t, lambda g: (left_codes[:, g, m], left_sc[:, g, m], codes_of[i, g][0].bitcast(E4M3X4), codes_of[i, g][1]))

        def empty_a(i, target):
            empty_slots(a_acc[i], w_bc[:, P * i : P * (i + 1)], target)

        out_banks, result = {}, {}

        def mult_out(i):
            rows = work.tile([P, SITES], F32, name="result", bufs=4)
            result[i] = rows
            for q in range(CHUNKS):
                cols = slice(BANK * q, BANK * (q + 1))
                bank = psum_bank(4 + (CHUNKS * i + q) % 4)
                out_banks[i, q] = bank
                nc.tensor.matmul_mx(
                    out=bank[:],
                    lhsT=codes_of["a", i][0].bitcast(E4M3X4),
                    lhsT_scale=codes_of["a", i][1],
                    rhs=c_codes[:, cols].bitcast(E4M3X4),
                    rhs_scale=c_sc[:, cols],
                    start=True,
                    stop=True,
                )

        def empty_and_store(i, stores, vector_bank=None):
            for q in range(CHUNKS):
                copy = on_vector if q == vector_bank else on_scalar
                copy(out=result[i][:, BANK * q : BANK * (q + 1)], in_=out_banks[i, q][:])
                for q0, q1 in stores:
                    if q1 == q + 1:
                        cols = slice(BANK * q0, BANK * q1)
                        nc.sync.dma_start(out=out[P * i : P * (i + 1), cols], in_=result[i][:, cols])

        with tc.manual_schedule():
            nc.vector.memset(field_rows[:].bitcast(U32), 0)
            nc.vector.memset(table[:], 0.0)
            nc.vector.memset(one[:], 1.0)
            make_identity(nc, ident[:])
            clear_scales(0, HINV_FIRST, nc.vector)
            on_vector(out=ident_bf[:], in_=ident[:])
            clear_scales(HINV_FIRST, TILES, nc.vector)
            nc.scalar.dma_start(out=field_rows[0:FIELD_ROWS, :], in_=field.rearrange("(j c) -> j c", c=FIELD_COLS))
            nc.scalar.activation(out=table[:], in_=table[:], func=EXP)

            load_hop(0, 1)
            load_hop(1, 2)
            nc.sync.dma_start(out=scale_cols[:], in_=hop_scale.rearrange("o (g n q) -> n (o g) q", n=P, q=PACK))
            load_hop(2, 3)
            load_left(0)
            for t in range(PACK):
                load_right(t)
            load_scales(0, HINV_FIRST)
            load_hinv(0, HINV_FIRST)
            load_hop(3, 4)
            nc.sync.dma_start(out=field_cols[:], in_=field.rearrange("(p c) -> p c", c=PARK_COLS))
            load_left(1)
            load_hop(4, 6)
            load_scales(HINV_FIRST, TILES)
            load_hinv(HINV_FIRST, 9)
            load_hop(6, 8)
            load_left(2)
            load_hinv(9, TILES)

            first = new_stage(bank_passes(0) + bank_passes(1) + bank_passes(2))
            second = new_stage(bank_passes(3) + bank_passes(4))
            grouped = work.tile([P, PACK * ORB], BF16, name="left_grouped", align_bytes=64, bufs=1)
            interleave_left(0, grouped[:])
            cast_first_bank()
            cast(2, 3)
            cast(3, 6)
            cast(6, 9)
            exp_field(*spread_field(0, 1))
            turn_hop(0, 2)
            turn_hop(1, 5)
            turn_hop(2, 6)
            turn_hop(3, 7)
            turn_right([(0, 0), (0, 1)], 0)
            turn_right([(0, 2)], 1)
            turn_right([(1, 0), (1, 1)], 3)
            turn_right([(1, 2)], 4)
            scale_hop(0, units_of(first, 0, 2))
            scale_hop(1, units_of(first, 2, 4))
            scale_hop(2, units_of(first, 4, 6))
            scale_hop(3, units_of(second, 0, 2))
            quantize_right(0, 2)
            quantize_left(0)
            quantize(first, 0, 4)
            turn_right([(2, 0), (3, 0)], 2)
            turn_right([(2, 1), (3, 1)], 0)
            turn_right([(2, 2), (3, 2)], 5)
            quantize_right(2, 4)
            quantize(first, 4, 6)
            interleave_left(1, units_of(first, 2, 6))
            cast(9, 12)
            for n in range(C_ROWS_FROM):
                c_acc[n] = psum_bank((4, 6, 7, 2)[n])
            for n in range(C_ROWS_FROM):
                for t in range(2):
                    mult_c(n, t)
            park_w()
            load_hop(8, 10)
            load_hop(10, 12)
            spread_w()
            sort_words(4, new_sorted(), on_scalar)
            sort_words(5, new_sorted(), on_scalar)
            cast(12, 18)
            sort_words(6, new_sorted(), on_scalar)
            sort_words(7, new_sorted(), on_scalar)
            for n in range(2):
                for t in range(2, PACK):
                    mult_c(n, t)
            turn_hop(4, 0)
            turn_hop(5, 5)
            for n in range(2, C_ROWS_FROM):
                for t in range(2, PACK):
                    mult_c(n, t)
            empty_c(0)
            empty_c(1)
            scale_hop(4, units_of(second, 2, 4))
            empty_c(2)
            empty_c(3)
            make_c_rows(4, 1)
            make_c_rows(5, 3)
            cast(18, 24)
            quantize_left(1)
            quantize(second, 0, 4)
            sort_words(8, units_of(second, 2, 4), nc.gpsimd.tensor_copy)
            interleave_left(2, grouped[:])
            third = new_stage(bank_passes(5) + bank_passes(6))
            scale_hop(5, units_of(third, 0, 2))
            make_c_rows(6, 4)
            turn_hop(6, 6)
            turn_c_rows(4, 6, 7)
            turn_hop(7, 0)
            scale_hop(6, units_of(third, 2, 4))
            fourth = new_stage(bank_passes(7) + bank_passes(8))
            scale_hop(7, units_of(fourth, 0, 2))
            make_c_rows(7, 2)
            make_c_rows(8, 1)
            turn_hop(8, 3)
            turn_hop(9, 5)
            turn_c_rows(6, 8, 4)
            scale_hop(8, units_of(fourth, 2, 4))
            sort_words(10, new_sorted(), on_scalar)
            make_c_rows(9, 7)
            sort_words(11, new_sorted(), on_scalar)
            make_c_rows(10, 6)
            make_c_rows(11, 2)
            cast(24, 27)

            whole, split, by_bank = ((0, CHUNKS),), ((0, 1), (1, CHUNKS)), ((0, 1), (1, 2), (2, CHUNKS))
            lead = 9
            stage = new_stage(bank_passes(lead) + (("a", 1),))
            scale_hop(lead, units_of(stage, 0, 2))
            quantize_left(2)
            quantize_c(0, 4)
            quantize_c(4, 8)
            mult_a(0)
            turn_c_rows(8, 10, 7)
            turn_c_rows(10, 12, 4)
            turn_hop(lead + 1, 3)
            turn_hop(lead + 2, 2)
            cast(27, 30)
            alone = new_stage((("a", 0),))
            quantize(third, 0, 4)
            empty_a(0, units_of(alone, 0, 1))
            quantize(fourth, 0, 4)
            quantize(alone, 0, 1)
            quantize_c(8, 10)
            quantize_c(10, 12)
            for i in range(1, TILES):
                b = i + lead
                mult_a(i)
                a_unit = 2 if b <= HOP_BANKS else 0
                empty_a(i, units_of(stage, a_unit, a_unit + 1))
                mult_out(i - 1)
                if i % 2 == 1 and 1 < i and b < HOP_BANKS:
                    turn_hop(b, 3)
                    turn_hop(b + 1, 2)
                if b < HOP_BANKS:
                    quantize(stage, 0, 2)
                quantize(stage, a_unit, a_unit + 1)
                if b == HOP_BANKS:
                    quantize(stage, 0, 2)
                if b + 2 < HOP_BANKS:
                    sort_words(b + 2, units_of(stage, 1, 3), nc.gpsimd.tensor_copy)
                if b < HOP_BANKS:
                    stage = new_stage(bank_passes(b) + (("a", i + 1),))
                    scale_hop(b, units_of(stage, 0, 2))
                elif i + 1 < TILES:
                    stage = new_stage((("a", i + 1),))
                empty_and_store(i - 1, whole if i < 5 or i > 9 else split, vector_bank={10: 2, 11: 1}.get(i))
                if i in (2, 4):
                    cast(PASSES * (9 + i // 2), PASSES * (10 + i // 2))
            mult_out(11)
            empty_and_store(11, whole, vector_bank=1)
